import numpy as np
import ml_dtypes


def mxq(x, axis, fmt="e4m3"):
    dtype, down = {"e4m3": (ml_dtypes.float8_e4m3fn, 7), "e5m2": (ml_dtypes.float8_e5m2, 14)}[fmt]
    v = np.moveaxis(np.asarray(x, np.float32).astype(ml_dtypes.bfloat16).astype(np.float64), axis, -1)
    blocks = v.reshape(v.shape[:-1] + (-1, 32))
    amax = np.abs(blocks).max(-1, keepdims=True)
    byte = np.maximum(np.where(amax > 0, np.frexp(amax)[1] - 1 + 127, 0) - down, 1)
    scale = np.exp2(byte - 127.0)
    codes = (blocks / scale).astype(np.float32).astype(dtype).astype(np.float64)
    return np.moveaxis((codes * scale).reshape(v.shape), -1, axis)


WIDE = False


def mx_kscale(k):
    if not WIDE:
        return np.ones(k)
    levels = np.array([10, -10, 5, -5, 0])
    if k % 512:
        return np.exp2(np.random.permutation(np.resize(levels, k // 32))).repeat(32)
    a = np.empty((k // 512, 16))
    for p in range(k // 512):
        a[p, :8] = np.random.permutation(np.resize(levels, 8))
        for g in range(8):
            far = levels[np.abs(levels - a[p, g]) >= 10]
            a[p, g + 8] = far[np.random.randint(len(far))]
    return np.exp2(a.ravel()).repeat(32)


def f64(x):
    return np.asarray(x).astype(np.float64)


def striped(idx):
    return np.tile(idx.reshape(-1, 16).T, (8, 1)).astype(np.uint16)


def unstriped(offs):
    return offs[:16].T.reshape(-1).astype(np.int64)


E2M1 = np.array([0.0, 0.5, 1.0, 1.5, 2.0, 3.0, 4.0, 6.0, -0.0, -0.5, -1.0, -1.5, -2.0, -3.0, -4.0, -6.0])


def pack_weight(w, fmt):
    k, n = w.shape
    w = f64(np.asarray(w, np.float32).astype(ml_dtypes.bfloat16)).reshape(k // 32, 32, n)
    amax = np.abs(w).max(1)
    if fmt == "e4m3":
        byte = np.frexp(amax)[1] - 1 + 127 - 7
    else:
        mant, ex = np.frexp(amax / 6.0)
        byte = np.where(mant > 0.5, ex, ex - 1) + 127
    byte = np.clip(np.where(amax > 0, byte, 1), 1, 254)
    scaled = (w * np.exp2(127.0 - byte)[:, None, :]).reshape(k, n).astype(np.float32)
    by_word = np.ascontiguousarray(scaled.reshape(k // 512, 128, 4, n).transpose(0, 1, 3, 2))
    if fmt == "e4m3":
        words = by_word.astype(ml_dtypes.float8_e4m3fn).view(np.uint8)
    else:
        c = by_word.astype(ml_dtypes.float4_e2m1fn).view(np.uint8) & 0xF
        words = (c[..., 0::2] | (c[..., 1::2] << 4)).reshape(k // 512, 128, 2 * n)
    return np.ascontiguousarray(words), np.ascontiguousarray(byte.astype(np.uint8).reshape(k // 512, 16, n))


def unpack_weight(words, scales, fmt):
    g, _, n = scales.shape
    words = np.ascontiguousarray(words).reshape(g, 128, n, -1)
    if fmt == "e4m3":
        vals = words.view(ml_dtypes.float8_e4m3fn).astype(np.float64)
    else:
        nib = np.empty((g, 128, n, 4), np.uint8)
        nib[..., 0::2] = words & 0xF
        nib[..., 1::2] = words >> 4
        vals = E2M1[nib]
    vals = vals * np.repeat(np.exp2(scales.astype(np.float64) - 127.0), 8, axis=1)[..., None]
    return vals.transpose(0, 1, 3, 2).reshape(g * 512, n)


def gelu(v):
    return 0.5 * v * (1.0 + np.tanh(np.sqrt(2.0 / np.pi) * (v + 0.044715 * v**3)))


K, H, N, T, S, T2 = 1024, 1024, 384, 4096, 1024, 2048


def setup_inputs():
    n = np.random.standard_normal
    s = mx_kscale(K)[:, None]
    u = mx_kscale(H)[:, None]
    tab_words, tab_scales = pack_weight(n((K, T)) * s, "e4m3")
    w4_words, w4_scales = pack_weight(n((H, N)) / np.sqrt(H) / u, "e2m1")
    return {
        "tab_words": tab_words,
        "tab_scales": tab_scales,
        "offs": striped(np.random.permutation(T)[:S]),
        "w1": (n((K, H)) / np.sqrt(K) / s).astype(np.float32),
        "b1": (0.5 * n(H)).astype(np.float32),
        "wgs": np.exp(-np.abs(0.3 * n((128, S)))).astype(np.float32),
        "offs2": striped(np.random.permutation(T2)[:S]),
        "old": (n((H, T2)) * u).astype(np.float32),
        "w4_words": w4_words,
        "w4_scales": w4_scales,
    }


def reference(tab_words, tab_scales, offs, w1, b1, wgs, offs2, old, w4_words, w4_scales):
    v = unpack_weight(tab_words, tab_scales, "e4m3")[:, unstriped(offs)]
    a = (mxq(f64(w1), 0, "e4m3").T @ v) + f64(b1)[:, None]
    h = 1.0 / (1.0 + np.exp(-a))
    page = np.zeros((H, T2))
    page[:, unstriped(offs2)] = np.tile(f64(wgs), (H // 128, 1)) * h
    z = f64(old) * (1.0 - page)
    zq = mxq(z, 0, "e4m3")
    w4 = unpack_weight(w4_words, w4_scales, "e2m1")
    return w4.T @ zq

@@ -1,0 +1,286 @@
+from contextlib import ExitStack
+
+import concourse.mybir as mybir
+
+K, H, N, T, S, T2 = 1024, 1024, 384, 4096, 1024, 2048
+FLOPS = 2 * K * H * S + 2 * H * N * T2
+
+F32 = mybir.dt.float32
+BF16 = mybir.dt.bfloat16
+I32 = mybir.dt.int32
+U32 = mybir.dt.uint32
+U16 = mybir.dt.uint16
+U8 = mybir.dt.uint8
+FP8X4 = mybir.dt.float8_e4m3fn_x4
+FP4X4 = mybir.dt.float4_e2m1fn_x4
+MULT = mybir.AluOpType.mult
+SIGMOID = mybir.ActivationFunctionType.Sigmoid
+COPY = mybir.ActivationFunctionType.Copy
+
+P = 128
+PACK = 4
+PASS = P * PACK
+BANK = 512
+PASSES = 2
+SLICES = PASSES * PACK
+CHUNKS = T2 // BANK
+NT = N // P
+PAGES = 3
+
+
+def tile_list_voxel_occupancy_map_kernel(
+    tc, tab_words, tab_scales, offs, w1, b1, wgs, offs2, old, w4_words, w4_scales, out
+):
+    nc = tc.nc
+    with ExitStack() as ctx:
+        keep = ctx.enter_context(tc.tile_pool(name="keep", bufs=1))
+        ring = ctx.enter_context(tc.tile_pool(name="ring", bufs=2))
+        psum = ctx.enter_context(tc.psum_pool(name="psum", bufs=1))
+
+        pick = keep.tile([P, S // 16], U16, name="pick")
+        place = keep.tile([P, S // 16], U16, name="place")
+        nc.sync.dma_start(pick[:], offs)
+
+        scale_win = keep.tile([P, T], U8, name="scale_win", align_bytes=64)
+        nc.vector.memset(scale_win[:].bitcast(I32), 0)
+        for q in range(4):
+            nc.gpsimd.dma_start(
+                out=scale_win[32 * q : 32 * q + 8, :].bitcast(I32),
+                in_=tab_scales[:, 4 * q : 4 * q + 4, :].bitcast(I32),
+            )
+        bias = keep.tile([P, PASSES, PACK], F32, name="bias")
+        nc.scalar.dma_start(out=bias[:], in_=b1.rearrange("(b p i) -> p b i", b=PASSES, i=PACK))
+        warm = keep.tile([P, 1], F32, name="warm")
+        nc.scalar.activation(warm[:], bias[:, 0, 0:1], SIGMOID)
+
+        w1_raw = {}
+
+        def load_w1(b):
+            for a in range(PASSES):
+                raw = ring.tile([P, PACK, PASS], F32, name="raw", tag="rows", bufs=5)
+                nc.sync.dma_start(
+                    out=raw[:],
+                    in_=w1[a * PASS : (a + 1) * PASS, b * PASS : (b + 1) * PASS].rearrange("(p j) c -> p j c", j=PACK),
+                )
+                w1_raw[(a, b)] = raw
+
+        w1_codes = [keep.tile([P, PASSES * PASS], U32, name="w1c%d" % b, align_bytes=64) for b in range(PASSES)]
+        w1_scales = [keep.tile([P, PASSES * PASS], U8, name="w1s%d" % b, align_bytes=64) for b in range(PASSES)]
+
+        def prep_w1(b, joint):
+            grouped = ring.tile([P, PASSES * PASS * PACK], BF16, name="grouped", bufs=1, align_bytes=64)
+            width = PASS * PACK
+            for a in range(PASSES):
+                nc.scalar.copy(
+                    out=grouped[:, a * width : (a + 1) * width].rearrange("p (t m j) -> p m j t", t=PACK, j=PACK),
+                    in_=w1_raw[(a, b)][:].rearrange("p j (m t) -> p m j t", t=PACK),
+                )
+                if not joint:
+                    nc.vector.quantize_mx(
+                        out=w1_codes[b][:, a * PASS : (a + 1) * PASS].bitcast(FP8X4),
+                        scales=w1_scales[b][:, a * PASS : (a + 1) * PASS],
+                        in_=grouped[:, a * width : (a + 1) * width],
+                    )
+            if joint:
+                nc.vector.quantize_mx(out=w1_codes[b][:].bitcast(FP8X4), scales=w1_scales[b][:], in_=grouped[:])
+
+        load_w1(0)
+        table = []
+        for a in range(PASSES):
+            words = ring.tile([P, T], I32, name="words", tag="wide", bufs=2, align_bytes=64)
+            nc.sync.dma_start(out=words[:], in_=tab_words[a].rearrange("p t i -> p (t i)").bitcast(I32))
+            table.append(words)
+        nc.sync.dma_start(place[:], offs2)
+
+        conf = [keep.tile([P, S], F32, name="conf%d" % i) for i in range(PACK)]
+        conf_rows = wgs.rearrange("(m i) j -> i m j", i=PACK)
+
+        def load_conf(i):
+            for q in (0, 2, 1, 3):
+                nc.sync.dma_start(out=conf[i][32 * q : 32 * q + 32, :], in_=conf_rows[i])
+
+        old_rows = old.rearrange("(b p i) t -> b i p t", b=PASSES, i=PACK)
+        old_tiles = {}
+
+        def load_old(s):
+            rows = ring.tile([P, T2], F32, name="rows", tag="rows", bufs=5)
+            nc.sync.dma_start(out=rows[:], in_=old_rows[s // PACK, s % PACK])
+            old_tiles[s] = rows
+
+        for i in range(3):
+            load_conf(i)
+        load_old(0)
+        load_conf(3)
+        load_w1(1)
+        load_old(1)
+        load_old(2)
+        w4_codes = keep.tile([P, PASSES, 2 * N], U8, name="w4_codes", align_bytes=64)
+        nc.sync.dma_start(out=w4_codes[:].bitcast(I32), in_=w4_words.rearrange("a p c -> p a c").bitcast(I32))
+        w4_plane = keep.tile([P, PASSES, N], U8, name="w4_plane", align_bytes=64)
+        nc.vector.memset(w4_plane[:].bitcast(I32), 0)
+        for q in range(4):
+            nc.sync.dma_start(
+                out=w4_plane[32 * q : 32 * q + 4, :, :].bitcast(I32),
+                in_=w4_scales[:, 4 * q : 4 * q + 4, :].rearrange("a r c -> r a c").bitcast(I32),
+            )
+        for s in range(3, SLICES):
+            load_old(s)
+
+        pages = [keep.tile([P, T2], F32, name="page%d" % n) for n in range(PAGES)]
+        for page in pages:
+            nc.vector.memset(page[:], 1.0)
+
+        prep_w1(0, False)
+
+        picked_scales = keep.tile([P, S], U8, name="picked_scales", align_bytes=64)
+        nc.vector.tensor_copy(picked_scales[:], scale_win[:].indirect(pick[:]))
+        picked = [keep.tile([P, S], I32, name="picked%d" % a, align_bytes=64) for a in range(PASSES)]
+        nc.vector.tensor_copy(picked[0][:].bitcast(U32), table[0][:].bitcast(U32).indirect(pick[:]))
+        for hf in range(2):
+            nc.vector.tensor_copy(
+                picked[1][:, hf * BANK : (hf + 1) * BANK].bitcast(U32),
+                table[1][:].bitcast(U32).indirect(pick[:, hf * 32 : (hf + 1) * 32]),
+            )
+
+        fade = {}
+
+        def front(s):
+            b, i = divmod(s, PACK)
+            occ = ring.tile([P, S], F32, name="occ", bufs=2)
+            keepf = ring.tile([P, S], F32, name="keepf", bufs=4)
+            fade[s] = keepf
+            for hf in range(2):
+                cols = slice(hf * BANK, (hf + 1) * BANK)
+                acc = psum.tile([P, BANK], F32, name="acc", tag="bank%d" % (4 + (2 * s + hf) % 4))
+                for a in range(PASSES):
+                    wcols = slice(a * PASS + i * P, a * PASS + (i + 1) * P)
+                    nc.tensor.matmul_mx(
+                        out=acc[:],
+                        lhsT=w1_codes[b][:, wcols].bitcast(FP8X4),
+                        lhsT_scale=w1_scales[b][:, wcols],
+                        rhs=picked[a][:, cols].bitcast(FP8X4),
+                        rhs_scale=picked_scales[4 * a : P, cols],
+                        start=(a == 0),
+                        stop=(a == PASSES - 1),
+                    )
+                nc.scalar.activation(occ[:, cols], acc[:], SIGMOID, bias=bias[:, b, i : i + 1])
+            parts = [slice(0, BANK), slice(BANK, S)] if s == 0 else [slice(0, S)]
+            for cols in parts:
+                nc.gpsimd.tensor_tensor(keepf[:, cols], occ[:, cols], conf[i][:, cols], MULT)
+                nc.scalar.activation(keepf[:, cols], keepf[:, cols], COPY, bias=1.0, scale=-1.0)
+
+        def scatter(s):
+            page = pages[s % PAGES]
+            if s == 0:
+                for hf in range(2):
+                    nc.vector.tensor_copy(
+                        page[:].indirect(place[:, hf * 32 : (hf + 1) * 32]), fade[s][:, hf * BANK : (hf + 1) * BANK]
+                    )
+            else:
+                nc.vector.tensor_copy(page[:].indirect(place[:]), fade[s][:])
+
+        planes = {}
+
+        def fade_old(s, eng, cols):
+            b, i = divmod(s, PACK)
+            if b not in planes:
+                planes[b] = ring.tile([P, PACK, T2], BF16, name="planes", tag="wide", bufs=2, align_bytes=64)
+            eng.tensor_tensor(planes[b][:, i, cols], old_tiles[s][:, cols], pages[s % PAGES][:, cols], MULT)
+
+        z_codes = [keep.tile([P, T2], U32, name="zc%d" % b, align_bytes=64) for b in range(PASSES)]
+        z_scales = [keep.tile([P, T2], U8, name="zs%d" % b, align_bytes=64) for b in range(PASSES)]
+        woven = {}
+
+        def weave(b, c, on_vector):
+            if c % 2 == 0:
+                woven[(b, c // 2)] = ring.tile([P, 2 * BANK * PACK], BF16, name="woven", bufs=2, align_bytes=64)
+            dst = woven[(b, c // 2)][:, (c % 2) * BANK * PACK : (c % 2 + 1) * BANK * PACK]
+            dst = dst.rearrange("p (c i t) -> p c t i", i=4, t=PACK)
+            src = planes[b][:, :, c * BANK : (c + 1) * BANK].rearrange("p t (c i) -> p c t i", i=4)
+            if on_vector:
+                nc.vector.tensor_copy(dst, src)
+            else:
+                nc.scalar.copy(dst, src)
+
+        def quantize_z(b, c0, count):
+            cols = slice(c0 * BANK, (c0 + count) * BANK)
+            lo = (c0 % 2) * BANK * PACK
+            nc.vector.quantize_mx(
+                out=z_codes[b][:, cols].bitcast(FP8X4),
+                scales=z_scales[b][:, cols],
+                in_=woven[(b, c0 // 2)][:, lo : lo + count * BANK * PACK],
+            )
+
+        sums = {}
+
+        def readout(g, b):
+            c, n = divmod(g, NT)
+            if b == 0:
+                sums[g] = psum.tile([P, BANK], F32, name="sums", tag="bank%d" % (g % 8))
+            cols = slice(c * BANK, (c + 1) * BANK)
+            nc.tensor.matmul_mx(
+                out=sums[g][:],
+                lhsT=w4_codes[:, b, 2 * n * P : 2 * (n + 1) * P].bitcast(FP4X4),
+                lhsT_scale=w4_plane[:, b, n * P : (n + 1) * P],
+                rhs=z_codes[b][:, cols].bitcast(FP8X4),
+                rhs_scale=z_scales[b][:, cols],
+                start=(b == 0),
+                stop=(b == PASSES - 1),
+            )
+
+        def store(g, on_vector):
+            c, n = divmod(g, NT)
+            staged = ring.tile([P, BANK], F32, name="staged", bufs=6)
+            if on_vector:
+                nc.vector.tensor_copy(staged[:], sums[g][:])
+            else:
+                nc.scalar.copy(staged[:], sums[g][:])
+            nc.sync.dma_start(out=out[n * P : (n + 1) * P, c * BANK : (c + 1) * BANK], in_=staged[:])
+
+        front(0)
+        front(1)
+        front(2)
+        prep_w1(1, True)
+        for s in range(SLICES - 1):
+            scatter(s)
+            for hf in range(2):
+                fade_old(s, nc.gpsimd, slice(hf * T2 // 2, (hf + 1) * T2 // 2))
+            if s + 3 < SLICES:
+                front(s + 3)
+            if s == PACK:
+                for c in range(CHUNKS):
+                    weave(0, c, False)
+                    if c % 2 == 1:
+                        quantize_z(0, c - 1, 2)
+                for g in range(8):
+                    readout(g, 0)
+        last = SLICES - 1
+        scatter(last)
+
+        def finish(c):
+            for g in range(c * NT, (c + 1) * NT):
+                readout(g, 1)
+            for g in range(c * NT, (c + 1) * NT):
+                store(g, c == CHUNKS - 1 and g % 2 == 0)
+                if g + 8 < CHUNKS * NT:
+                    readout(g + 8, 0)
+
+        def chunk(c):
+            return slice(c * BANK, (c + 1) * BANK)
+
+        fade_old(last, nc.vector, chunk(0))
+        fade_old(last, nc.vector, chunk(1))
+        weave(1, 0, True)
+        weave(1, 1, False)
+        fade_old(last, nc.vector, chunk(2))
+        quantize_z(1, 0, 1)
+        finish(0)
+        fade_old(last, nc.vector, chunk(3))
+        weave(1, 2, True)
+        quantize_z(1, 1, 1)
+        finish(1)
+        weave(1, 3, True)
+        quantize_z(1, 2, 1)
+        finish(2)
+        quantize_z(1, 3, 1)
+        finish(3)

@@ -14,6 +14,7 @@ U8 = mybir.dt.uint8
 FP8X4 = mybir.dt.float8_e4m3fn_x4
 FP4X4 = mybir.dt.float4_e2m1fn_x4
 MULT = mybir.AluOpType.mult
+ADD = mybir.AluOpType.add
 SIGMOID = mybir.ActivationFunctionType.Sigmoid
 COPY = mybir.ActivationFunctionType.Copy
 
@@ -25,7 +26,7 @@ PASSES = 2
 SLICES = PASSES * PACK
 CHUNKS = T2 // BANK
 NT = N // P
-PAGES = 3
+PAGES = 2
 
 
 def tile_list_voxel_occupancy_map_kernel(
@@ -42,7 +43,7 @@ def tile_list_voxel_occupancy_map_kernel(
         nc.sync.dma_start(pick[:], offs)
 
         scale_win = keep.tile([P, T], U8, name="scale_win", align_bytes=64)
-        nc.vector.memset(scale_win[:].bitcast(I32), 0)
+        nc.gpsimd.memset(scale_win[:].bitcast(I32), 0)
         for q in range(4):
             nc.gpsimd.dma_start(
                 out=scale_win[32 * q : 32 * q + 8, :].bitcast(I32),
@@ -67,8 +68,11 @@ def tile_list_voxel_occupancy_map_kernel(
         w1_codes = [keep.tile([P, PASSES * PASS], U32, name="w1c%d" % b, align_bytes=64) for b in range(PASSES)]
         w1_scales = [keep.tile([P, PASSES * PASS], U8, name="w1s%d" % b, align_bytes=64) for b in range(PASSES)]
 
+        grouped = keep.tile([P, PASSES * PASS * PACK], BF16, name="grouped", align_bytes=64)
+        woven = [keep.tile([P, 2 * BANK * PACK], BF16, name="woven%d" % n, align_bytes=64) for n in range(2)]
+        swap = [keep.tile([P, T2], F32, name="swap%d" % n) for n in range(2)]
+
         def prep_w1(b, joint):
-            grouped = ring.tile([P, PASSES * PASS * PACK], BF16, name="grouped", bufs=1, align_bytes=64)
             width = PASS * PACK
             for a in range(PASSES):
                 nc.scalar.copy(
@@ -84,9 +88,10 @@ def tile_list_voxel_occupancy_map_kernel(
             if joint:
                 nc.vector.quantize_mx(out=w1_codes[b][:].bitcast(FP8X4), scales=w1_scales[b][:], in_=grouped[:])
 
-        load_w1(0)
         table = []
         for a in range(PASSES):
+            if a == 1:
+                load_w1(0)
             words = ring.tile([P, T], I32, name="words", tag="wide", bufs=2, align_bytes=64)
             nc.sync.dma_start(out=words[:], in_=tab_words[a].rearrange("p t i -> p (t i)").bitcast(I32))
             table.append(words)
@@ -107,17 +112,18 @@ def tile_list_voxel_occupancy_map_kernel(
             nc.sync.dma_start(out=rows[:], in_=old_rows[s // PACK, s % PACK])
             old_tiles[s] = rows
 
-        for i in range(3):
-            load_conf(i)
+        load_conf(0)
+        load_conf(1)
+        load_conf(2)
         load_old(0)
-        load_conf(3)
         load_w1(1)
+        load_conf(3)
         load_old(1)
         load_old(2)
         w4_codes = keep.tile([P, PASSES, 2 * N], U8, name="w4_codes", align_bytes=64)
         nc.sync.dma_start(out=w4_codes[:].bitcast(I32), in_=w4_words.rearrange("a p c -> p a c").bitcast(I32))
         w4_plane = keep.tile([P, PASSES, N], U8, name="w4_plane", align_bytes=64)
-        nc.vector.memset(w4_plane[:].bitcast(I32), 0)
+        nc.gpsimd.memset(w4_plane[:].bitcast(I32), 0)
         for q in range(4):
             nc.sync.dma_start(
                 out=w4_plane[32 * q : 32 * q + 4, :, :].bitcast(I32),
@@ -128,14 +134,17 @@ def tile_list_voxel_occupancy_map_kernel(
 
         pages = [keep.tile([P, T2], F32, name="page%d" % n) for n in range(PAGES)]
         for page in pages:
-            nc.vector.memset(page[:], 1.0)
+            nc.gpsimd.memset(page[:], 0.0)
 
         prep_w1(0, False)
 
         picked_scales = keep.tile([P, S], U8, name="picked_scales", align_bytes=64)
-        nc.vector.tensor_copy(picked_scales[:], scale_win[:].indirect(pick[:]))
         picked = [keep.tile([P, S], I32, name="picked%d" % a, align_bytes=64) for a in range(PASSES)]
         nc.vector.tensor_copy(picked[0][:].bitcast(U32), table[0][:].bitcast(U32).indirect(pick[:]))
+        for hf in range(2):
+            nc.vector.tensor_copy(
+                picked_scales[:, hf * BANK : (hf + 1) * BANK], scale_win[:].indirect(pick[:, hf * 32 : (hf + 1) * 32])
+            )
         for hf in range(2):
             nc.vector.tensor_copy(
                 picked[1][:, hf * BANK : (hf + 1) * BANK].bitcast(U32),
@@ -144,11 +153,29 @@ def tile_list_voxel_occupancy_map_kernel(
 
         fade = {}
 
-        def front(s):
-            b, i = divmod(s, PACK)
-            occ = ring.tile([P, S], F32, name="occ", bufs=2)
-            keepf = ring.tile([P, S], F32, name="keepf", bufs=4)
+        occs = {}
+
+        def weigh(s):
+            i = s % PACK
+            occ = occs[s]
+            if s == 0:
+                keepf = grouped[:, 0 : 2 * S].bitcast(F32)
+            elif s >= SLICES - 2:
+                keepf = woven[s % 2][:, 0 : 2 * S].bitcast(F32)
+            else:
+                keepf = swap[s % 2][:, 0:S]
             fade[s] = keepf
+            parts = [slice(0, BANK), slice(BANK, S)] if s == 0 else [slice(0, S)]
+            for cols in parts:
+                nc.vector.scalar_tensor_tensor(keepf[:, cols], occ[:, cols], -1.0, conf[i][:, cols], MULT, MULT)
+
+        def logits(s):
+            b, i = divmod(s, PACK)
+            if s == 0:
+                occ = swap[0][:, 0:S]
+            else:
+                occ = ring.tile([P, S], F32, name="occ", bufs=1)
+            occs[s] = occ
             for hf in range(2):
                 cols = slice(hf * BANK, (hf + 1) * BANK)
                 acc = psum.tile([P, BANK], F32, name="acc", tag="bank%d" % (4 + (2 * s + hf) % 4))
@@ -164,20 +191,20 @@ def tile_list_voxel_occupancy_map_kernel(
                         stop=(a == PASSES - 1),
                     )
                 nc.scalar.activation(occ[:, cols], acc[:], SIGMOID, bias=bias[:, b, i : i + 1])
-            parts = [slice(0, BANK), slice(BANK, S)] if s == 0 else [slice(0, S)]
-            for cols in parts:
-                nc.gpsimd.tensor_tensor(keepf[:, cols], occ[:, cols], conf[i][:, cols], MULT)
-                nc.scalar.activation(keepf[:, cols], keepf[:, cols], COPY, bias=1.0, scale=-1.0)
 
         def scatter(s):
             page = pages[s % PAGES]
             if s == 0:
                 for hf in range(2):
+                    if hf == 1:
+                        logits(1)
+                        weigh(1)
+                        logits(2)
                     nc.vector.tensor_copy(
                         page[:].indirect(place[:, hf * 32 : (hf + 1) * 32]), fade[s][:, hf * BANK : (hf + 1) * BANK]
                     )
             else:
-                nc.vector.tensor_copy(page[:].indirect(place[:]), fade[s][:])
+                nc.vector.tensor_copy(page[:].indirect(place[:]), fade[s])
 
         planes = {}
 
@@ -185,16 +212,19 @@ def tile_list_voxel_occupancy_map_kernel(
             b, i = divmod(s, PACK)
             if b not in planes:
                 planes[b] = ring.tile([P, PACK, T2], BF16, name="planes", tag="wide", bufs=2, align_bytes=64)
-            eng.tensor_tensor(planes[b][:, i, cols], old_tiles[s][:, cols], pages[s % PAGES][:, cols], MULT)
+            page = pages[s % PAGES]
+            if s == SLICES - 1:
+                eng.scalar_tensor_tensor(planes[b][:, i, cols], page[:, cols], 1.0, old_tiles[s][:, cols], ADD, MULT)
+            else:
+                left = swap[s % 2]
+                nc.scalar.activation(left[:], page[:], COPY, bias=1.0)
+                eng.tensor_tensor(planes[b][:, i, :], old_tiles[s][:], left[:], MULT)
 
         z_codes = [keep.tile([P, T2], U32, name="zc%d" % b, align_bytes=64) for b in range(PASSES)]
         z_scales = [keep.tile([P, T2], U8, name="zs%d" % b, align_bytes=64) for b in range(PASSES)]
-        woven = {}
 
         def weave(b, c, on_vector):
-            if c % 2 == 0:
-                woven[(b, c // 2)] = ring.tile([P, 2 * BANK * PACK], BF16, name="woven", bufs=2, align_bytes=64)
-            dst = woven[(b, c // 2)][:, (c % 2) * BANK * PACK : (c % 2 + 1) * BANK * PACK]
+            dst = woven[c // 2][:, (c % 2) * BANK * PACK : (c % 2 + 1) * BANK * PACK]
             dst = dst.rearrange("p (c i t) -> p c t i", i=4, t=PACK)
             src = planes[b][:, :, c * BANK : (c + 1) * BANK].rearrange("p t (c i) -> p c t i", i=4)
             if on_vector:
@@ -208,7 +238,7 @@ def tile_list_voxel_occupancy_map_kernel(
             nc.vector.quantize_mx(
                 out=z_codes[b][:, cols].bitcast(FP8X4),
                 scales=z_scales[b][:, cols],
-                in_=woven[(b, c0 // 2)][:, lo : lo + count * BANK * PACK],
+                in_=woven[c0 // 2][:, lo : lo + count * BANK * PACK],
             )
 
         sums = {}
@@ -237,23 +267,23 @@ def tile_list_voxel_occupancy_map_kernel(
                 nc.scalar.copy(staged[:], sums[g][:])
             nc.sync.dma_start(out=out[n * P : (n + 1) * P, c * BANK : (c + 1) * BANK], in_=staged[:])
 
-        front(0)
-        front(1)
-        front(2)
-        prep_w1(1, True)
+        logits(0)
+        weigh(0)
         for s in range(SLICES - 1):
             scatter(s)
-            for hf in range(2):
-                fade_old(s, nc.gpsimd, slice(hf * T2 // 2, (hf + 1) * T2 // 2))
-            if s + 3 < SLICES:
-                front(s + 3)
-            if s == PACK:
-                for c in range(CHUNKS):
+            if s > PACK:
+                for c in range(2 * (s - PACK - 1), 2 * (s - PACK)):
                     weave(0, c, False)
-                    if c % 2 == 1:
-                        quantize_z(0, c - 1, 2)
-                for g in range(8):
-                    readout(g, 0)
+                quantize_z(0, 2 * (s - PACK - 1), 2)
+            fade_old(s, nc.gpsimd, slice(0, T2))
+            if s == 0:
+                prep_w1(1, True)
+            else:
+                weigh(s + 1)
+                if s + 2 < SLICES:
+                    logits(s + 2)
+        for g in range(8):
+            readout(g, 0)
         last = SLICES - 1
         scatter(last)
 
@@ -261,7 +291,7 @@ def tile_list_voxel_occupancy_map_kernel(
             for g in range(c * NT, (c + 1) * NT):
                 readout(g, 1)
             for g in range(c * NT, (c + 1) * NT):
-                store(g, c == CHUNKS - 1 and g % 2 == 0)
+                store(g, c == CHUNKS - 1 and g % 2 == 1)
                 if g + 8 < CHUNKS * NT:
                     readout(g + 8, 0)
 
@@ -279,8 +309,8 @@ def tile_list_voxel_occupancy_map_kernel(
         weave(1, 2, True)
         quantize_z(1, 1, 1)
         finish(1)
-        weave(1, 3, True)
         quantize_z(1, 2, 1)
         finish(2)
+        weave(1, 3, True)
         quantize_z(1, 3, 1)
         finish(3)

@@ -27,6 +27,8 @@ SLICES = PASSES * PACK
 CHUNKS = T2 // BANK
 NT = N // P
 PAGES = 2
+AHEAD = 3
+HALF = BANK // 16
 
 
 def tile_list_voxel_occupancy_map_kernel(
@@ -42,8 +44,8 @@ def tile_list_voxel_occupancy_map_kernel(
         place = keep.tile([P, S // 16], U16, name="place")
         nc.sync.dma_start(pick[:], offs)
 
-        scale_win = keep.tile([P, T], U8, name="scale_win", align_bytes=64)
-        nc.gpsimd.memset(scale_win[:].bitcast(I32), 0)
+        scale_win = ring.tile([P, T], U8, name="scale_win", tag="scale_win", bufs=1, align_bytes=64)
+        nc.vector.memset(scale_win[:].bitcast(I32), 0)
         for q in range(4):
             nc.gpsimd.dma_start(
                 out=scale_win[32 * q : 32 * q + 8, :].bitcast(I32),
@@ -51,48 +53,40 @@ def tile_list_voxel_occupancy_map_kernel(
             )
         bias = keep.tile([P, PASSES, PACK], F32, name="bias")
         nc.scalar.dma_start(out=bias[:], in_=b1.rearrange("(b p i) -> p b i", b=PASSES, i=PACK))
-        warm = keep.tile([P, 1], F32, name="warm")
-        nc.scalar.activation(warm[:], bias[:, 0, 0:1], SIGMOID)
 
         w1_raw = {}
 
-        def load_w1(b):
-            for a in range(PASSES):
-                raw = ring.tile([P, PACK, PASS], F32, name="raw", tag="rows", bufs=5)
-                nc.sync.dma_start(
-                    out=raw[:],
-                    in_=w1[a * PASS : (a + 1) * PASS, b * PASS : (b + 1) * PASS].rearrange("(p j) c -> p j c", j=PACK),
-                )
-                w1_raw[(a, b)] = raw
+        def load_w1(b, a):
+            raw = ring.tile([P, PACK, PASS], F32, name="raw", tag="rows%d" % (2 * b + a), bufs=1, align_bytes=64)
+            nc.sync.dma_start(
+                out=raw[:],
+                in_=w1[a * PASS : (a + 1) * PASS, b * PASS : (b + 1) * PASS].rearrange("(p j) c -> p j c", j=PACK),
+            )
+            w1_raw[(a, b)] = raw
 
-        w1_codes = [keep.tile([P, PASSES * PASS], U32, name="w1c%d" % b, align_bytes=64) for b in range(PASSES)]
+        w1_codes = {0: keep.tile([P, PASSES * PASS], U32, name="w1c0", align_bytes=64)}
         w1_scales = [keep.tile([P, PASSES * PASS], U8, name="w1s%d" % b, align_bytes=64) for b in range(PASSES)]
-
         grouped = keep.tile([P, PASSES * PASS * PACK], BF16, name="grouped", align_bytes=64)
-        woven = [keep.tile([P, 2 * BANK * PACK], BF16, name="woven%d" % n, align_bytes=64) for n in range(2)]
-        swap = [keep.tile([P, T2], F32, name="swap%d" % n) for n in range(2)]
+        width = PASS * PACK
 
-        def prep_w1(b, joint):
-            width = PASS * PACK
-            for a in range(PASSES):
-                nc.scalar.copy(
-                    out=grouped[:, a * width : (a + 1) * width].rearrange("p (t m j) -> p m j t", t=PACK, j=PACK),
-                    in_=w1_raw[(a, b)][:].rearrange("p j (m t) -> p m j t", t=PACK),
-                )
-                if not joint:
-                    nc.vector.quantize_mx(
-                        out=w1_codes[b][:, a * PASS : (a + 1) * PASS].bitcast(FP8X4),
-                        scales=w1_scales[b][:, a * PASS : (a + 1) * PASS],
-                        in_=grouped[:, a * width : (a + 1) * width],
-                    )
-            if joint:
-                nc.vector.quantize_mx(out=w1_codes[b][:].bitcast(FP8X4), scales=w1_scales[b][:], in_=grouped[:])
+        def cast_w1(b, a, copy):
+            copy(
+                grouped[:, a * width : (a + 1) * width].rearrange("p (t m j) -> p m j t", t=PACK, j=PACK),
+                w1_raw[(a, b)][:].rearrange("p j (m t) -> p m j t", t=PACK),
+            )
 
+        def quantize_w1(b, a0, count):
+            nc.vector.quantize_mx(
+                out=w1_codes[b][:, a0 * PASS : (a0 + count) * PASS].bitcast(FP8X4),
+                scales=w1_scales[b][:, a0 * PASS : (a0 + count) * PASS],
+                in_=grouped[:, a0 * width : (a0 + count) * width],
+            )
+
+        load_w1(0, 0)
+        load_w1(0, 1)
         table = []
         for a in range(PASSES):
-            if a == 1:
-                load_w1(0)
-            words = ring.tile([P, T], I32, name="words", tag="wide", bufs=2, align_bytes=64)
+            words = ring.tile([P, T], I32, name="words", tag="wide%d" % a, bufs=1, align_bytes=64)
             nc.sync.dma_start(out=words[:], in_=tab_words[a].rearrange("p t i -> p (t i)").bitcast(I32))
             table.append(words)
         nc.sync.dma_start(place[:], offs2)
@@ -108,73 +102,63 @@ def tile_list_voxel_occupancy_map_kernel(
         old_tiles = {}
 
         def load_old(s):
-            rows = ring.tile([P, T2], F32, name="rows", tag="rows", bufs=5)
+            slot = "rows%d" % (s % PACK if s < SLICES - 1 else PACK)
+            rows = ring.tile([P, T2], F32, name="rows", tag=slot, bufs=1, align_bytes=64)
             nc.sync.dma_start(out=rows[:], in_=old_rows[s // PACK, s % PACK])
             old_tiles[s] = rows
 
         load_conf(0)
         load_conf(1)
+        load_w1(1, 0)
         load_conf(2)
+        load_w1(1, 1)
         load_old(0)
-        load_w1(1)
         load_conf(3)
         load_old(1)
-        load_old(2)
         w4_codes = keep.tile([P, PASSES, 2 * N], U8, name="w4_codes", align_bytes=64)
         nc.sync.dma_start(out=w4_codes[:].bitcast(I32), in_=w4_words.rearrange("a p c -> p a c").bitcast(I32))
         w4_plane = keep.tile([P, PASSES, N], U8, name="w4_plane", align_bytes=64)
-        nc.gpsimd.memset(w4_plane[:].bitcast(I32), 0)
+        nc.vector.memset(w4_plane[:].bitcast(I32), 0)
         for q in range(4):
             nc.sync.dma_start(
                 out=w4_plane[32 * q : 32 * q + 4, :, :].bitcast(I32),
                 in_=w4_scales[:, 4 * q : 4 * q + 4, :].rearrange("a r c -> r a c").bitcast(I32),
             )
-        for s in range(3, SLICES):
-            load_old(s)
+        load_old(SLICES - 1)
 
         pages = [keep.tile([P, T2], F32, name="page%d" % n) for n in range(PAGES)]
         for page in pages:
-            nc.gpsimd.memset(page[:], 0.0)
+            nc.vector.memset(page[:], 1.0)
 
-        prep_w1(0, False)
+        for a in range(PASSES):
+            cast_w1(0, a, nc.vector.tensor_copy)
+            quantize_w1(0, a, 1)
 
         picked_scales = keep.tile([P, S], U8, name="picked_scales", align_bytes=64)
-        picked = [keep.tile([P, S], I32, name="picked%d" % a, align_bytes=64) for a in range(PASSES)]
+        nc.vector.tensor_copy(picked_scales[:], scale_win[:].indirect(pick[:]))
+        picked = [
+            ring.tile([P, S], I32, name="picked0", tag="scale_win", bufs=1, align_bytes=64),
+            keep.tile([P, S], I32, name="picked1", align_bytes=64),
+        ]
         nc.vector.tensor_copy(picked[0][:].bitcast(U32), table[0][:].bitcast(U32).indirect(pick[:]))
         for hf in range(2):
             nc.vector.tensor_copy(
-                picked_scales[:, hf * BANK : (hf + 1) * BANK], scale_win[:].indirect(pick[:, hf * 32 : (hf + 1) * 32])
-            )
-        for hf in range(2):
-            nc.vector.tensor_copy(
                 picked[1][:, hf * BANK : (hf + 1) * BANK].bitcast(U32),
-                table[1][:].bitcast(U32).indirect(pick[:, hf * 32 : (hf + 1) * 32]),
+                table[1][:].bitcast(U32).indirect(pick[:, hf * HALF : (hf + 1) * HALF]),
             )
 
-        fade = {}
-
+        occ_first = keep.tile([P, S], F32, name="occ_first")
         occs = {}
-
-        def weigh(s):
-            i = s % PACK
-            occ = occs[s]
-            if s == 0:
-                keepf = grouped[:, 0 : 2 * S].bitcast(F32)
-            elif s >= SLICES - 2:
-                keepf = woven[s % 2][:, 0 : 2 * S].bitcast(F32)
-            else:
-                keepf = swap[s % 2][:, 0:S]
-            fade[s] = keepf
-            parts = [slice(0, BANK), slice(BANK, S)] if s == 0 else [slice(0, S)]
-            for cols in parts:
-                nc.vector.scalar_tensor_tensor(keepf[:, cols], occ[:, cols], -1.0, conf[i][:, cols], MULT, MULT)
+        left = {}
 
         def logits(s):
             b, i = divmod(s, PACK)
             if s == 0:
-                occ = swap[0][:, 0:S]
+                occ = occ_first[:]
+            elif s == 1:
+                occ = grouped[:, width // 2 : width // 2 + width].bitcast(F32)
             else:
-                occ = ring.tile([P, S], F32, name="occ", bufs=1)
+                occ = planes[s - 2].bitcast(F32)
             occs[s] = occ
             for hf in range(2):
                 cols = slice(hf * BANK, (hf + 1) * BANK)
@@ -192,53 +176,49 @@ def tile_list_voxel_occupancy_map_kernel(
                     )
                 nc.scalar.activation(occ[:, cols], acc[:], SIGMOID, bias=bias[:, b, i : i + 1])
 
+        def weigh(s):
+            i = s % PACK
+            slot = "left%d" % s if s < AHEAD else "rows%d" % ((s - AHEAD) % PACK)
+            left[s] = ring.tile([P, S], F32, name="left", tag=slot, bufs=1, align_bytes=64)
+            cols = slice(0, S)
+            if s == 0:
+                first = slice(0, BANK)
+                nc.vector.tensor_tensor(left[s][:, first], occs[s][:, first], conf[i][:, first], MULT)
+                nc.vector.tensor_scalar(left[s][:, first], left[s][:, first], -1.0, 1.0, MULT, ADD)
+                cols = slice(BANK, S)
+            nc.gpsimd.tensor_tensor(left[s][:, cols], occs[s][:, cols], conf[i][:, cols], MULT)
+            nc.scalar.activation(left[s][:, cols], left[s][:, cols], COPY, bias=1.0, scale=-1.0)
+
         def scatter(s):
             page = pages[s % PAGES]
             if s == 0:
                 for hf in range(2):
-                    if hf == 1:
-                        logits(1)
-                        weigh(1)
-                        logits(2)
                     nc.vector.tensor_copy(
-                        page[:].indirect(place[:, hf * 32 : (hf + 1) * 32]), fade[s][:, hf * BANK : (hf + 1) * BANK]
+                        page[:].indirect(place[:, hf * HALF : (hf + 1) * HALF]), left[s][:, hf * BANK : (hf + 1) * BANK]
                     )
             else:
-                nc.vector.tensor_copy(page[:].indirect(place[:]), fade[s])
+                nc.vector.tensor_copy(page[:].indirect(place[:]), left[s][:])
 
         planes = {}
 
         def fade_old(s, eng, cols):
-            b, i = divmod(s, PACK)
-            if b not in planes:
-                planes[b] = ring.tile([P, PACK, T2], BF16, name="planes", tag="wide", bufs=2, align_bytes=64)
-            page = pages[s % PAGES]
-            if s == SLICES - 1:
-                eng.scalar_tensor_tensor(planes[b][:, i, cols], page[:, cols], 1.0, old_tiles[s][:, cols], ADD, MULT)
-            else:
-                left = swap[s % 2]
-                nc.scalar.activation(left[:], page[:], COPY, bias=1.0)
-                eng.tensor_tensor(planes[b][:, i, :], old_tiles[s][:], left[:], MULT)
+            eng.tensor_tensor(planes[s][:, cols], old_tiles[s][:, cols], pages[s % PAGES][:, cols], MULT)
 
-        z_codes = [keep.tile([P, T2], U32, name="zc%d" % b, align_bytes=64) for b in range(PASSES)]
+        woven = {}
+        z_codes = {}
         z_scales = [keep.tile([P, T2], U8, name="zs%d" % b, align_bytes=64) for b in range(PASSES)]
 
-        def weave(b, c, on_vector):
-            dst = woven[c // 2][:, (c % 2) * BANK * PACK : (c % 2 + 1) * BANK * PACK]
-            dst = dst.rearrange("p (c i t) -> p c t i", i=4, t=PACK)
-            src = planes[b][:, :, c * BANK : (c + 1) * BANK].rearrange("p t (c i) -> p c t i", i=4)
-            if on_vector:
-                nc.vector.tensor_copy(dst, src)
-            else:
-                nc.scalar.copy(dst, src)
+        def weave(dst, source, t0, c, copy):
+            count = source.shape[1] // T2
+            dst = dst.rearrange("p (c i t) -> p c t i", i=4, t=PACK)[:, :, t0 : t0 + count, :]
+            src = source[:].rearrange("p (t c) -> p t c", t=count)[:, :, c * BANK : (c + 1) * BANK]
+            copy(dst, src.rearrange("p t (c i) -> p c t i", i=4))
 
-        def quantize_z(b, c0, count):
-            cols = slice(c0 * BANK, (c0 + count) * BANK)
-            lo = (c0 % 2) * BANK * PACK
+        def quantize_z(b, c0, count, source):
             nc.vector.quantize_mx(
-                out=z_codes[b][:, cols].bitcast(FP8X4),
-                scales=z_scales[b][:, cols],
-                in_=woven[c0 // 2][:, lo : lo + count * BANK * PACK],
+                out=z_codes[b][:, c0 * BANK : (c0 + count) * BANK].bitcast(FP8X4),
+                scales=z_scales[b][:, c0 * BANK : (c0 + count) * BANK],
+                in_=source,
             )
 
         sums = {}
@@ -247,70 +227,107 @@ def tile_list_voxel_occupancy_map_kernel(
             c, n = divmod(g, NT)
             if b == 0:
                 sums[g] = psum.tile([P, BANK], F32, name="sums", tag="bank%d" % (g % 8))
-            cols = slice(c * BANK, (c + 1) * BANK)
             nc.tensor.matmul_mx(
                 out=sums[g][:],
                 lhsT=w4_codes[:, b, 2 * n * P : 2 * (n + 1) * P].bitcast(FP4X4),
                 lhsT_scale=w4_plane[:, b, n * P : (n + 1) * P],
-                rhs=z_codes[b][:, cols].bitcast(FP8X4),
-                rhs_scale=z_scales[b][:, cols],
+                rhs=z_codes[b][:, c * BANK : (c + 1) * BANK].bitcast(FP8X4),
+                rhs_scale=z_scales[b][:, c * BANK : (c + 1) * BANK],
                 start=(b == 0),
                 stop=(b == PASSES - 1),
             )
 
-        def store(g, on_vector):
+        def store(g, copy):
             c, n = divmod(g, NT)
             staged = ring.tile([P, BANK], F32, name="staged", bufs=6)
-            if on_vector:
-                nc.vector.tensor_copy(staged[:], sums[g][:])
-            else:
-                nc.scalar.copy(staged[:], sums[g][:])
+            copy(staged[:], sums[g][:])
             nc.sync.dma_start(out=out[n * P : (n + 1) * P, c * BANK : (c + 1) * BANK], in_=staged[:])
 
+        quad = ring.tile([P, PACK * T2], BF16, name="quad", tag="wide0", bufs=1, align_bytes=64)
+        pair_low = ring.tile([P, 2 * T2], BF16, name="pair_low", tag="wide1", bufs=1, align_bytes=64)
+        for i in range(PACK):
+            planes[i] = quad[:, i * T2 : (i + 1) * T2]
+        for i in range(2):
+            planes[PACK + i] = pair_low[:, i * T2 : (i + 1) * T2]
+        for half in range(2):
+            woven[half] = ring.tile(
+                [P, 2 * BANK * PACK], BF16, name="woven", tag="woven%d" % half, bufs=1, align_bytes=64
+            )
+        woven_last = [keep.tile([P, BANK * PACK], BF16, name="woven_last%d" % c, align_bytes=64) for c in range(CHUNKS)]
+
         logits(0)
+        logits(1)
         weigh(0)
-        for s in range(SLICES - 1):
-            scatter(s)
-            if s > PACK:
-                for c in range(2 * (s - PACK - 1), 2 * (s - PACK)):
-                    weave(0, c, False)
-                quantize_z(0, 2 * (s - PACK - 1), 2)
+        logits(2)
+        scatter(0)
+        logits(3)
+        weigh(1)
+        cast_w1(1, 0, nc.scalar.copy)
+        load_old(2)
+        weigh(2)
+        cast_w1(1, 1, nc.scalar.copy)
+        load_old(3)
+        last = SLICES - 1
+        for s in range(last):
+            if s > 0:
+                scatter(s)
+            if s == 1:
+                w1_codes[1] = ring.tile([P, PASSES * PASS], U32, name="w1c1", tag="left1", bufs=1, align_bytes=64)
+                quantize_w1(1, 0, PASSES)
+            if AHEAD <= s < last - 1:
+                load_old(s + 1)
+            if s == last - 1:
+                z_codes[0] = ring.tile([P, T2], U32, name="zc0", tag="rows%d" % (s - AHEAD), bufs=1, align_bytes=64)
+                for half in range(2):
+                    quantize_z(0, 2 * half, 2, woven[half][:])
+                pair_high = ring.tile([P, 2 * T2], BF16, name="pair_high", tag="woven1", bufs=1, align_bytes=64)
+                for i in range(2):
+                    planes[s + i] = pair_high[:, i * T2 : (i + 1) * T2]
             fade_old(s, nc.gpsimd, slice(0, T2))
-            if s == 0:
-                prep_w1(1, True)
-            else:
-                weigh(s + 1)
-                if s + 2 < SLICES:
-                    logits(s + 2)
+            if 1 <= s and s + AHEAD < SLICES:
+                logits(s + AHEAD)
+            if s + AHEAD < SLICES:
+                weigh(s + AHEAD)
+            if s == PACK - 1:
+                for c in range(CHUNKS):
+                    lo = (c % 2) * BANK * PACK
+                    weave(woven[c // 2][:, lo : lo + BANK * PACK], quad, 0, c, nc.scalar.copy)
+            if s == PACK + 1:
+                for c in range(CHUNKS):
+                    weave(woven_last[c][:], pair_low, 0, c, nc.scalar.copy)
         for g in range(8):
             readout(g, 0)
-        last = SLICES - 1
         scatter(last)
+
+        z_codes[1] = keep.tile([P, T2], U32, name="zc1", align_bytes=64)
 
         def finish(c):
             for g in range(c * NT, (c + 1) * NT):
                 readout(g, 1)
             for g in range(c * NT, (c + 1) * NT):
-                store(g, c == CHUNKS - 1 and g % 2 == 1)
+                store(g, nc.vector.tensor_copy if c == CHUNKS - 1 and g % 2 == 1 else nc.scalar.copy)
                 if g + 8 < CHUNKS * NT:
                     readout(g + 8, 0)
 
         def chunk(c):
             return slice(c * BANK, (c + 1) * BANK)
 
+        def weave_last(c, copy):
+            weave(woven_last[c][:], pair_high, 2, c, copy)
+
         fade_old(last, nc.vector, chunk(0))
         fade_old(last, nc.vector, chunk(1))
-        weave(1, 0, True)
-        weave(1, 1, False)
+        weave_last(0, nc.vector.tensor_copy)
+        weave_last(1, nc.scalar.copy)
         fade_old(last, nc.vector, chunk(2))
-        quantize_z(1, 0, 1)
+        quantize_z(1, 0, 1, woven_last[0][:])
         finish(0)
         fade_old(last, nc.vector, chunk(3))
-        weave(1, 2, True)
-        quantize_z(1, 1, 1)
+        weave_last(2, nc.vector.tensor_copy)
+        quantize_z(1, 1, 1, woven_last[1][:])
         finish(1)
-        quantize_z(1, 2, 1)
+        weave_last(3, nc.vector.tensor_copy)
+        quantize_z(1, 2, 1, woven_last[2][:])
         finish(2)
-        weave(1, 3, True)
-        quantize_z(1, 3, 1)
+        quantize_z(1, 3, 1, woven_last[3][:])
         finish(3)

@@ -26,7 +26,7 @@ PASSES = 2
 SLICES = PASSES * PACK
 CHUNKS = T2 // BANK
 NT = N // P
-PAGES = 2
+PAGES = 3
 AHEAD = 3
 HALF = BANK // 16
 
@@ -66,7 +66,7 @@ def tile_list_voxel_occupancy_map_kernel(
 
         w1_codes = {0: keep.tile([P, PASSES * PASS], U32, name="w1c0", align_bytes=64)}
         w1_scales = [keep.tile([P, PASSES * PASS], U8, name="w1s%d" % b, align_bytes=64) for b in range(PASSES)]
-        grouped = keep.tile([P, PASSES * PASS * PACK], BF16, name="grouped", align_bytes=64)
+        grouped = ring.tile([P, PASSES * PASS * PACK], BF16, name="grouped", tag="grouped", bufs=1, align_bytes=64)
         width = PASS * PACK
 
         def cast_w1(b, a, copy):
@@ -82,10 +82,11 @@ def tile_list_voxel_occupancy_map_kernel(
                 in_=grouped[:, a0 * width : (a0 + count) * width],
             )
 
-        load_w1(0, 0)
-        load_w1(0, 1)
         table = []
         for a in range(PASSES):
+            if a == 1:
+                load_w1(0, 0)
+                load_w1(0, 1)
             words = ring.tile([P, T], I32, name="words", tag="wide%d" % a, bufs=1, align_bytes=64)
             nc.sync.dma_start(out=words[:], in_=tab_words[a].rearrange("p t i -> p (t i)").bitcast(I32))
             table.append(words)
@@ -130,17 +131,18 @@ def tile_list_voxel_occupancy_map_kernel(
         for page in pages:
             nc.vector.memset(page[:], 1.0)
 
+        def page_of(s):
+            return pages[0] if s == 0 else pages[(2 - s) % PAGES]
+
         for a in range(PASSES):
             cast_w1(0, a, nc.vector.tensor_copy)
             quantize_w1(0, a, 1)
 
         picked_scales = keep.tile([P, S], U8, name="picked_scales", align_bytes=64)
-        nc.vector.tensor_copy(picked_scales[:], scale_win[:].indirect(pick[:]))
-        picked = [
-            ring.tile([P, S], I32, name="picked0", tag="scale_win", bufs=1, align_bytes=64),
-            keep.tile([P, S], I32, name="picked1", align_bytes=64),
-        ]
+        picked = [keep.tile([P, S], I32, name="picked0", align_bytes=64)]
         nc.vector.tensor_copy(picked[0][:].bitcast(U32), table[0][:].bitcast(U32).indirect(pick[:]))
+        nc.vector.tensor_copy(picked_scales[:], scale_win[:].indirect(pick[:]))
+        picked.append(ring.tile([P, S], I32, name="picked1", tag="scale_win", bufs=1, align_bytes=64))
         for hf in range(2):
             nc.vector.tensor_copy(
                 picked[1][:, hf * BANK : (hf + 1) * BANK].bitcast(U32),
@@ -156,7 +158,8 @@ def tile_list_voxel_occupancy_map_kernel(
             if s == 0:
                 occ = occ_first[:]
             elif s == 1:
-                occ = grouped[:, width // 2 : width // 2 + width].bitcast(F32)
+                occ_second = ring.tile([P, S], F32, name="occ_second", tag="left2", bufs=1, align_bytes=64)
+                occ = occ_second[:]
             else:
                 occ = planes[s - 2].bitcast(F32)
             occs[s] = occ
@@ -186,11 +189,16 @@ def tile_list_voxel_occupancy_map_kernel(
                 nc.vector.tensor_tensor(left[s][:, first], occs[s][:, first], conf[i][:, first], MULT)
                 nc.vector.tensor_scalar(left[s][:, first], left[s][:, first], -1.0, 1.0, MULT, ADD)
                 cols = slice(BANK, S)
-            nc.gpsimd.tensor_tensor(left[s][:, cols], occs[s][:, cols], conf[i][:, cols], MULT)
-            nc.scalar.activation(left[s][:, cols], left[s][:, cols], COPY, bias=1.0, scale=-1.0)
+            product = grouped[:, width // 2 : width // 2 + width].bitcast(F32) if s == 1 else left[s][:, cols]
+            views = [occs[s][:, cols], conf[i][:, cols], left[s][:, cols]]
+            if s == 0:
+                product = quad[:, 0 : 2 * T2].bitcast(F32).rearrange("p (q c) -> p q c", q=4)[:, :, 0:P]
+                views = [view.rearrange("p (q c) -> p q c", q=4) for view in views]
+            nc.gpsimd.tensor_tensor(product, views[0], views[1], MULT)
+            nc.scalar.activation(views[2], product, COPY, bias=1.0, scale=-1.0)
 
         def scatter(s):
-            page = pages[s % PAGES]
+            page = page_of(s)
             if s == 0:
                 for hf in range(2):
                     nc.vector.tensor_copy(
@@ -202,7 +210,7 @@ def tile_list_voxel_occupancy_map_kernel(
         planes = {}
 
         def fade_old(s, eng, cols):
-            eng.tensor_tensor(planes[s][:, cols], old_tiles[s][:, cols], pages[s % PAGES][:, cols], MULT)
+            eng.tensor_tensor(planes[s][:, cols], old_tiles[s][:, cols], page_of(s)[:, cols], MULT)
 
         woven = {}
         z_codes = {}
@@ -277,10 +285,7 @@ def tile_list_voxel_occupancy_map_kernel(
             if AHEAD <= s < last - 1:
                 load_old(s + 1)
             if s == last - 1:
-                z_codes[0] = ring.tile([P, T2], U32, name="zc0", tag="rows%d" % (s - AHEAD), bufs=1, align_bytes=64)
-                for half in range(2):
-                    quantize_z(0, 2 * half, 2, woven[half][:])
-                pair_high = ring.tile([P, 2 * T2], BF16, name="pair_high", tag="woven1", bufs=1, align_bytes=64)
+                pair_high = ring.tile([P, 2 * T2], BF16, name="pair_high", tag="rows1", bufs=1, align_bytes=64)
                 for i in range(2):
                     planes[s + i] = pair_high[:, i * T2 : (i + 1) * T2]
             fade_old(s, nc.gpsimd, slice(0, T2))
@@ -295,19 +300,16 @@ def tile_list_voxel_occupancy_map_kernel(
             if s == PACK + 1:
                 for c in range(CHUNKS):
                     weave(woven_last[c][:], pair_low, 0, c, nc.scalar.copy)
-        for g in range(8):
-            readout(g, 0)
         scatter(last)
 
+        z_codes[0] = ring.tile([P, T2], U32, name="zc0", tag="rows0", bufs=1, align_bytes=64)
         z_codes[1] = keep.tile([P, T2], U32, name="zc1", align_bytes=64)
 
         def finish(c):
             for g in range(c * NT, (c + 1) * NT):
                 readout(g, 1)
             for g in range(c * NT, (c + 1) * NT):
-                store(g, nc.vector.tensor_copy if c == CHUNKS - 1 and g % 2 == 1 else nc.scalar.copy)
-                if g + 8 < CHUNKS * NT:
-                    readout(g + 8, 0)
+                store(g, nc.vector.tensor_copy if c == CHUNKS - 1 and g % 2 == 0 else nc.scalar.copy)
 
         def chunk(c):
             return slice(c * BANK, (c + 1) * BANK)
@@ -315,19 +317,26 @@ def tile_list_voxel_occupancy_map_kernel(
         def weave_last(c, copy):
             weave(woven_last[c][:], pair_high, 2, c, copy)
 
+        def first_pass(c):
+            lo = (c % 2) * BANK * PACK
+            quantize_z(0, c, 1, woven[c // 2][:, lo : lo + BANK * PACK])
+            for g in range(c * NT, (c + 1) * NT):
+                readout(g, 0)
+
+        def second_pass(c):
+            quantize_z(1, c, 1, woven_last[c][:])
+            finish(c)
+
         fade_old(last, nc.vector, chunk(0))
+        first_pass(0)
         fade_old(last, nc.vector, chunk(1))
         weave_last(0, nc.vector.tensor_copy)
         weave_last(1, nc.scalar.copy)
-        fade_old(last, nc.vector, chunk(2))
-        quantize_z(1, 0, 1, woven_last[0][:])
-        finish(0)
-        fade_old(last, nc.vector, chunk(3))
-        weave_last(2, nc.vector.tensor_copy)
-        quantize_z(1, 1, 1, woven_last[1][:])
-        finish(1)
-        weave_last(3, nc.vector.tensor_copy)
-        quantize_z(1, 2, 1, woven_last[2][:])
-        finish(2)
-        quantize_z(1, 3, 1, woven_last[3][:])
-        finish(3)
+        first_pass(1)
+        second_pass(0)
+        for c in range(2, CHUNKS):
+            fade_old(last, nc.vector, chunk(c))
+            second_pass(c - 1)
+            weave_last(c, nc.vector.tensor_copy)
+            first_pass(c)
+        second_pass(CHUNKS - 1)

@@ -26,7 +26,8 @@ PASSES = 2
 SLICES = PASSES * PACK
 CHUNKS = T2 // BANK
 NT = N // P
-PAGES = 3
+PAGES = 2
+ON_VECTOR = (3, 5)
 AHEAD = 3
 HALF = BANK // 16
 
@@ -113,8 +114,8 @@ def tile_list_voxel_occupancy_map_kernel(
         load_w1(1, 0)
         load_conf(2)
         load_w1(1, 1)
-        load_old(0)
         load_conf(3)
+        load_old(0)
         load_old(1)
         w4_codes = keep.tile([P, PASSES, 2 * N], U8, name="w4_codes", align_bytes=64)
         nc.sync.dma_start(out=w4_codes[:].bitcast(I32), in_=w4_words.rearrange("a p c -> p a c").bitcast(I32))
@@ -132,7 +133,7 @@ def tile_list_voxel_occupancy_map_kernel(
             nc.vector.memset(page[:], 1.0)
 
         def page_of(s):
-            return pages[0] if s == 0 else pages[(2 - s) % PAGES]
+            return pages[s % PAGES]
 
         for a in range(PASSES):
             cast_w1(0, a, nc.vector.tensor_copy)
@@ -149,7 +150,8 @@ def tile_list_voxel_occupancy_map_kernel(
                 table[1][:].bitcast(U32).indirect(pick[:, hf * HALF : (hf + 1) * HALF]),
             )
 
-        occ_first = keep.tile([P, S], F32, name="occ_first")
+        occ_first = keep.tile([P, BANK], F32, name="occ_first")
+        handover = grouped[:, width // 2 : width // 2 + width].bitcast(F32)
         occs = {}
         left = {}
 
@@ -165,6 +167,8 @@ def tile_list_voxel_occupancy_map_kernel(
             occs[s] = occ
             for hf in range(2):
                 cols = slice(hf * BANK, (hf + 1) * BANK)
+                if s == 0 and hf == 1:
+                    occ = handover
                 acc = psum.tile([P, BANK], F32, name="acc", tag="bank%d" % (4 + (2 * s + hf) % 4))
                 for a in range(PASSES):
                     wcols = slice(a * PASS + i * P, a * PASS + (i + 1) * P)
@@ -189,12 +193,15 @@ def tile_list_voxel_occupancy_map_kernel(
                 nc.vector.tensor_tensor(left[s][:, first], occs[s][:, first], conf[i][:, first], MULT)
                 nc.vector.tensor_scalar(left[s][:, first], left[s][:, first], -1.0, 1.0, MULT, ADD)
                 cols = slice(BANK, S)
-            product = grouped[:, width // 2 : width // 2 + width].bitcast(F32) if s == 1 else left[s][:, cols]
-            views = [occs[s][:, cols], conf[i][:, cols], left[s][:, cols]]
+            product = handover if s == 1 else left[s][:, cols]
+            views = [(handover if s == 0 else occs[s])[:, cols], conf[i][:, cols], left[s][:, cols]]
             if s == 0:
                 product = quad[:, 0 : 2 * T2].bitcast(F32).rearrange("p (q c) -> p q c", q=4)[:, :, 0:P]
                 views = [view.rearrange("p (q c) -> p q c", q=4) for view in views]
-            nc.gpsimd.tensor_tensor(product, views[0], views[1], MULT)
+            if s == AHEAD:
+                product = pair_low[:, T2 // 2 : T2 // 2 + T2].bitcast(F32)
+            engine = nc.vector if s in ON_VECTOR else nc.gpsimd
+            engine.tensor_tensor(product, views[0], views[1], MULT)
             nc.scalar.activation(views[2], product, COPY, bias=1.0, scale=-1.0)
 
         def scatter(s):
@@ -282,6 +289,8 @@ def tile_list_voxel_occupancy_map_kernel(
             if s == 1:
                 w1_codes[1] = ring.tile([P, PASSES * PASS], U32, name="w1c1", tag="left1", bufs=1, align_bytes=64)
                 quantize_w1(1, 0, PASSES)
+            if s + AHEAD - 1 in ON_VECTOR:
+                weigh(s + AHEAD - 1)
             if AHEAD <= s < last - 1:
                 load_old(s + 1)
             if s == last - 1:
@@ -291,7 +300,7 @@ def tile_list_voxel_occupancy_map_kernel(
             fade_old(s, nc.gpsimd, slice(0, T2))
             if 1 <= s and s + AHEAD < SLICES:
                 logits(s + AHEAD)
-            if s + AHEAD < SLICES:
+            if s + AHEAD < SLICES and s + AHEAD not in ON_VECTOR:
                 weigh(s + AHEAD)
             if s == PACK - 1:
                 for c in range(CHUNKS):

@@ -26,8 +26,7 @@ PASSES = 2
 SLICES = PASSES * PACK
 CHUNKS = T2 // BANK
 NT = N // P
-PAGES = 2
-ON_VECTOR = (3, 5)
+PAGES = 3
 AHEAD = 3
 HALF = BANK // 16
 
@@ -47,11 +46,12 @@ def tile_list_voxel_occupancy_map_kernel(
 
         scale_win = ring.tile([P, T], U8, name="scale_win", tag="scale_win", bufs=1, align_bytes=64)
         nc.vector.memset(scale_win[:].bitcast(I32), 0)
-        for q in range(4):
-            nc.gpsimd.dma_start(
-                out=scale_win[32 * q : 32 * q + 8, :].bitcast(I32),
-                in_=tab_scales[:, 4 * q : 4 * q + 4, :].bitcast(I32),
-            )
+        for a in range(PASSES):
+            for q in range(4):
+                nc.scalar.dma_start(
+                    out=scale_win[32 * q + 4 * a : 32 * q + 4 * a + 4, :].bitcast(I32),
+                    in_=tab_scales[a, 4 * q : 4 * q + 4, :].bitcast(I32),
+                )
         bias = keep.tile([P, PASSES, PACK], F32, name="bias")
         nc.scalar.dma_start(out=bias[:], in_=b1.rearrange("(b p i) -> p b i", b=PASSES, i=PACK))
 
@@ -93,18 +93,20 @@ def tile_list_voxel_occupancy_map_kernel(
             table.append(words)
         nc.sync.dma_start(place[:], offs2)
 
-        conf = [keep.tile([P, S], F32, name="conf%d" % i) for i in range(PACK)]
+        conf_pairs = [keep.tile([P, 2 * S], F32, name="conf%d" % n, align_bytes=64) for n in range(2)]
+        conf = [conf_pairs[i // 2][:, (i % 2) * S : (i % 2 + 1) * S] for i in range(PACK)]
         conf_rows = wgs.rearrange("(m i) j -> i m j", i=PACK)
 
         def load_conf(i):
             for q in (0, 2, 1, 3):
-                nc.sync.dma_start(out=conf[i][32 * q : 32 * q + 32, :], in_=conf_rows[i])
+                nc.sync.dma_start(out=conf_pairs[i // 2][32 * q : 32 * q + 32, (i % 2) * S : (i % 2 + 1) * S], in_=conf_rows[i])
 
         old_rows = old.rearrange("(b p i) t -> b i p t", b=PASSES, i=PACK)
         old_tiles = {}
+        old_slot = ["rows0", "rows1", "rows2", "rows3", "wide1", "rows4", "rows2", "rows5"]
 
         def load_old(s):
-            slot = "rows%d" % (s % PACK if s < SLICES - 1 else PACK)
+            slot = old_slot[s]
             rows = ring.tile([P, T2], F32, name="rows", tag=slot, bufs=1, align_bytes=64)
             nc.sync.dma_start(out=rows[:], in_=old_rows[s // PACK, s % PACK])
             old_tiles[s] = rows
@@ -126,6 +128,7 @@ def tile_list_voxel_occupancy_map_kernel(
                 out=w4_plane[32 * q : 32 * q + 4, :, :].bitcast(I32),
                 in_=w4_scales[:, 4 * q : 4 * q + 4, :].rearrange("a r c -> r a c").bitcast(I32),
             )
+        load_old(PACK + 1)
         load_old(SLICES - 1)
 
         pages = [keep.tile([P, T2], F32, name="page%d" % n) for n in range(PAGES)]
@@ -133,7 +136,7 @@ def tile_list_voxel_occupancy_map_kernel(
             nc.vector.memset(page[:], 1.0)
 
         def page_of(s):
-            return pages[s % PAGES]
+            return pages[0] if s == 0 else pages[(2 - s) % PAGES]
 
         for a in range(PASSES):
             cast_w1(0, a, nc.vector.tensor_copy)
@@ -153,6 +156,7 @@ def tile_list_voxel_occupancy_map_kernel(
         occ_first = keep.tile([P, BANK], F32, name="occ_first")
         handover = grouped[:, width // 2 : width // 2 + width].bitcast(F32)
         occs = {}
+        spare = {}
         left = {}
 
         def logits(s):
@@ -162,8 +166,10 @@ def tile_list_voxel_occupancy_map_kernel(
             elif s == 1:
                 occ_second = ring.tile([P, S], F32, name="occ_second", tag="left2", bufs=1, align_bytes=64)
                 occ = occ_second[:]
-            else:
+            elif s < SLICES - 2:
                 occ = planes[s - 2].bitcast(F32)
+            else:
+                occ = spare[s - AHEAD]
             occs[s] = occ
             for hf in range(2):
                 cols = slice(hf * BANK, (hf + 1) * BANK)
@@ -185,23 +191,25 @@ def tile_list_voxel_occupancy_map_kernel(
 
         def weigh(s):
             i = s % PACK
-            slot = "left%d" % s if s < AHEAD else "rows%d" % ((s - AHEAD) % PACK)
-            left[s] = ring.tile([P, S], F32, name="left", tag=slot, bufs=1, align_bytes=64)
+            slot = "left%d" % s if s < AHEAD else old_slot[s - AHEAD]
+            if s in (AHEAD, AHEAD + 1):
+                both = ring.tile([P, 2 * S], F32, name="both", tag=slot, bufs=1, align_bytes=64)
+                left[s], spare[s] = both[:, 0:S], both[:, S : 2 * S]
+            else:
+                left_tile = ring.tile([P, S], F32, name="left_tile", tag=slot, bufs=1, align_bytes=64)
+                left[s] = left_tile[:]
             cols = slice(0, S)
             if s == 0:
                 first = slice(0, BANK)
                 nc.vector.tensor_tensor(left[s][:, first], occs[s][:, first], conf[i][:, first], MULT)
                 nc.vector.tensor_scalar(left[s][:, first], left[s][:, first], -1.0, 1.0, MULT, ADD)
                 cols = slice(BANK, S)
-            product = handover if s == 1 else left[s][:, cols]
+            product = handover if s == 1 else spare.get(s, left[s])[:, cols]
             views = [(handover if s == 0 else occs[s])[:, cols], conf[i][:, cols], left[s][:, cols]]
             if s == 0:
                 product = quad[:, 0 : 2 * T2].bitcast(F32).rearrange("p (q c) -> p q c", q=4)[:, :, 0:P]
                 views = [view.rearrange("p (q c) -> p q c", q=4) for view in views]
-            if s == AHEAD:
-                product = pair_low[:, T2 // 2 : T2 // 2 + T2].bitcast(F32)
-            engine = nc.vector if s in ON_VECTOR else nc.gpsimd
-            engine.tensor_tensor(product, views[0], views[1], MULT)
+            nc.gpsimd.tensor_tensor(product, views[0], views[1], MULT)
             nc.scalar.activation(views[2], product, COPY, bias=1.0, scale=-1.0)
 
         def scatter(s):
@@ -212,7 +220,7 @@ def tile_list_voxel_occupancy_map_kernel(
                         page[:].indirect(place[:, hf * HALF : (hf + 1) * HALF]), left[s][:, hf * BANK : (hf + 1) * BANK]
                     )
             else:
-                nc.vector.tensor_copy(page[:].indirect(place[:]), left[s][:])
+                nc.vector.tensor_copy(page[:].indirect(place[:]), left[s])
 
         planes = {}
 
@@ -226,7 +234,7 @@ def tile_list_voxel_occupancy_map_kernel(
         def weave(dst, source, t0, c, copy):
             count = source.shape[1] // T2
             dst = dst.rearrange("p (c i t) -> p c t i", i=4, t=PACK)[:, :, t0 : t0 + count, :]
-            src = source[:].rearrange("p (t c) -> p t c", t=count)[:, :, c * BANK : (c + 1) * BANK]
+            src = source.rearrange("p (t c) -> p t c", t=count)[:, :, c * BANK : (c + 1) * BANK]
             copy(dst, src.rearrange("p t (c i) -> p c t i", i=4))
 
         def quantize_z(b, c0, count, source):
@@ -254,12 +262,12 @@ def tile_list_voxel_occupancy_map_kernel(
 
         def store(g, copy):
             c, n = divmod(g, NT)
-            staged = ring.tile([P, BANK], F32, name="staged", bufs=6)
+            staged = ring.tile([P, BANK], F32, name="staged", bufs=12)
             copy(staged[:], sums[g][:])
             nc.sync.dma_start(out=out[n * P : (n + 1) * P, c * BANK : (c + 1) * BANK], in_=staged[:])
 
         quad = ring.tile([P, PACK * T2], BF16, name="quad", tag="wide0", bufs=1, align_bytes=64)
-        pair_low = ring.tile([P, 2 * T2], BF16, name="pair_low", tag="wide1", bufs=1, align_bytes=64)
+        pair_low = conf_pairs[1][:].bitcast(BF16)
         for i in range(PACK):
             planes[i] = quad[:, i * T2 : (i + 1) * T2]
         for i in range(2):
@@ -282,6 +290,7 @@ def tile_list_voxel_occupancy_map_kernel(
         weigh(2)
         cast_w1(1, 1, nc.scalar.copy)
         load_old(3)
+        load_old(4)
         last = SLICES - 1
         for s in range(last):
             if s > 0:
@@ -289,29 +298,27 @@ def tile_list_voxel_occupancy_map_kernel(
             if s == 1:
                 w1_codes[1] = ring.tile([P, PASSES * PASS], U32, name="w1c1", tag="left1", bufs=1, align_bytes=64)
                 quantize_w1(1, 0, PASSES)
-            if s + AHEAD - 1 in ON_VECTOR:
-                weigh(s + AHEAD - 1)
-            if AHEAD <= s < last - 1:
+            if s == last - 2:
                 load_old(s + 1)
             if s == last - 1:
-                pair_high = ring.tile([P, 2 * T2], BF16, name="pair_high", tag="rows1", bufs=1, align_bytes=64)
+                pair_high = ring.tile([P, 2 * T2], BF16, name="pair_high", tag=old_slot[s - 1], bufs=1, align_bytes=64)
                 for i in range(2):
                     planes[s + i] = pair_high[:, i * T2 : (i + 1) * T2]
             fade_old(s, nc.gpsimd, slice(0, T2))
             if 1 <= s and s + AHEAD < SLICES:
                 logits(s + AHEAD)
-            if s + AHEAD < SLICES and s + AHEAD not in ON_VECTOR:
+            if s + AHEAD < SLICES:
                 weigh(s + AHEAD)
             if s == PACK - 1:
                 for c in range(CHUNKS):
                     lo = (c % 2) * BANK * PACK
-                    weave(woven[c // 2][:, lo : lo + BANK * PACK], quad, 0, c, nc.scalar.copy)
+                    weave(woven[c // 2][:, lo : lo + BANK * PACK], quad[:], 0, c, nc.scalar.copy)
             if s == PACK + 1:
                 for c in range(CHUNKS):
                     weave(woven_last[c][:], pair_low, 0, c, nc.scalar.copy)
         scatter(last)
 
-        z_codes[0] = ring.tile([P, T2], U32, name="zc0", tag="rows0", bufs=1, align_bytes=64)
+        z_codes[0] = ring.tile([P, T2], U32, name="zc0", tag=old_slot[last - AHEAD], bufs=1, align_bytes=64)
         z_codes[1] = keep.tile([P, T2], U32, name="zc1", align_bytes=64)
 
         def finish(c):
@@ -324,7 +331,7 @@ def tile_list_voxel_occupancy_map_kernel(
             return slice(c * BANK, (c + 1) * BANK)
 
         def weave_last(c, copy):
-            weave(woven_last[c][:], pair_high, 2, c, copy)
+            weave(woven_last[c][:], pair_high[:], 2, c, copy)
 
         def first_pass(c):
             lo = (c % 2) * BANK * PACK
@@ -338,11 +345,11 @@ def tile_list_voxel_occupancy_map_kernel(
 
         fade_old(last, nc.vector, chunk(0))
         first_pass(0)
-        fade_old(last, nc.vector, chunk(1))
         weave_last(0, nc.vector.tensor_copy)
+        fade_old(last, nc.vector, chunk(1))
         weave_last(1, nc.scalar.copy)
-        first_pass(1)
         second_pass(0)
+        first_pass(1)
         for c in range(2, CHUNKS):
             fade_old(last, nc.vector, chunk(c))
             second_pass(c - 1)

@@ -113,24 +113,12 @@ def tile_list_voxel_occupancy_map_kernel(
 
         load_conf(0)
         load_conf(1)
-        load_w1(1, 0)
         load_conf(2)
+        load_old(0)
+        load_w1(1, 0)
         load_w1(1, 1)
         load_conf(3)
-        load_old(0)
         load_old(1)
-        w4_codes = keep.tile([P, PASSES, 2 * N], U8, name="w4_codes", align_bytes=64)
-        nc.sync.dma_start(out=w4_codes[:].bitcast(I32), in_=w4_words.rearrange("a p c -> p a c").bitcast(I32))
-        w4_plane = keep.tile([P, PASSES, N], U8, name="w4_plane", align_bytes=64)
-        nc.vector.memset(w4_plane[:].bitcast(I32), 0)
-        for q in range(4):
-            nc.sync.dma_start(
-                out=w4_plane[32 * q : 32 * q + 4, :, :].bitcast(I32),
-                in_=w4_scales[:, 4 * q : 4 * q + 4, :].rearrange("a r c -> r a c").bitcast(I32),
-            )
-        load_old(PACK + 1)
-        load_old(SLICES - 1)
-
         pages = [keep.tile([P, T2], F32, name="page%d" % n) for n in range(PAGES)]
         for page in pages:
             nc.vector.memset(page[:], 1.0)
@@ -187,11 +175,18 @@ def tile_list_voxel_occupancy_map_kernel(
                         start=(a == 0),
                         stop=(a == PASSES - 1),
                     )
-                nc.scalar.activation(occ[:, cols], acc[:], SIGMOID, bias=bias[:, b, i : i + 1])
+                step = BANK // 2 if s == 0 and hf == 0 else BANK
+                for lo in range(0, BANK, step):
+                    part = slice(cols.start + lo, cols.start + lo + step)
+                    nc.scalar.activation(occ[:, part], acc[:, lo : lo + step], SIGMOID, bias=bias[:, b, i : i + 1])
 
         def weigh(s):
             i = s % PACK
             slot = "left%d" % s if s < AHEAD else old_slot[s - AHEAD]
+            if s == 2:
+                product_tile = ring.tile([P, S], F32, name="product_tile", tag=slot, bufs=1, align_bytes=64)
+                spare[s] = product_tile[:]
+                slot = old_slot[3]
             if s in (AHEAD, AHEAD + 1):
                 both = ring.tile([P, 2 * S], F32, name="both", tag=slot, bufs=1, align_bytes=64)
                 left[s], spare[s] = both[:, 0:S], both[:, S : 2 * S]
@@ -200,9 +195,11 @@ def tile_list_voxel_occupancy_map_kernel(
                 left[s] = left_tile[:]
             cols = slice(0, S)
             if s == 0:
-                first = slice(0, BANK)
-                nc.vector.tensor_tensor(left[s][:, first], occs[s][:, first], conf[i][:, first], MULT)
-                nc.vector.tensor_scalar(left[s][:, first], left[s][:, first], -1.0, 1.0, MULT, ADD)
+                quarters = [slice(0, BANK // 2), slice(BANK // 2, BANK)]
+                for part in quarters:
+                    nc.vector.tensor_tensor(left[s][:, part], occs[s][:, part], conf[i][:, part], MULT)
+                for part in quarters:
+                    nc.vector.tensor_scalar(left[s][:, part], left[s][:, part], -1.0, 1.0, MULT, ADD)
                 cols = slice(BANK, S)
             product = handover if s == 1 else spare.get(s, left[s])[:, cols]
             views = [(handover if s == 0 else occs[s])[:, cols], conf[i][:, cols], left[s][:, cols]]
@@ -287,10 +284,21 @@ def tile_list_voxel_occupancy_map_kernel(
         weigh(1)
         cast_w1(1, 0, nc.scalar.copy)
         load_old(2)
-        weigh(2)
         cast_w1(1, 1, nc.scalar.copy)
-        load_old(3)
+        weigh(2)
         load_old(4)
+        w4_codes = keep.tile([P, PASSES, 2 * N], U8, name="w4_codes", align_bytes=64)
+        nc.sync.dma_start(out=w4_codes[:].bitcast(I32), in_=w4_words.rearrange("a p c -> p a c").bitcast(I32))
+        w4_plane = keep.tile([P, PASSES, N], U8, name="w4_plane", align_bytes=64)
+        nc.vector.memset(w4_plane[:].bitcast(I32), 0)
+        for q in range(4):
+            nc.sync.dma_start(
+                out=w4_plane[32 * q : 32 * q + 4, :, :].bitcast(I32),
+                in_=w4_scales[:, 4 * q : 4 * q + 4, :].rearrange("a r c -> r a c").bitcast(I32),
+            )
+        load_old(PACK + 1)
+        load_old(SLICES - 1)
+        load_old(3)
         last = SLICES - 1
         for s in range(last):
             if s > 0:

@@ -28,7 +28,8 @@ CHUNKS = T2 // BANK
 NT = N // P
 PAGES = 3
 AHEAD = 3
-HALF = BANK // 16
+STRIPE = 16
+QUARTER = BANK // 2
 
 
 def tile_list_voxel_occupancy_map_kernel(
@@ -37,14 +38,17 @@ def tile_list_voxel_occupancy_map_kernel(
     nc = tc.nc
     with ExitStack() as ctx:
         keep = ctx.enter_context(tc.tile_pool(name="keep", bufs=1))
-        ring = ctx.enter_context(tc.tile_pool(name="ring", bufs=2))
+        slots = ctx.enter_context(tc.tile_pool(name="slots", bufs=1))
         psum = ctx.enter_context(tc.psum_pool(name="psum", bufs=1))
 
-        pick = keep.tile([P, S // 16], U16, name="pick")
-        place = keep.tile([P, S // 16], U16, name="place")
+        def tenant(tag, columns, dtype):
+            return slots.tile([P, columns], dtype, name="tenant", tag=tag, align_bytes=64)
+
+        pick = keep.tile([P, S // STRIPE], U16, name="pick")
+        place = keep.tile([P, S // STRIPE], U16, name="place")
         nc.sync.dma_start(pick[:], offs)
 
-        scale_win = ring.tile([P, T], U8, name="scale_win", tag="scale_win", bufs=1, align_bytes=64)
+        scale_win = tenant("scale_win", T, U8)
         nc.vector.memset(scale_win[:].bitcast(I32), 0)
         for a in range(PASSES):
             for q in range(4):
@@ -58,22 +62,22 @@ def tile_list_voxel_occupancy_map_kernel(
         w1_raw = {}
 
         def load_w1(b, a):
-            raw = ring.tile([P, PACK, PASS], F32, name="raw", tag="rows%d" % (2 * b + a), bufs=1, align_bytes=64)
+            raw = tenant("rows%d" % (2 * b + a), PACK * PASS, F32)
             nc.sync.dma_start(
-                out=raw[:],
+                out=raw[:].rearrange("p (j c) -> p j c", j=PACK),
                 in_=w1[a * PASS : (a + 1) * PASS, b * PASS : (b + 1) * PASS].rearrange("(p j) c -> p j c", j=PACK),
             )
             w1_raw[(a, b)] = raw
 
-        w1_codes = {0: keep.tile([P, PASSES * PASS], U32, name="w1c0", align_bytes=64)}
+        w1_codes = [keep.tile([P, PASSES * PASS], U32, name="w1c%d" % b, align_bytes=64) for b in range(PASSES)]
         w1_scales = [keep.tile([P, PASSES * PASS], U8, name="w1s%d" % b, align_bytes=64) for b in range(PASSES)]
-        grouped = ring.tile([P, PASSES * PASS * PACK], BF16, name="grouped", tag="grouped", bufs=1, align_bytes=64)
+        grouped = keep.tile([P, PASSES * PASS * PACK], BF16, name="grouped", align_bytes=64)
         width = PASS * PACK
 
         def cast_w1(b, a, copy):
             copy(
                 grouped[:, a * width : (a + 1) * width].rearrange("p (t m j) -> p m j t", t=PACK, j=PACK),
-                w1_raw[(a, b)][:].rearrange("p j (m t) -> p m j t", t=PACK),
+                w1_raw[(a, b)][:].rearrange("p (j m t) -> p m j t", j=PACK, t=PACK),
             )
 
         def quantize_w1(b, a0, count):
@@ -88,12 +92,12 @@ def tile_list_voxel_occupancy_map_kernel(
             if a == 1:
                 load_w1(0, 0)
                 load_w1(0, 1)
-            words = ring.tile([P, T], I32, name="words", tag="wide%d" % a, bufs=1, align_bytes=64)
+            words = tenant("wide%d" % a, T, I32)
             nc.sync.dma_start(out=words[:], in_=tab_words[a].rearrange("p t i -> p (t i)").bitcast(I32))
             table.append(words)
         nc.sync.dma_start(place[:], offs2)
 
-        conf_pairs = [keep.tile([P, 2 * S], F32, name="conf%d" % n, align_bytes=64) for n in range(2)]
+        conf_pairs = [tenant("conf%d" % n, 2 * S, F32) for n in range(2)]
         conf = [conf_pairs[i // 2][:, (i % 2) * S : (i % 2 + 1) * S] for i in range(PACK)]
         conf_rows = wgs.rearrange("(m i) j -> i m j", i=PACK)
 
@@ -103,13 +107,23 @@ def tile_list_voxel_occupancy_map_kernel(
 
         old_rows = old.rearrange("(b p i) t -> b i p t", b=PASSES, i=PACK)
         old_tiles = {}
-        old_slot = ["rows0", "rows1", "rows2", "rows3", "wide1", "rows4", "rows2", "rows5"]
+        old_slot = ["rows4", "rows5", "rows0", "rows1", "rows2", "rows3"]
 
         def load_old(s):
-            slot = old_slot[s]
-            rows = ring.tile([P, T2], F32, name="rows", tag=slot, bufs=1, align_bytes=64)
-            nc.sync.dma_start(out=rows[:], in_=old_rows[s // PACK, s % PACK])
+            if s == 6:
+                rows = pair_words(1, F32)[:, :, 1, :]
+            else:
+                rows_tile = tenant(old_slot[s], T2, F32)
+                rows = rows_tile[:].rearrange("p (c t) -> p c t", c=CHUNKS)
+            nc.sync.dma_start(out=rows, in_=old_rows[s // PACK, s % PACK].rearrange("p (c t) -> p c t", c=CHUNKS))
             old_tiles[s] = rows
+
+        old_last = {}
+
+        def load_old_last():
+            for c in range(CHUNKS):
+                old_last[c] = tenant("last%d" % c, BANK, F32)
+                nc.sync.dma_start(out=old_last[c][:], in_=old_rows[PASSES - 1, PACK - 1][:, c * BANK : (c + 1) * BANK])
 
         load_conf(0)
         load_conf(1)
@@ -123,169 +137,186 @@ def tile_list_voxel_occupancy_map_kernel(
         for page in pages:
             nc.vector.memset(page[:], 1.0)
 
-        def page_of(s):
-            return pages[0] if s == 0 else pages[(2 - s) % PAGES]
-
+        cast_w1(0, 0, nc.scalar.copy)
+        cast_w1(0, 1, nc.vector.tensor_copy)
         for a in range(PASSES):
-            cast_w1(0, a, nc.vector.tensor_copy)
             quantize_w1(0, a, 1)
+        load_old(2)
+        load_old(3)
 
         picked_scales = keep.tile([P, S], U8, name="picked_scales", align_bytes=64)
         picked = [keep.tile([P, S], I32, name="picked0", align_bytes=64)]
         nc.vector.tensor_copy(picked[0][:].bitcast(U32), table[0][:].bitcast(U32).indirect(pick[:]))
         nc.vector.tensor_copy(picked_scales[:], scale_win[:].indirect(pick[:]))
-        picked.append(ring.tile([P, S], I32, name="picked1", tag="scale_win", bufs=1, align_bytes=64))
-        for hf in range(2):
-            nc.vector.tensor_copy(
-                picked[1][:, hf * BANK : (hf + 1) * BANK].bitcast(U32),
-                table[1][:].bitcast(U32).indirect(pick[:, hf * HALF : (hf + 1) * HALF]),
-            )
+        picked.append(tenant("scale_win", S, I32))
 
-        occ_first = keep.tile([P, BANK], F32, name="occ_first")
-        handover = grouped[:, width // 2 : width // 2 + width].bitcast(F32)
-        occs = {}
-        spare = {}
+        def entries(offsets, cols):
+            return offsets[:, cols.start // STRIPE : cols.stop // STRIPE]
+
+        for hf in range(2):
+            cols = slice(hf * BANK, (hf + 1) * BANK)
+            nc.vector.tensor_copy(picked[1][:, cols].bitcast(U32), table[1][:].bitcast(U32).indirect(entries(pick, cols)))
+
+        pairs = [tenant("wide%d" % b, PACK * T2, BF16) for b in range(PASSES)]
+        spare_occ = [keep.tile([P, S], F32, name="spare_occ%d" % n, align_bytes=64) for n in range(2)]
+
+        pair_order = ["h c t", "c h t"]
+
+        def pair_words(b, word):
+            return pairs[b][:].bitcast(word).rearrange("p (%s) -> p c h t" % pair_order[b], c=CHUNKS, h=2)
+
+        def plane_of(s):
+            b, i = divmod(s, PACK)
+            halves = pairs[b][:].rearrange("p (%s e) -> p c h t e" % pair_order[b], c=CHUNKS, h=2, e=2)
+            return halves[:, :, i // 2, :, i % 2]
+
+        def occ_of(s):
+            if s in (2, 4):
+                return pairs[0][:].bitcast(F32)[:, (s // 2 - 1) * T2 : (s // 2 - 1) * T2 + S]
+            if s in (6, 7):
+                return pairs[1][:].bitcast(F32)[:, (s - 6) * S : (s - 5) * S]
+            return spare_occ[{0: 0, 1: 1, 3: 0, 5: 1}[s]][:]
+
+        def pieces_of(s):
+            if s == 0:
+                return [slice(0, QUARTER), slice(QUARTER, BANK), slice(BANK, S)]
+            return [slice(0, BANK), slice(BANK, S)]
+
+        banks_used = [0]
+
+        def logits(s, cols):
+            b, i = divmod(s, PACK)
+            acc = psum.tile([P, BANK], F32, name="acc", tag="bank%d" % (4 + banks_used[0] % 4))
+            banks_used[0] = banks_used[0] + 1
+            count = cols.stop - cols.start
+            for a in range(PASSES):
+                wcols = slice(a * PASS + i * P, a * PASS + (i + 1) * P)
+                nc.tensor.matmul_mx(
+                    out=acc[:, 0:count],
+                    lhsT=w1_codes[b][:, wcols].bitcast(FP8X4),
+                    lhsT_scale=w1_scales[b][:, wcols],
+                    rhs=picked[a][:, cols].bitcast(FP8X4),
+                    rhs_scale=picked_scales[4 * a : P, cols],
+                    start=(a == 0),
+                    stop=(a == PASSES - 1),
+                )
+            nc.scalar.activation(occ_of(s)[:, cols], acc[:, 0:count], SIGMOID, bias=bias[:, b, i : i + 1])
+
+        product = {}
         left = {}
 
-        def logits(s):
-            b, i = divmod(s, PACK)
-            if s == 0:
-                occ = occ_first[:]
-            elif s == 1:
-                occ_second = ring.tile([P, S], F32, name="occ_second", tag="left2", bufs=1, align_bytes=64)
-                occ = occ_second[:]
-            elif s < SLICES - 2:
-                occ = planes[s - 2].bitcast(F32)
-            else:
-                occ = spare[s - AHEAD]
-            occs[s] = occ
-            for hf in range(2):
-                cols = slice(hf * BANK, (hf + 1) * BANK)
-                if s == 0 and hf == 1:
-                    occ = handover
-                acc = psum.tile([P, BANK], F32, name="acc", tag="bank%d" % (4 + (2 * s + hf) % 4))
-                for a in range(PASSES):
-                    wcols = slice(a * PASS + i * P, a * PASS + (i + 1) * P)
-                    nc.tensor.matmul_mx(
-                        out=acc[:],
-                        lhsT=w1_codes[b][:, wcols].bitcast(FP8X4),
-                        lhsT_scale=w1_scales[b][:, wcols],
-                        rhs=picked[a][:, cols].bitcast(FP8X4),
-                        rhs_scale=picked_scales[4 * a : P, cols],
-                        start=(a == 0),
-                        stop=(a == PASSES - 1),
-                    )
-                step = BANK // 2 if s == 0 and hf == 0 else BANK
-                for lo in range(0, BANK, step):
-                    part = slice(cols.start + lo, cols.start + lo + step)
-                    nc.scalar.activation(occ[:, part], acc[:, lo : lo + step], SIGMOID, bias=bias[:, b, i : i + 1])
-
-        def weigh(s):
-            i = s % PACK
-            slot = "left%d" % s if s < AHEAD else old_slot[s - AHEAD]
+        def open_left(s):
+            if s < PACK:
+                product_tile = tenant("left%d" % (s % AHEAD), S, F32)
+                product[s] = product_tile[:]
+            elif s == PACK:
+                both = tenant(old_slot[1], 2 * S, F32)
+                product[s], product[s + 1] = both[:, 0:S], both[:, S : 2 * S]
+            elif s > PACK + 1:
+                product_tile = tenant(old_slot[s - PACK], S, F32)
+                product[s] = product_tile[:]
             if s == 2:
-                product_tile = ring.tile([P, S], F32, name="product_tile", tag=slot, bufs=1, align_bytes=64)
-                spare[s] = product_tile[:]
-                slot = old_slot[3]
-            if s in (AHEAD, AHEAD + 1):
-                both = ring.tile([P, 2 * S], F32, name="both", tag=slot, bufs=1, align_bytes=64)
-                left[s], spare[s] = both[:, 0:S], both[:, S : 2 * S]
+                left[s] = tenant("rows3", S, F32)
+            elif s == 3:
+                left[s] = grouped[:, 0 : 2 * S].bitcast(F32)
             else:
-                left_tile = ring.tile([P, S], F32, name="left_tile", tag=slot, bufs=1, align_bytes=64)
-                left[s] = left_tile[:]
-            cols = slice(0, S)
-            if s == 0:
-                quarters = [slice(0, BANK // 2), slice(BANK // 2, BANK)]
-                for part in quarters:
-                    nc.vector.tensor_tensor(left[s][:, part], occs[s][:, part], conf[i][:, part], MULT)
-                for part in quarters:
-                    nc.vector.tensor_scalar(left[s][:, part], left[s][:, part], -1.0, 1.0, MULT, ADD)
-                cols = slice(BANK, S)
-            product = handover if s == 1 else spare.get(s, left[s])[:, cols]
-            views = [(handover if s == 0 else occs[s])[:, cols], conf[i][:, cols], left[s][:, cols]]
-            if s == 0:
-                product = quad[:, 0 : 2 * T2].bitcast(F32).rearrange("p (q c) -> p q c", q=4)[:, :, 0:P]
-                views = [view.rearrange("p (q c) -> p q c", q=4) for view in views]
-            nc.gpsimd.tensor_tensor(product, views[0], views[1], MULT)
-            nc.scalar.activation(views[2], product, COPY, bias=1.0, scale=-1.0)
+                left[s] = product[s]
 
-        def scatter(s):
-            page = page_of(s)
+        def product_of(s, cols):
             if s == 0:
-                for hf in range(2):
-                    nc.vector.tensor_copy(
-                        page[:].indirect(place[:, hf * HALF : (hf + 1) * HALF]), left[s][:, hf * BANK : (hf + 1) * BANK]
-                    )
-            else:
-                nc.vector.tensor_copy(page[:].indirect(place[:]), left[s])
+                return occ_of(cols.stop // BANK)[:, 0 : cols.stop - cols.start]
+            return product[s][:, cols]
 
-        planes = {}
+        def complement(s, cols):
+            nc.scalar.activation(left[s][:, cols], product_of(s, cols), COPY, bias=1.0, scale=-1.0)
 
-        def fade_old(s, eng, cols):
-            eng.tensor_tensor(planes[s][:, cols], old_tiles[s][:, cols], page_of(s)[:, cols], MULT)
+        def weigh(s, cols):
+            nc.gpsimd.tensor_tensor(product_of(s, cols), occ_of(s)[:, cols], conf[s % PACK][:, cols], MULT)
+            if s != 3:
+                complement(s, cols)
+
+        def scatter(s, cols):
+            nc.vector.tensor_copy(pages[s % PAGES][:].indirect(entries(place, cols)), left[s][:, cols])
+
+        def fade_old(s):
+            page = pages[s % PAGES][:].rearrange("p (c t) -> p c t", c=CHUNKS)
+            nc.gpsimd.tensor_tensor(plane_of(s), old_tiles[s], page, MULT)
+
+        def fade_last(c):
+            page = pages[last % PAGES]
+            nc.vector.tensor_tensor(plane_of(last)[:, c, :], old_last[c][:], page[:, chunk(c)], MULT)
 
         woven = {}
         z_codes = {}
         z_scales = [keep.tile([P, T2], U8, name="zs%d" % b, align_bytes=64) for b in range(PASSES)]
 
-        def weave(dst, source, t0, c, copy):
-            count = source.shape[1] // T2
-            dst = dst.rearrange("p (c i t) -> p c t i", i=4, t=PACK)[:, :, t0 : t0 + count, :]
-            src = source.rearrange("p (t c) -> p t c", t=count)[:, :, c * BANK : (c + 1) * BANK]
-            copy(dst, src.rearrange("p t (c i) -> p c t i", i=4))
+        def chunk(c):
+            return slice(c * BANK, (c + 1) * BANK)
 
-        def quantize_z(b, c0, count, source):
+        def woven_chunk(b, c):
+            return woven[b][:, c * BANK * PACK : (c + 1) * BANK * PACK]
+
+        def weave(b, c, copy, word):
+            copy(
+                woven_chunk(b, c).bitcast(word).rearrange("p (t h) -> p t h", h=2),
+                pair_words(b, word)[:, c, :, :].rearrange("p h t -> p t h"),
+            )
+
+        def quantize_z(b, c):
             nc.vector.quantize_mx(
-                out=z_codes[b][:, c0 * BANK : (c0 + count) * BANK].bitcast(FP8X4),
-                scales=z_scales[b][:, c0 * BANK : (c0 + count) * BANK],
-                in_=source,
+                out=z_codes[(b, c)].bitcast(FP8X4),
+                scales=z_scales[b][:, chunk(c)],
+                in_=woven_chunk(b, c),
             )
 
         sums = {}
+        staged = {}
 
-        def readout(g, b):
-            c, n = divmod(g, NT)
-            if b == 0:
-                sums[g] = psum.tile([P, BANK], F32, name="sums", tag="bank%d" % (g % 8))
-            nc.tensor.matmul_mx(
-                out=sums[g][:],
-                lhsT=w4_codes[:, b, 2 * n * P : 2 * (n + 1) * P].bitcast(FP4X4),
-                lhsT_scale=w4_plane[:, b, n * P : (n + 1) * P],
-                rhs=z_codes[b][:, c * BANK : (c + 1) * BANK].bitcast(FP8X4),
-                rhs_scale=z_scales[b][:, c * BANK : (c + 1) * BANK],
-                start=(b == 0),
-                stop=(b == PASSES - 1),
-            )
+        def readout(c, b):
+            for n in range(NT):
+                g = c * NT + n
+                if b == 0:
+                    sums[g] = psum.tile([P, BANK], F32, name="sums", tag="bank%d" % (g % 8))
+                nc.tensor.matmul_mx(
+                    out=sums[g][:],
+                    lhsT=w4_codes[:, b, 2 * n * P : 2 * (n + 1) * P].bitcast(FP4X4),
+                    lhsT_scale=w4_plane[:, b, n * P : (n + 1) * P],
+                    rhs=z_codes[(b, c)].bitcast(FP8X4),
+                    rhs_scale=z_scales[b][:, chunk(c)],
+                    start=(b == 0),
+                    stop=(b == PASSES - 1),
+                )
 
-        def store(g, copy):
-            c, n = divmod(g, NT)
-            staged = ring.tile([P, BANK], F32, name="staged", bufs=12)
-            copy(staged[:], sums[g][:])
-            nc.sync.dma_start(out=out[n * P : (n + 1) * P, c * BANK : (c + 1) * BANK], in_=staged[:])
+        def store(c, copies):
+            staged[c] = tenant(["rows1", "rows2", "rows4", "rows5"][c], NT * BANK, F32)
+            for n in range(NT):
+                copies[n](staged[c][:, chunk(n)], sums[c * NT + n][:])
+                nc.sync.dma_start(out=out[n * P : (n + 1) * P, chunk(c)], in_=staged[c][:, chunk(n)])
 
-        quad = ring.tile([P, PACK * T2], BF16, name="quad", tag="wide0", bufs=1, align_bytes=64)
-        pair_low = conf_pairs[1][:].bitcast(BF16)
-        for i in range(PACK):
-            planes[i] = quad[:, i * T2 : (i + 1) * T2]
-        for i in range(2):
-            planes[PACK + i] = pair_low[:, i * T2 : (i + 1) * T2]
-        for half in range(2):
-            woven[half] = ring.tile(
-                [P, 2 * BANK * PACK], BF16, name="woven", tag="woven%d" % half, bufs=1, align_bytes=64
-            )
-        woven_last = [keep.tile([P, BANK * PACK], BF16, name="woven_last%d" % c, align_bytes=64) for c in range(CHUNKS)]
-
-        logits(0)
-        logits(1)
-        weigh(0)
-        logits(2)
-        scatter(0)
-        logits(3)
-        weigh(1)
+        whole = slice(0, S)
+        first, second, third = pieces_of(0)
+        for cols in pieces_of(0):
+            logits(0, cols)
+        open_left(0)
+        for cols in (first, second):
+            nc.vector.tensor_tensor(left[0][:, cols], occ_of(0)[:, cols], conf[0][:, cols], MULT)
+        for cols in (first, second):
+            nc.vector.tensor_scalar(left[0][:, cols], left[0][:, cols], -1.0, 1.0, MULT, ADD)
+        scatter(0, slice(0, BANK))
+        for cols in pieces_of(1):
+            logits(1, cols)
+        weigh(0, third)
+        scatter(0, third)
+        for cols in pieces_of(2):
+            logits(2, cols)
+        open_left(1)
+        weigh(1, whole)
+        for cols in pieces_of(3):
+            logits(3, cols)
         cast_w1(1, 0, nc.scalar.copy)
-        load_old(2)
         cast_w1(1, 1, nc.scalar.copy)
-        weigh(2)
+        open_left(2)
+        weigh(2, whole)
         load_old(4)
         w4_codes = keep.tile([P, PASSES, 2 * N], U8, name="w4_codes", align_bytes=64)
         nc.sync.dma_start(out=w4_codes[:].bitcast(I32), in_=w4_words.rearrange("a p c -> p a c").bitcast(I32))
@@ -296,71 +327,66 @@ def tile_list_voxel_occupancy_map_kernel(
                 out=w4_plane[32 * q : 32 * q + 4, :, :].bitcast(I32),
                 in_=w4_scales[:, 4 * q : 4 * q + 4, :].rearrange("a r c -> r a c").bitcast(I32),
             )
-        load_old(PACK + 1)
-        load_old(SLICES - 1)
-        load_old(3)
         last = SLICES - 1
         for s in range(last):
             if s > 0:
-                scatter(s)
+                scatter(s, whole)
             if s == 1:
-                w1_codes[1] = ring.tile([P, PASSES * PASS], U32, name="w1c1", tag="left1", bufs=1, align_bytes=64)
                 quantize_w1(1, 0, PASSES)
-            if s == last - 2:
-                load_old(s + 1)
-            if s == last - 1:
-                pair_high = ring.tile([P, 2 * T2], BF16, name="pair_high", tag=old_slot[s - 1], bufs=1, align_bytes=64)
-                for i in range(2):
-                    planes[s + i] = pair_high[:, i * T2 : (i + 1) * T2]
-            fade_old(s, nc.gpsimd, slice(0, T2))
-            if 1 <= s and s + AHEAD < SLICES:
-                logits(s + AHEAD)
-            if s + AHEAD < SLICES:
-                weigh(s + AHEAD)
+                complement(3, whole)
+            if s == 2:
+                load_old(5)
+            fade_old(s)
+            if s == 1:
+                load_old_last()
+            for ahead in {0: [3], 1: [4], 2: [5], 3: [6, 7]}.get(s, []):
+                if ahead > AHEAD:
+                    for cols in pieces_of(ahead):
+                        logits(ahead, cols)
+                open_left(ahead)
+                weigh(ahead, whole)
             if s == PACK - 1:
+                load_old(6)
+            if s == PACK - 1:
+                woven[0] = keep.tile([P, PACK * T2], BF16, name="woven0", align_bytes=64)
                 for c in range(CHUNKS):
-                    lo = (c % 2) * BANK * PACK
-                    weave(woven[c // 2][:, lo : lo + BANK * PACK], quad[:], 0, c, nc.scalar.copy)
-            if s == PACK + 1:
-                for c in range(CHUNKS):
-                    weave(woven_last[c][:], pair_low, 0, c, nc.scalar.copy)
-        scatter(last)
+                    weave(0, c, nc.scalar.copy, U32)
 
-        z_codes[0] = ring.tile([P, T2], U32, name="zc0", tag=old_slot[last - AHEAD], bufs=1, align_bytes=64)
-        z_codes[1] = keep.tile([P, T2], U32, name="zc1", align_bytes=64)
-
-        def finish(c):
-            for g in range(c * NT, (c + 1) * NT):
-                readout(g, 1)
-            for g in range(c * NT, (c + 1) * NT):
-                store(g, nc.vector.tensor_copy if c == CHUNKS - 1 and g % 2 == 0 else nc.scalar.copy)
-
-        def chunk(c):
-            return slice(c * BANK, (c + 1) * BANK)
-
-        def weave_last(c, copy):
-            weave(woven_last[c][:], pair_high[:], 2, c, copy)
+        woven[1] = tenant("wide0", PACK * T2, BF16)
+        second_codes = tenant("conf0", T2, U32)
+        first_slot = [old_slot[2], "last0", "last2", "last3"]
+        on_scalar = nc.scalar.copy
+        on_vector = nc.vector.tensor_copy
 
         def first_pass(c):
-            lo = (c % 2) * BANK * PACK
-            quantize_z(0, c, 1, woven[c // 2][:, lo : lo + BANK * PACK])
-            for g in range(c * NT, (c + 1) * NT):
-                readout(g, 0)
+            first_codes = tenant(first_slot[c], BANK, U32)
+            z_codes[(0, c)] = first_codes[:]
+            quantize_z(0, c)
+            readout(c, 0)
 
         def second_pass(c):
-            quantize_z(1, c, 1, woven_last[c][:])
-            finish(c)
+            z_codes[(1, c)] = second_codes[:, chunk(c)]
+            quantize_z(1, c)
+            readout(c, 1)
 
-        fade_old(last, nc.vector, chunk(0))
         first_pass(0)
-        weave_last(0, nc.vector.tensor_copy)
-        fade_old(last, nc.vector, chunk(1))
-        weave_last(1, nc.scalar.copy)
+        scatter(last, whole)
+        fade_last(0)
+        fade_last(1)
+        weave(1, 0, on_vector, I32)
+        weave(1, 1, on_scalar, U32)
         second_pass(0)
+        store(0, [on_scalar] * NT)
         first_pass(1)
-        for c in range(2, CHUNKS):
-            fade_old(last, nc.vector, chunk(c))
-            second_pass(c - 1)
-            weave_last(c, nc.vector.tensor_copy)
-            first_pass(c)
-        second_pass(CHUNKS - 1)
+        second_pass(1)
+        store(1, [on_scalar] * NT)
+        fade_last(2)
+        fade_last(3)
+        weave(1, 2, on_vector, I32)
+        first_pass(2)
+        second_pass(2)
+        weave(1, 3, on_vector, I32)
+        first_pass(3)
+        second_pass(3)
+        store(2, [on_scalar] * NT)
+        store(3, [on_vector, on_scalar, on_vector])

@@ -111,12 +111,11 @@ def tile_list_voxel_occupancy_map_kernel(
 
         def load_old(s):
             if s == 6:
-                rows = pair_words(1, F32)[:, :, 1, :]
+                old_tiles[s] = old_sixth
             else:
-                rows_tile = tenant(old_slot[s], T2, F32)
-                rows = rows_tile[:].rearrange("p (c t) -> p c t", c=CHUNKS)
-            nc.sync.dma_start(out=rows, in_=old_rows[s // PACK, s % PACK].rearrange("p (c t) -> p c t", c=CHUNKS))
-            old_tiles[s] = rows
+                rows = tenant(old_slot[s], T2, F32)
+                old_tiles[s] = rows[:]
+            nc.sync.dma_start(out=old_tiles[s], in_=old_rows[s // PACK, s % PACK])
 
         old_last = {}
 
@@ -157,24 +156,18 @@ def tile_list_voxel_occupancy_map_kernel(
             cols = slice(hf * BANK, (hf + 1) * BANK)
             nc.vector.tensor_copy(picked[1][:, cols].bitcast(U32), table[1][:].bitcast(U32).indirect(entries(pick, cols)))
 
-        pairs = [tenant("wide%d" % b, PACK * T2, BF16) for b in range(PASSES)]
+        pairs = [tenant("wide%d" % b, (PACK + b) * T2, BF16) for b in range(PASSES)]
+        old_sixth = pairs[1][:, (PACK - 1) * T2 : (PACK + 1) * T2].bitcast(F32)
         spare_occ = [keep.tile([P, S], F32, name="spare_occ%d" % n, align_bytes=64) for n in range(2)]
 
-        pair_order = ["h c t", "c h t"]
-
-        def pair_words(b, word):
-            return pairs[b][:].bitcast(word).rearrange("p (%s) -> p c h t" % pair_order[b], c=CHUNKS, h=2)
-
         def plane_of(s):
-            b, i = divmod(s, PACK)
-            halves = pairs[b][:].rearrange("p (%s e) -> p c h t e" % pair_order[b], c=CHUNKS, h=2, e=2)
-            return halves[:, :, i // 2, :, i % 2]
+            return pairs[s // PACK][:, (s % PACK) * T2 : (s % PACK + 1) * T2]
 
         def occ_of(s):
-            if s in (2, 4):
-                return pairs[0][:].bitcast(F32)[:, (s // 2 - 1) * T2 : (s // 2 - 1) * T2 + S]
-            if s in (6, 7):
-                return pairs[1][:].bitcast(F32)[:, (s - 6) * S : (s - 5) * S]
+            if s in (2, 4, 6):
+                return plane_of(s - 2).bitcast(F32)
+            if s == 7:
+                return old_sixth[:, 0:S]
             return spare_occ[{0: 0, 1: 1, 3: 0, 5: 1}[s]][:]
 
         def pieces_of(s):
@@ -206,45 +199,51 @@ def tile_list_voxel_occupancy_map_kernel(
         left = {}
 
         def open_left(s):
-            if s < PACK:
-                product_tile = tenant("left%d" % (s % AHEAD), S, F32)
+            if s < AHEAD:
+                product_tile = tenant("left%d" % s, S, F32)
                 product[s] = product_tile[:]
+            elif s == AHEAD:
+                product[s] = grouped[:, 0 : 2 * S].bitcast(F32)
             elif s == PACK:
                 both = tenant(old_slot[1], 2 * S, F32)
                 product[s], product[s + 1] = both[:, 0:S], both[:, S : 2 * S]
             elif s > PACK + 1:
                 product_tile = tenant(old_slot[s - PACK], S, F32)
                 product[s] = product_tile[:]
-            if s == 2:
-                left[s] = tenant("rows3", S, F32)
-            elif s == 3:
-                left[s] = grouped[:, 0 : 2 * S].bitcast(F32)
-            else:
-                left[s] = product[s]
+            left[s] = product[s]
 
         def product_of(s, cols):
             if s == 0:
                 return occ_of(cols.stop // BANK)[:, 0 : cols.stop - cols.start]
             return product[s][:, cols]
 
+        after_cast = {}
+
+        def left_of(s, cols):
+            if s == 1 and cols.start > 0:
+                return after_cast[0][:, 0:QUARTER]
+            if s == 2:
+                return after_cast[0][:, QUARTER : QUARTER + S]
+            return left[s][:, cols]
+
         def complement(s, cols):
-            nc.scalar.activation(left[s][:, cols], product_of(s, cols), COPY, bias=1.0, scale=-1.0)
+            nc.scalar.activation(left_of(s, cols), product_of(s, cols), COPY, bias=1.0, scale=-1.0)
+
+        def multiply(s, cols):
+            nc.gpsimd.tensor_tensor(product_of(s, cols), occ_of(s)[:, cols], conf[s % PACK][:, cols], MULT)
 
         def weigh(s, cols):
-            nc.gpsimd.tensor_tensor(product_of(s, cols), occ_of(s)[:, cols], conf[s % PACK][:, cols], MULT)
-            if s != 3:
-                complement(s, cols)
+            multiply(s, cols)
+            complement(s, cols)
 
         def scatter(s, cols):
-            nc.vector.tensor_copy(pages[s % PAGES][:].indirect(entries(place, cols)), left[s][:, cols])
+            nc.vector.tensor_copy(pages[s % PAGES][:].indirect(entries(place, cols)), left_of(s, cols))
 
         def fade_old(s):
-            page = pages[s % PAGES][:].rearrange("p (c t) -> p c t", c=CHUNKS)
-            nc.gpsimd.tensor_tensor(plane_of(s), old_tiles[s], page, MULT)
+            nc.gpsimd.tensor_tensor(plane_of(s), old_tiles[s], pages[s % PAGES][:], MULT)
 
         def fade_last(c):
-            page = pages[last % PAGES]
-            nc.vector.tensor_tensor(plane_of(last)[:, c, :], old_last[c][:], page[:, chunk(c)], MULT)
+            nc.vector.tensor_tensor(plane_of(last)[:, chunk(c)], old_last[c][:], pages[last % PAGES][:, chunk(c)], MULT)
 
         woven = {}
         z_codes = {}
@@ -256,11 +255,10 @@ def tile_list_voxel_occupancy_map_kernel(
         def woven_chunk(b, c):
             return woven[b][:, c * BANK * PACK : (c + 1) * BANK * PACK]
 
-        def weave(b, c, copy, word):
-            copy(
-                woven_chunk(b, c).bitcast(word).rearrange("p (t h) -> p t h", h=2),
-                pair_words(b, word)[:, c, :, :].rearrange("p h t -> p t h"),
-            )
+        def weave(b, c, copy, first_plane, count):
+            dst = woven_chunk(b, c).rearrange("p (m i t) -> p m t i", i=4, t=PACK)
+            src = pairs[b][:].rearrange("p (t c) -> p t c", c=T2)[:, first_plane : first_plane + count, chunk(c)]
+            copy(dst[:, :, first_plane : first_plane + count, :], src.rearrange("p t (m i) -> p m t i", i=4))
 
         def quantize_z(b, c):
             nc.vector.quantize_mx(
@@ -288,7 +286,7 @@ def tile_list_voxel_occupancy_map_kernel(
                 )
 
         def store(c, copies):
-            staged[c] = tenant(["rows1", "rows2", "rows4", "rows5"][c], NT * BANK, F32)
+            staged[c] = tenant(["rows0", "rows2", "rows4", "rows5"][c], NT * BANK, F32)
             for n in range(NT):
                 copies[n](staged[c][:, chunk(n)], sums[c * NT + n][:])
                 nc.sync.dma_start(out=out[n * P : (n + 1) * P, chunk(c)], in_=staged[c][:, chunk(n)])
@@ -310,11 +308,15 @@ def tile_list_voxel_occupancy_map_kernel(
         for cols in pieces_of(2):
             logits(2, cols)
         open_left(1)
-        weigh(1, whole)
+        early, late = slice(0, S - QUARTER), slice(S - QUARTER, S)
+        multiply(1, whole)
+        complement(1, early)
         for cols in pieces_of(3):
             logits(3, cols)
         cast_w1(1, 0, nc.scalar.copy)
         cast_w1(1, 1, nc.scalar.copy)
+        after_cast[0] = tenant("rows3", QUARTER + S, F32)
+        complement(1, late)
         open_left(2)
         weigh(2, whole)
         load_old(4)
@@ -329,20 +331,22 @@ def tile_list_voxel_occupancy_map_kernel(
             )
         last = SLICES - 1
         for s in range(last):
-            if s > 0:
-                scatter(s, whole)
             if s == 1:
+                scatter(s, early)
                 quantize_w1(1, 0, PASSES)
-                complement(3, whole)
+                scatter(s, late)
+                open_left(AHEAD)
+                weigh(AHEAD, whole)
+            if s > 1:
+                scatter(s, whole)
             if s == 2:
                 load_old(5)
             fade_old(s)
             if s == 1:
                 load_old_last()
-            for ahead in {0: [3], 1: [4], 2: [5], 3: [6, 7]}.get(s, []):
-                if ahead > AHEAD:
-                    for cols in pieces_of(ahead):
-                        logits(ahead, cols)
+            for ahead in {1: [4], 2: [5], 3: [6, 7]}.get(s, []):
+                for cols in pieces_of(ahead):
+                    logits(ahead, cols)
                 open_left(ahead)
                 weigh(ahead, whole)
             if s == PACK - 1:
@@ -350,11 +354,14 @@ def tile_list_voxel_occupancy_map_kernel(
             if s == PACK - 1:
                 woven[0] = keep.tile([P, PACK * T2], BF16, name="woven0", align_bytes=64)
                 for c in range(CHUNKS):
-                    weave(0, c, nc.scalar.copy, U32)
+                    weave(0, c, nc.scalar.copy, 0, PACK)
+            if s == PACK + 1:
+                woven[1] = tenant("wide0", PACK * T2, BF16)
+                for c in range(CHUNKS):
+                    weave(1, c, nc.scalar.copy, 0, 2)
 
-        woven[1] = tenant("wide0", PACK * T2, BF16)
         second_codes = tenant("conf0", T2, U32)
-        first_slot = [old_slot[2], "last0", "last2", "last3"]
+        first_slot = [old_slot[3], "last1", "last2", "last3"]
         on_scalar = nc.scalar.copy
         on_vector = nc.vector.tensor_copy
 
@@ -369,24 +376,24 @@ def tile_list_voxel_occupancy_map_kernel(
             quantize_z(1, c)
             readout(c, 1)
 
-        first_pass(0)
         scatter(last, whole)
+        first_pass(0)
         fade_last(0)
         fade_last(1)
-        weave(1, 0, on_vector, I32)
-        weave(1, 1, on_scalar, U32)
+        weave(1, 1, on_scalar, 2, 2)
+        weave(1, 0, on_vector, 2, 2)
+        fade_last(2)
+        weave(1, 2, on_scalar, 2, 2)
         second_pass(0)
         store(0, [on_scalar] * NT)
         first_pass(1)
         second_pass(1)
         store(1, [on_scalar] * NT)
-        fade_last(2)
-        fade_last(3)
-        weave(1, 2, on_vector, I32)
         first_pass(2)
+        fade_last(3)
         second_pass(2)
-        weave(1, 3, on_vector, I32)
+        weave(1, 3, on_vector, 2, 2)
+        store(2, [on_scalar] * NT)
         first_pass(3)
         second_pass(3)
-        store(2, [on_scalar] * NT)
         store(3, [on_vector, on_scalar, on_vector])

@@ -49,7 +49,8 @@ def tile_list_voxel_occupancy_map_kernel(
         nc.sync.dma_start(pick[:], offs)
 
         scale_win = tenant("scale_win", T, U8)
-        nc.vector.memset(scale_win[:].bitcast(I32), 0)
+        nc.gpsimd.memset(scale_win[:, 0 : T // 2].bitcast(I32), 0)
+        nc.vector.memset(scale_win[:, T // 2 : T].bitcast(I32), 0)
         for a in range(PASSES):
             for q in range(4):
                 nc.scalar.dma_start(
@@ -57,7 +58,6 @@ def tile_list_voxel_occupancy_map_kernel(
                     in_=tab_scales[a, 4 * q : 4 * q + 4, :].bitcast(I32),
                 )
         bias = keep.tile([P, PASSES, PACK], F32, name="bias")
-        nc.scalar.dma_start(out=bias[:], in_=b1.rearrange("(b p i) -> p b i", b=PASSES, i=PACK))
 
         w1_raw = {}
 
@@ -90,12 +90,13 @@ def tile_list_voxel_occupancy_map_kernel(
         table = []
         for a in range(PASSES):
             if a == 1:
+                nc.sync.dma_start(place[:], offs2)
+                nc.sync.dma_start(out=bias[:], in_=b1.rearrange("(b p i) -> p b i", b=PASSES, i=PACK))
                 load_w1(0, 0)
                 load_w1(0, 1)
             words = tenant("wide%d" % a, T, I32)
             nc.sync.dma_start(out=words[:], in_=tab_words[a].rearrange("p t i -> p (t i)").bitcast(I32))
             table.append(words)
-        nc.sync.dma_start(place[:], offs2)
 
         conf_pairs = [tenant("conf%d" % n, 2 * S, F32) for n in range(2)]
         conf = [conf_pairs[i // 2][:, (i % 2) * S : (i % 2 + 1) * S] for i in range(PACK)]
@@ -255,9 +256,9 @@ def tile_list_voxel_occupancy_map_kernel(
         def woven_chunk(b, c):
             return woven[b][:, c * BANK * PACK : (c + 1) * BANK * PACK]
 
-        def weave(b, c, copy, first_plane, count):
-            dst = woven_chunk(b, c).rearrange("p (m i t) -> p m t i", i=4, t=PACK)
-            src = pairs[b][:].rearrange("p (t c) -> p t c", c=T2)[:, first_plane : first_plane + count, chunk(c)]
+        def weave(b, cols, copy, first_plane, count):
+            dst = woven[b][:, cols.start * PACK : cols.stop * PACK].rearrange("p (m i t) -> p m t i", i=4, t=PACK)
+            src = pairs[b][:].rearrange("p (t c) -> p t c", c=T2)[:, first_plane : first_plane + count, cols]
             copy(dst[:, :, first_plane : first_plane + count, :], src.rearrange("p t (m i) -> p m t i", i=4))
 
         def quantize_z(b, c):
@@ -354,11 +355,11 @@ def tile_list_voxel_occupancy_map_kernel(
             if s == PACK - 1:
                 woven[0] = keep.tile([P, PACK * T2], BF16, name="woven0", align_bytes=64)
                 for c in range(CHUNKS):
-                    weave(0, c, nc.scalar.copy, 0, PACK)
+                    weave(0, chunk(c), nc.scalar.copy, 0, PACK)
             if s == PACK + 1:
                 woven[1] = tenant("wide0", PACK * T2, BF16)
                 for c in range(CHUNKS):
-                    weave(1, c, nc.scalar.copy, 0, 2)
+                    weave(1, chunk(c), nc.scalar.copy, 0, 2)
 
         second_codes = tenant("conf0", T2, U32)
         first_slot = [old_slot[3], "last1", "last2", "last3"]
@@ -376,23 +377,27 @@ def tile_list_voxel_occupancy_map_kernel(
             quantize_z(1, c)
             readout(c, 1)
 
+        def half(c, h):
+            return slice(c * BANK + h * QUARTER, c * BANK + (h + 1) * QUARTER)
+
         scatter(last, whole)
         first_pass(0)
         fade_last(0)
         fade_last(1)
-        weave(1, 1, on_scalar, 2, 2)
-        weave(1, 0, on_vector, 2, 2)
+        weave(1, chunk(1), on_scalar, 2, 2)
+        weave(1, chunk(0), on_vector, 2, 2)
         fade_last(2)
-        weave(1, 2, on_scalar, 2, 2)
+        weave(1, half(2, 0), on_scalar, 2, 2)
         second_pass(0)
         store(0, [on_scalar] * NT)
         first_pass(1)
         second_pass(1)
         store(1, [on_scalar] * NT)
+        weave(1, half(2, 1), on_vector, 2, 2)
         first_pass(2)
         fade_last(3)
         second_pass(2)
-        weave(1, 3, on_vector, 2, 2)
+        weave(1, chunk(3), on_vector, 2, 2)
         store(2, [on_scalar] * NT)
         first_pass(3)
         second_pass(3)

@@ -49,14 +49,14 @@ def tile_list_voxel_occupancy_map_kernel(
         nc.sync.dma_start(pick[:], offs)
 
         scale_win = tenant("scale_win", T, U8)
-        nc.gpsimd.memset(scale_win[:, 0 : T // 2].bitcast(I32), 0)
-        nc.vector.memset(scale_win[:, T // 2 : T].bitcast(I32), 0)
-        for a in range(PASSES):
-            for q in range(4):
-                nc.scalar.dma_start(
-                    out=scale_win[32 * q + 4 * a : 32 * q + 4 * a + 4, :].bitcast(I32),
-                    in_=tab_scales[a, 4 * q : 4 * q + 4, :].bitcast(I32),
-                )
+        nc.sync.dma_start(
+            out=scale_win[0:32, :].bitcast(I32),
+            in_=tab_scales.rearrange("a m t -> m a t").bitcast(I32),
+        )
+        nc.gpsimd.memset(scale_win[32:64, :].bitcast(I32), 0)
+        nc.vector.memset(scale_win[64:P, :].bitcast(I32), 0)
+        table_plane = keep.tile([P, PASSES * S], U8, name="table_plane", align_bytes=64)
+        nc.gpsimd.memset(table_plane[:].bitcast(I32), 0)
         bias = keep.tile([P, PASSES, PACK], F32, name="bias")
 
         w1_raw = {}
@@ -146,8 +146,13 @@ def tile_list_voxel_occupancy_map_kernel(
 
         picked_scales = keep.tile([P, S], U8, name="picked_scales", align_bytes=64)
         picked = [keep.tile([P, S], I32, name="picked0", align_bytes=64)]
-        nc.vector.tensor_copy(picked[0][:].bitcast(U32), table[0][:].bitcast(U32).indirect(pick[:]))
         nc.vector.tensor_copy(picked_scales[:], scale_win[:].indirect(pick[:]))
+        for q in range(4):
+            nc.gpsimd.dma_start(
+                out=table_plane[32 * q : 32 * q + 4, :].bitcast(I32),
+                in_=picked_scales[8 * q : 8 * q + 8, :].bitcast(I32),
+            )
+        nc.vector.tensor_copy(picked[0][:].bitcast(U32), table[0][:].bitcast(U32).indirect(pick[:]))
         picked.append(tenant("scale_win", S, I32))
 
         def entries(offsets, cols):
@@ -190,7 +195,7 @@ def tile_list_voxel_occupancy_map_kernel(
                     lhsT=w1_codes[b][:, wcols].bitcast(FP8X4),
                     lhsT_scale=w1_scales[b][:, wcols],
                     rhs=picked[a][:, cols].bitcast(FP8X4),
-                    rhs_scale=picked_scales[4 * a : P, cols],
+                    rhs_scale=table_plane[:, a * S + cols.start : a * S + cols.stop],
                     start=(a == 0),
                     stop=(a == PASSES - 1),
                 )

@@ -1,6 +1,7 @@
 from contextlib import ExitStack
 
 import concourse.mybir as mybir
+from concourse.masks import make_identity
 
 K, H, N, T, S, T2 = 1024, 1024, 384, 4096, 1024, 2048
 FLOPS = 2 * K * H * S + 2 * H * N * T2
@@ -30,6 +31,7 @@ PAGES = 3
 AHEAD = 3
 STRIPE = 16
 QUARTER = BANK // 2
+BLOCKS = T2 // P
 
 
 def tile_list_voxel_occupancy_map_kernel(
@@ -48,67 +50,54 @@ def tile_list_voxel_occupancy_map_kernel(
         place = keep.tile([P, S // STRIPE], U16, name="place")
         nc.sync.dma_start(pick[:], offs)
 
-        scale_win = tenant("scale_win", T, U8)
+        scale_win = keep.tile([P, T], U8, name="scale_win", align_bytes=64)
         nc.sync.dma_start(
             out=scale_win[0:32, :].bitcast(I32),
             in_=tab_scales.rearrange("a m t -> m a t").bitcast(I32),
         )
-        nc.gpsimd.memset(scale_win[32:64, :].bitcast(I32), 0)
+        nc.vector.memset(scale_win[32:64, :].bitcast(I32), 0)
         nc.vector.memset(scale_win[64:P, :].bitcast(I32), 0)
         table_plane = keep.tile([P, PASSES * S], U8, name="table_plane", align_bytes=64)
         nc.gpsimd.memset(table_plane[:].bitcast(I32), 0)
-        bias = keep.tile([P, PASSES, PACK], F32, name="bias")
-
-        w1_raw = {}
-
-        def load_w1(b, a):
-            raw = tenant("rows%d" % (2 * b + a), PACK * PASS, F32)
-            nc.sync.dma_start(
-                out=raw[:].rearrange("p (j c) -> p j c", j=PACK),
-                in_=w1[a * PASS : (a + 1) * PASS, b * PASS : (b + 1) * PASS].rearrange("(p j) c -> p j c", j=PACK),
-            )
-            w1_raw[(a, b)] = raw
-
-        w1_codes = [keep.tile([P, PASSES * PASS], U32, name="w1c%d" % b, align_bytes=64) for b in range(PASSES)]
-        w1_scales = [keep.tile([P, PASSES * PASS], U8, name="w1s%d" % b, align_bytes=64) for b in range(PASSES)]
-        grouped = keep.tile([P, PASSES * PASS * PACK], BF16, name="grouped", align_bytes=64)
-        width = PASS * PACK
-
-        def cast_w1(b, a, copy):
-            copy(
-                grouped[:, a * width : (a + 1) * width].rearrange("p (t m j) -> p m j t", t=PACK, j=PACK),
-                w1_raw[(a, b)][:].rearrange("p (j m t) -> p m j t", j=PACK, t=PACK),
-            )
-
-        def quantize_w1(b, a0, count):
-            nc.vector.quantize_mx(
-                out=w1_codes[b][:, a0 * PASS : (a0 + count) * PASS].bitcast(FP8X4),
-                scales=w1_scales[b][:, a0 * PASS : (a0 + count) * PASS],
-                in_=grouped[:, a0 * width : (a0 + count) * width],
-            )
+        ident_pairs = keep.tile([P, P], F32, name="ident_pairs")
+        ident = keep.tile([P, P], BF16, name="ident")
+        make_identity(nc, ident_pairs[:])
+        make_identity(nc, ident[:])
 
         table = []
-        for a in range(PASSES):
-            if a == 1:
-                nc.sync.dma_start(place[:], offs2)
-                nc.sync.dma_start(out=bias[:], in_=b1.rearrange("(b p i) -> p b i", b=PASSES, i=PACK))
-                load_w1(0, 0)
-                load_w1(0, 1)
+
+        def load_table(a):
             words = tenant("wide%d" % a, T, I32)
             nc.sync.dma_start(out=words[:], in_=tab_words[a].rearrange("p t i -> p (t i)").bitcast(I32))
             table.append(words)
 
-        conf_pairs = [tenant("conf%d" % n, 2 * S, F32) for n in range(2)]
-        conf = [conf_pairs[i // 2][:, (i % 2) * S : (i % 2 + 1) * S] for i in range(PACK)]
-        conf_rows = wgs.rearrange("(m i) j -> i m j", i=PACK)
+        def load_w1(raw, a, first, count):
+            nc.sync.dma_start(
+                out=raw.rearrange("p (j c) -> p j c", j=PACK),
+                in_=w1[a * PASS : (a + 1) * PASS, first : first + count].rearrange("(p j) c -> p j c", j=PACK),
+            )
 
-        def load_conf(i):
-            for q in (0, 2, 1, 3):
-                nc.sync.dma_start(out=conf_pairs[i // 2][32 * q : 32 * q + 32, (i % 2) * S : (i % 2 + 1) * S], in_=conf_rows[i])
+        bias = [keep.tile([P, PACK], F32, name="bias%d" % b) for b in range(PASSES)]
+        load_table(0)
+        nc.sync.dma_start(place[:], offs2)
+        with nc.allow_non_contiguous_dma(reason="one bias value a partition"):
+            nc.sync.dma_start(out=bias[0][:], in_=b1[0:PASS].rearrange("(q p) -> p q", p=P))
+        nc.sync.dma_start(out=bias[1][:], in_=b1[PASS : 2 * PASS].rearrange("(p i) -> p i", i=PACK))
+        raw_head = [tenant("page%d" % (1 + a), PACK * 2 * P, F32) for a in range(PASSES)]
+        for a in range(PASSES):
+            load_w1(raw_head[a][:], a, 0, 2 * P)
+        load_table(1)
+        conf_plain = keep.tile([P, S], F32, name="conf_plain")
+        nc.sync.dma_start(out=conf_plain[:], in_=wgs)
+        raw_next = tenant("rows3", 2 * PASSES * PASS, F32)
+        for q in (2, 3):
+            for a in range(PASSES):
+                first = ((q - 2) * PASSES + a) * PASS
+                load_w1(raw_next[:, first : first + PASS], a, q * P, P)
 
         old_rows = old.rearrange("(b p i) t -> b i p t", b=PASSES, i=PACK)
         old_tiles = {}
-        old_slot = ["rows4", "rows5", "rows0", "rows1", "rows2", "rows3"]
+        old_slot = ["rows0", "rows1", "rows2", "rows3", "rows4", "rows5"]
 
         def load_old(s):
             if s == 6:
@@ -116,36 +105,44 @@ def tile_list_voxel_occupancy_map_kernel(
             else:
                 rows = tenant(old_slot[s], T2, F32)
                 old_tiles[s] = rows[:]
-            nc.sync.dma_start(out=old_tiles[s], in_=old_rows[s // PACK, s % PACK])
+            source = old[s * P : (s + 1) * P, :] if s < PACK else old_rows[1, s - PACK]
+            nc.sync.dma_start(out=old_tiles[s], in_=source)
+
+        raw_late = [tenant("rows%d" % (4 + a), PACK * PASS, F32) for a in range(PASSES)]
+        load_w1(raw_late[0][:], 0, PASS, PASS)
+        load_old(0)
+        load_w1(raw_late[1][:], 1, PASS, PASS)
+        load_old(1)
+        conf_pairs = [tenant("conf%d" % n, 2 * S, F32) for n in range(2)]
+        conf_rows = wgs.rearrange("(m n i) j -> n m (i j)", n=2, i=2)
+        for n in range(2):
+            for q in (0, 2, 1, 3):
+                nc.sync.dma_start(out=conf_pairs[n][32 * q : 32 * q + 32, :], in_=conf_rows[n])
+        load_old(2)
+
+        def conf_of(s):
+            if s < PACK:
+                return conf_plain[:]
+            i = s - PACK
+            return conf_pairs[i // 2][:, (i % 2) * S : (i % 2 + 1) * S]
 
         old_last = {}
+        for c in range(CHUNKS):
+            old_last[c] = tenant("last%d" % c, BANK, F32)
+            nc.sync.dma_start(out=old_last[c][:], in_=old_rows[PASSES - 1, PACK - 1][:, c * BANK : (c + 1) * BANK])
+        w4_codes = keep.tile([P, PASSES, 2 * N], U8, name="w4_codes", align_bytes=64)
+        nc.sync.dma_start(out=w4_codes[:].bitcast(I32), in_=w4_words.rearrange("a p c -> p a c").bitcast(I32))
 
-        def load_old_last():
-            for c in range(CHUNKS):
-                old_last[c] = tenant("last%d" % c, BANK, F32)
-                nc.sync.dma_start(out=old_last[c][:], in_=old_rows[PASSES - 1, PACK - 1][:, c * BANK : (c + 1) * BANK])
+        pages = {}
 
-        load_conf(0)
-        load_conf(1)
-        load_conf(2)
-        load_old(0)
-        load_w1(1, 0)
-        load_w1(1, 1)
-        load_conf(3)
-        load_old(1)
-        pages = [keep.tile([P, T2], F32, name="page%d" % n) for n in range(PAGES)]
-        for page in pages:
-            nc.vector.memset(page[:], 1.0)
+        def open_page(n):
+            pages[n] = tenant("page%d" % n, T2, F32)
+            nc.vector.memset(pages[n][:], 1.0)
 
-        cast_w1(0, 0, nc.scalar.copy)
-        cast_w1(0, 1, nc.vector.tensor_copy)
-        for a in range(PASSES):
-            quantize_w1(0, a, 1)
-        load_old(2)
-        load_old(3)
+        open_page(0)
 
         picked_scales = keep.tile([P, S], U8, name="picked_scales", align_bytes=64)
-        picked = [keep.tile([P, S], I32, name="picked0", align_bytes=64)]
+        picked = [keep.tile([P, S], I32, name="picked%d" % a, align_bytes=64) for a in range(PASSES)]
         nc.vector.tensor_copy(picked_scales[:], scale_win[:].indirect(pick[:]))
         for q in range(4):
             nc.gpsimd.dma_start(
@@ -153,7 +150,31 @@ def tile_list_voxel_occupancy_map_kernel(
                 in_=picked_scales[8 * q : 8 * q + 8, :].bitcast(I32),
             )
         nc.vector.tensor_copy(picked[0][:].bitcast(U32), table[0][:].bitcast(U32).indirect(pick[:]))
-        picked.append(tenant("scale_win", S, I32))
+
+        plain = {s: keep.tile([P, T2], BF16, name="plain%d" % s, align_bytes=64) for s in (0, 2, 3)}
+        grouped = keep.tile([P, 10 * PASS], BF16, name="grouped", align_bytes=64)
+        head_codes = keep.tile([P, 4 * P], U32, name="head_codes", align_bytes=64)
+        head_scales = keep.tile([P, 4 * P], U8, name="head_scales", align_bytes=64)
+        next_codes = keep.tile([P, 2 * P], U32, name="next_codes", align_bytes=64)
+        next_scales = keep.tile([P, 2 * P], U8, name="next_scales", align_bytes=64)
+        late_scales = keep.tile([P, 10 * P], U8, name="late_scales", align_bytes=64)
+
+        def interleave(copy, dst, src, groups):
+            copy(
+                dst.rearrange("p (a m i j) -> p a m j i", a=groups, i=4, j=PACK),
+                src.rearrange("p (a j m i) -> p a m j i", a=groups, i=4, j=PACK),
+            )
+
+        def quantize(codes, scales, values):
+            nc.vector.quantize_mx(out=codes.bitcast(FP8X4), scales=scales, in_=values)
+
+        wide = 2 * PASS
+        interleave(nc.scalar.copy, plain[0][:, 0:wide], raw_head[0][:], 1)
+        quantize(head_codes[:, 0 : 2 * P], head_scales[:, 0 : 2 * P], plain[0][:, 0:wide])
+        interleave(nc.vector.tensor_copy, plain[0][:, wide : 2 * wide], raw_head[1][:], 1)
+        quantize(head_codes[:, 2 * P : 4 * P], head_scales[:, 2 * P : 4 * P], plain[0][:, wide : 2 * wide])
+        open_page(1)
+        open_page(2)
 
         def entries(offsets, cols):
             return offsets[:, cols.start // STRIPE : cols.stop // STRIPE]
@@ -162,94 +183,101 @@ def tile_list_voxel_occupancy_map_kernel(
             cols = slice(hf * BANK, (hf + 1) * BANK)
             nc.vector.tensor_copy(picked[1][:, cols].bitcast(U32), table[1][:].bitcast(U32).indirect(entries(pick, cols)))
 
-        pairs = [tenant("wide%d" % b, (PACK + b) * T2, BF16) for b in range(PASSES)]
-        old_sixth = pairs[1][:, (PACK - 1) * T2 : (PACK + 1) * T2].bitcast(F32)
-        spare_occ = [keep.tile([P, S], F32, name="spare_occ%d" % n, align_bytes=64) for n in range(2)]
+        late_planes = tenant("wide1", (PACK + 1) * T2, BF16)
+        old_sixth = late_planes[:, (PACK - 1) * T2 : (PACK + 1) * T2].bitcast(F32)
 
         def plane_of(s):
-            return pairs[s // PACK][:, (s % PACK) * T2 : (s % PACK + 1) * T2]
+            if s == 1:
+                return raw_late[1][:, S : 2 * S].bitcast(BF16)
+            if s < PACK:
+                return plain[s][:]
+            return late_planes[:, (s - PACK) * T2 : (s - PACK + 1) * T2]
 
-        def occ_of(s):
-            if s in (2, 4, 6):
-                return plane_of(s - 2).bitcast(F32)
-            if s == 7:
-                return old_sixth[:, 0:S]
-            return spare_occ[{0: 0, 1: 1, 3: 0, 5: 1}[s]][:]
+        scratch = grouped[:].bitcast(F32)
+        occ_one = keep.tile([P, S], F32, name="occ_one", align_bytes=64)
 
-        def pieces_of(s):
+        def occ_of(s, cols):
             if s == 0:
-                return [slice(0, QUARTER), slice(QUARTER, BANK), slice(BANK, S)]
-            return [slice(0, BANK), slice(BANK, S)]
+                return scratch[:, BANK + cols.start : BANK + cols.stop]
+            if s == 1:
+                return occ_one[:, cols]
+            if s == 2 and cols.start == 0:
+                return scratch[:, 5 * QUARTER : 7 * QUARTER]
+            if s == 7:
+                return late_planes[:, 3 * T2 // 2 : 5 * T2 // 2].bitcast(F32)[:, cols]
+            return plane_of(s - 2).bitcast(F32)[:, cols]
+
+        late_codes = keep.tile([P, 10 * P], U32, name="late_codes", align_bytes=64)
+
+        def weights_of(s, a):
+            if s < 2:
+                at = a * 2 * P + s * P
+                return head_codes[:, at : at + P], head_scales[:, at : at + P]
+            if s == 2:
+                return next_codes[:, a * P : (a + 1) * P], next_scales[:, a * P : (a + 1) * P]
+            at = a * P if s == 3 else 2 * P + a * PASS + (s - PACK) * P
+            return late_codes[:, at : at + P], late_scales[:, at : at + P]
 
         banks_used = [0]
 
         def logits(s, cols):
-            b, i = divmod(s, PACK)
             acc = psum.tile([P, BANK], F32, name="acc", tag="bank%d" % (4 + banks_used[0] % 4))
             banks_used[0] = banks_used[0] + 1
             count = cols.stop - cols.start
             for a in range(PASSES):
-                wcols = slice(a * PASS + i * P, a * PASS + (i + 1) * P)
+                codes, scales = weights_of(s, a)
                 nc.tensor.matmul_mx(
                     out=acc[:, 0:count],
-                    lhsT=w1_codes[b][:, wcols].bitcast(FP8X4),
-                    lhsT_scale=w1_scales[b][:, wcols],
+                    lhsT=codes.bitcast(FP8X4),
+                    lhsT_scale=scales,
                     rhs=picked[a][:, cols].bitcast(FP8X4),
                     rhs_scale=table_plane[:, a * S + cols.start : a * S + cols.stop],
                     start=(a == 0),
                     stop=(a == PASSES - 1),
                 )
-            nc.scalar.activation(occ_of(s)[:, cols], acc[:, 0:count], SIGMOID, bias=bias[:, b, i : i + 1])
+            nc.scalar.activation(occ_of(s, cols), acc[:, 0:count], SIGMOID, bias=bias[s // PACK][:, s % PACK : s % PACK + 1])
 
-        product = {}
-        left = {}
+        low, high, whole = slice(0, BANK), slice(BANK, S), slice(0, S)
 
-        def open_left(s):
-            if s < AHEAD:
-                product_tile = tenant("left%d" % s, S, F32)
-                product[s] = product_tile[:]
-            elif s == AHEAD:
-                product[s] = grouped[:, 0 : 2 * S].bitcast(F32)
-            elif s == PACK:
-                both = tenant(old_slot[1], 2 * S, F32)
-                product[s], product[s + 1] = both[:, 0:S], both[:, S : 2 * S]
-            elif s > PACK + 1:
-                product_tile = tenant(old_slot[s - PACK], S, F32)
-                product[s] = product_tile[:]
-            left[s] = product[s]
+        def both_logits(s):
+            logits(s, low)
+            logits(s, high)
 
-        def product_of(s, cols):
-            if s == 0:
-                return occ_of(cols.stop // BANK)[:, 0 : cols.stop - cols.start]
-            return product[s][:, cols]
+        def multiply(s, cols, product):
+            nc.gpsimd.tensor_tensor(product, occ_of(s, cols), conf_of(s)[:, cols], MULT)
 
-        after_cast = {}
+        def complement(left, product):
+            nc.scalar.activation(left, product, COPY, bias=1.0, scale=-1.0)
 
-        def left_of(s, cols):
-            if s == 1 and cols.start > 0:
-                return after_cast[0][:, 0:QUARTER]
-            if s == 2:
-                return after_cast[0][:, QUARTER : QUARTER + S]
-            return left[s][:, cols]
-
-        def complement(s, cols):
-            nc.scalar.activation(left_of(s, cols), product_of(s, cols), COPY, bias=1.0, scale=-1.0)
-
-        def multiply(s, cols):
-            nc.gpsimd.tensor_tensor(product_of(s, cols), occ_of(s)[:, cols], conf[s % PACK][:, cols], MULT)
-
-        def weigh(s, cols):
-            multiply(s, cols)
-            complement(s, cols)
-
-        def scatter(s, cols):
-            nc.vector.tensor_copy(pages[s % PAGES][:].indirect(entries(place, cols)), left_of(s, cols))
+        def scatter(s, cols, left):
+            nc.vector.tensor_copy(pages[s % PAGES][:].indirect(entries(place, cols)), left)
 
         def fade_old(s):
             nc.gpsimd.tensor_tensor(plane_of(s), old_tiles[s], pages[s % PAGES][:], MULT)
 
         def fade_last(c):
             nc.vector.tensor_tensor(plane_of(last)[:, chunk(c)], old_last[c][:], pages[last % PAGES][:, chunk(c)], MULT)
+
+        turned = {}
+
+        def turn(q):
+            for g in range(2):
+                bank = psum.tile([P, 8 * P], BF16, name="turn", tag="bank%d" % g)
+                for k in range(8):
+                    at = (8 * g + k) * P
+                    nc.tensor.transpose(bank[:, k * P : (k + 1) * P], plane_of(q)[:, at : at + P], ident[:])
+                dst = turned[0][:].rearrange("p (k r) -> p k r", r=PASS)[:, 8 * g : 8 * g + 8, q * P : (q + 1) * P]
+                nc.scalar.copy(dst, bank[:].rearrange("p (k r) -> p k r", r=P))
+
+        def turn_back(g):
+            bank = psum.tile([P, BANK], F32, name="back", tag="bank%d" % (g % 4))
+            for k in range(2):
+                at = (2 * g + k) * PASS
+                words = turned[0][:, at : at + PASS].bitcast(F32)
+                for u in range(2):
+                    nc.tensor.transpose(bank[:, (2 * k + u) * P : (2 * k + u + 1) * P], words[:, u : 2 * P : 2], ident_pairs[:])
+            dst = woven[0][:, 2 * g * PASS : (2 * g + 2) * PASS].bitcast(F32).rearrange("p (k t u) -> p k t u", k=2, u=2)
+            nc.scalar.copy(dst, bank[:].rearrange("p (k u t) -> p k t u", k=2, u=2))
 
         woven = {}
         z_codes = {}
@@ -258,20 +286,13 @@ def tile_list_voxel_occupancy_map_kernel(
         def chunk(c):
             return slice(c * BANK, (c + 1) * BANK)
 
-        def woven_chunk(b, c):
-            return woven[b][:, c * BANK * PACK : (c + 1) * BANK * PACK]
-
-        def weave(b, cols, copy, first_plane, count):
-            dst = woven[b][:, cols.start * PACK : cols.stop * PACK].rearrange("p (m i t) -> p m t i", i=4, t=PACK)
-            src = pairs[b][:].rearrange("p (t c) -> p t c", c=T2)[:, first_plane : first_plane + count, cols]
-            copy(dst[:, :, first_plane : first_plane + count, :], src.rearrange("p t (m i) -> p m t i", i=4))
+        def weave(cols, copy, first_plane):
+            dst = woven[1][:, cols.start * PACK : cols.stop * PACK].rearrange("p (m i t) -> p m t i", i=4, t=PACK)
+            src = late_planes[:].rearrange("p (t c) -> p t c", c=T2)[:, first_plane : first_plane + 2, cols]
+            copy(dst[:, :, first_plane : first_plane + 2, :], src.rearrange("p t (m i) -> p m t i", i=4))
 
         def quantize_z(b, c):
-            nc.vector.quantize_mx(
-                out=z_codes[(b, c)].bitcast(FP8X4),
-                scales=z_scales[b][:, chunk(c)],
-                in_=woven_chunk(b, c),
-            )
+            quantize(z_codes[(b, c)], z_scales[b][:, chunk(c)], woven[b][:, c * BANK * PACK : (c + 1) * BANK * PACK])
 
         sums = {}
         staged = {}
@@ -292,42 +313,60 @@ def tile_list_voxel_occupancy_map_kernel(
                 )
 
         def store(c, copies):
-            staged[c] = tenant(["rows0", "rows2", "rows4", "rows5"][c], NT * BANK, F32)
+            staged[c] = tenant(old_slot[c], NT * BANK, F32)
             for n in range(NT):
                 copies[n](staged[c][:, chunk(n)], sums[c * NT + n][:])
                 nc.sync.dma_start(out=out[n * P : (n + 1) * P, chunk(c)], in_=staged[c][:, chunk(n)])
 
-        whole = slice(0, S)
-        first, second, third = pieces_of(0)
-        for cols in pieces_of(0):
+        first, second = slice(0, QUARTER), slice(QUARTER, BANK)
+        for cols in (first, second, high):
             logits(0, cols)
-        open_left(0)
+        left_first = keep.tile([P, BANK], F32, name="left_first")
+        shared = scratch[:, 0:BANK]
         for cols in (first, second):
-            nc.vector.tensor_tensor(left[0][:, cols], occ_of(0)[:, cols], conf[0][:, cols], MULT)
+            nc.vector.tensor_tensor(shared[:, cols], occ_of(0, cols), conf_plain[:, cols], MULT)
         for cols in (first, second):
-            nc.vector.tensor_scalar(left[0][:, cols], left[0][:, cols], -1.0, 1.0, MULT, ADD)
-        scatter(0, slice(0, BANK))
-        for cols in pieces_of(1):
-            logits(1, cols)
-        weigh(0, third)
-        scatter(0, third)
-        for cols in pieces_of(2):
-            logits(2, cols)
-        open_left(1)
-        early, late = slice(0, S - QUARTER), slice(S - QUARTER, S)
-        multiply(1, whole)
-        complement(1, early)
-        for cols in pieces_of(3):
-            logits(3, cols)
-        cast_w1(1, 0, nc.scalar.copy)
-        cast_w1(1, 1, nc.scalar.copy)
-        after_cast[0] = tenant("rows3", QUARTER + S, F32)
-        complement(1, late)
-        open_left(2)
-        weigh(2, whole)
+            nc.vector.tensor_scalar(left_first[:, cols], shared[:, cols], -1.0, 1.0, MULT, ADD)
+        scatter(0, low, left_first[:])
+        both_logits(1)
+        product_zero = scratch[:, BANK:S]
+        multiply(0, high, product_zero)
+        left_one = raw_next[:, BANK : BANK + S]
+        product_one = [scratch[:, 6 * QUARTER : 8 * QUARTER], occ_of(2, high)]
+        for hf, cols in enumerate((low, high)):
+            multiply(1, cols, product_one[hf])
+        interleave(nc.scalar.copy, grouped[:, 0:wide], raw_next[:, 0:wide], PASSES)
+        quantize(next_codes[:], next_scales[:], grouped[:, 0:wide])
+        complement(raw_next[:, 0:BANK], product_zero)
+        scatter(0, high, raw_next[:, 0:BANK])
+        complement(left_one[:, low], product_one[0])
+        nc.gpsimd.tensor_scalar(
+            grouped[:, 0:wide].rearrange("p (a c j) -> p a c j", a=PASSES, j=PACK),
+            raw_next[:, wide : 2 * wide].rearrange("p (a j c) -> p a c j", a=PASSES, j=PACK),
+            1.0,
+            0.0,
+            MULT,
+            ADD,
+        )
+        complement(left_one[:, high], product_one[1])
+        both_logits(2)
+        quantize(late_codes[:, 0 : 2 * P], late_scales[:, 0 : 2 * P], grouped[:, 0:wide])
+        scatter(1, whole, left_one)
+        turned[0] = tenant("wide0", BLOCKS * PASS, BF16)
+        product_two = [turned[0][:, 7 * PASS : 9 * PASS].bitcast(F32), shared]
+        for hf, cols in enumerate((low, high)):
+            multiply(2, cols, product_two[hf])
+        for a in range(PASSES):
+            nc.scalar.copy(
+                grouped[:, (2 + 4 * a) * PASS : (6 + 4 * a) * PASS].rearrange("p (t m j) -> p m j t", t=PACK, j=PACK),
+                raw_late[a][:].rearrange("p (j m t) -> p m j t", j=PACK, t=PACK),
+            )
+        left = {2: raw_late[1][:, 0:S]}
+        both_logits(3)
+        for hf, cols in ((1, high), (0, low)):
+            complement(left[2][:, cols], product_two[hf])
+        load_old(3)
         load_old(4)
-        w4_codes = keep.tile([P, PASSES, 2 * N], U8, name="w4_codes", align_bytes=64)
-        nc.sync.dma_start(out=w4_codes[:].bitcast(I32), in_=w4_words.rearrange("a p c -> p a c").bitcast(I32))
         w4_plane = keep.tile([P, PASSES, N], U8, name="w4_plane", align_bytes=64)
         nc.vector.memset(w4_plane[:].bitcast(I32), 0)
         for q in range(4):
@@ -335,39 +374,45 @@ def tile_list_voxel_occupancy_map_kernel(
                 out=w4_plane[32 * q : 32 * q + 4, :, :].bitcast(I32),
                 in_=w4_scales[:, 4 * q : 4 * q + 4, :].rearrange("a r c -> r a c").bitcast(I32),
             )
+        fade_old(0)
+        turn(0)
+        quantize(late_codes[:, 2 * P : 10 * P], late_scales[:, 2 * P : 10 * P], grouped[:, 2 * PASS : 10 * PASS])
+
+        def weigh(s):
+            if s == AHEAD:
+                left[s] = scratch[:, BANK : BANK + S]
+            else:
+                product = tenant(old_slot[s - AHEAD], S, F32)
+                left[s] = product[:]
+            multiply(s, whole, left[s])
+            complement(left[s], left[s])
+            if s < last:
+                both_logits(s + 1)
+
         last = SLICES - 1
-        for s in range(last):
-            if s == 1:
-                scatter(s, early)
-                quantize_w1(1, 0, PASSES)
-                scatter(s, late)
-                open_left(AHEAD)
-                weigh(AHEAD, whole)
+        for s in range(1, last):
             if s > 1:
-                scatter(s, whole)
+                scatter(s, whole, left[s])
+            if s + 2 <= last:
+                weigh(s + 2)
+            if s == PACK + 1:
+                load_old(6)
+            fade_old(s)
+            if s < PACK:
+                turn(s)
             if s == 2:
                 load_old(5)
-            fade_old(s)
-            if s == 1:
-                load_old_last()
-            for ahead in {1: [4], 2: [5], 3: [6, 7]}.get(s, []):
-                for cols in pieces_of(ahead):
-                    logits(ahead, cols)
-                open_left(ahead)
-                weigh(ahead, whole)
-            if s == PACK - 1:
-                load_old(6)
             if s == PACK - 1:
                 woven[0] = keep.tile([P, PACK * T2], BF16, name="woven0", align_bytes=64)
-                for c in range(CHUNKS):
-                    weave(0, chunk(c), nc.scalar.copy, 0, PACK)
+                for g in range(BLOCKS // 2):
+                    turn_back(g)
             if s == PACK + 1:
                 woven[1] = tenant("wide0", PACK * T2, BF16)
                 for c in range(CHUNKS):
-                    weave(1, chunk(c), nc.scalar.copy, 0, 2)
+                    weave(chunk(c), nc.scalar.copy, 0)
 
         second_codes = tenant("conf0", T2, U32)
-        first_slot = [old_slot[3], "last1", "last2", "last3"]
+        first_slot = [old_slot[4], "last1", "last2", "last3"]
         on_scalar = nc.scalar.copy
         on_vector = nc.vector.tensor_copy
 
@@ -385,24 +430,24 @@ def tile_list_voxel_occupancy_map_kernel(
         def half(c, h):
             return slice(c * BANK + h * QUARTER, c * BANK + (h + 1) * QUARTER)
 
-        scatter(last, whole)
+        scatter(last, whole, left[last])
         first_pass(0)
         fade_last(0)
         fade_last(1)
-        weave(1, chunk(1), on_scalar, 2, 2)
-        weave(1, chunk(0), on_vector, 2, 2)
+        weave(chunk(1), on_scalar, 2)
+        weave(chunk(0), on_vector, 2)
         fade_last(2)
-        weave(1, half(2, 0), on_scalar, 2, 2)
+        weave(half(2, 0), on_scalar, 2)
         second_pass(0)
         store(0, [on_scalar] * NT)
         first_pass(1)
         second_pass(1)
         store(1, [on_scalar] * NT)
-        weave(1, half(2, 1), on_vector, 2, 2)
+        weave(half(2, 1), on_vector, 2)
         first_pass(2)
         fade_last(3)
         second_pass(2)
-        weave(1, chunk(3), on_vector, 2, 2)
+        weave(chunk(3), on_vector, 2)
         store(2, [on_scalar] * NT)
         first_pass(3)
         second_pass(3)

@@ -50,7 +50,7 @@ def tile_list_voxel_occupancy_map_kernel(
         place = keep.tile([P, S // STRIPE], U16, name="place")
         nc.sync.dma_start(pick[:], offs)
 
-        scale_win = keep.tile([P, T], U8, name="scale_win", align_bytes=64)
+        scale_win = tenant("page1", T, U8)
         nc.sync.dma_start(
             out=scale_win[0:32, :].bitcast(I32),
             in_=tab_scales.rearrange("a m t -> m a t").bitcast(I32),
@@ -83,9 +83,10 @@ def tile_list_voxel_occupancy_map_kernel(
         with nc.allow_non_contiguous_dma(reason="one bias value a partition"):
             nc.sync.dma_start(out=bias[0][:], in_=b1[0:PASS].rearrange("(q p) -> p q", p=P))
         nc.sync.dma_start(out=bias[1][:], in_=b1[PASS : 2 * PASS].rearrange("(p i) -> p i", i=PACK))
-        raw_head = [tenant("page%d" % (1 + a), PACK * 2 * P, F32) for a in range(PASSES)]
+        woven = {0: keep.tile([P, PACK * T2], BF16, name="woven0", align_bytes=64)}
+        raw_head = [woven[0][:].bitcast(F32)[:, a * S : (a + 1) * S] for a in range(PASSES)]
         for a in range(PASSES):
-            load_w1(raw_head[a][:], a, 0, 2 * P)
+            load_w1(raw_head[a], a, 0, 2 * P)
         load_table(1)
         conf_plain = keep.tile([P, S], F32, name="conf_plain")
         nc.sync.dma_start(out=conf_plain[:], in_=wgs)
@@ -137,7 +138,7 @@ def tile_list_voxel_occupancy_map_kernel(
 
         def open_page(n):
             pages[n] = tenant("page%d" % n, T2, F32)
-            nc.vector.memset(pages[n][:], 1.0)
+            (nc.gpsimd if n == 2 else nc.vector).memset(pages[n][:], 1.0)
 
         open_page(0)
 
@@ -149,10 +150,11 @@ def tile_list_voxel_occupancy_map_kernel(
                 out=table_plane[32 * q : 32 * q + 4, :].bitcast(I32),
                 in_=picked_scales[8 * q : 8 * q + 8, :].bitcast(I32),
             )
+        open_page(1)
         nc.vector.tensor_copy(picked[0][:].bitcast(U32), table[0][:].bitcast(U32).indirect(pick[:]))
 
         plain = {s: keep.tile([P, T2], BF16, name="plain%d" % s, align_bytes=64) for s in (0, 2, 3)}
-        grouped = keep.tile([P, 10 * PASS], BF16, name="grouped", align_bytes=64)
+        grouped = keep.tile([P, 12 * PASS], BF16, name="grouped", align_bytes=64)
         head_codes = keep.tile([P, 4 * P], U32, name="head_codes", align_bytes=64)
         head_scales = keep.tile([P, 4 * P], U8, name="head_scales", align_bytes=64)
         next_codes = keep.tile([P, 2 * P], U32, name="next_codes", align_bytes=64)
@@ -169,18 +171,17 @@ def tile_list_voxel_occupancy_map_kernel(
             nc.vector.quantize_mx(out=codes.bitcast(FP8X4), scales=scales, in_=values)
 
         wide = 2 * PASS
-        interleave(nc.scalar.copy, plain[0][:, 0:wide], raw_head[0][:], 1)
-        quantize(head_codes[:, 0 : 2 * P], head_scales[:, 0 : 2 * P], plain[0][:, 0:wide])
-        interleave(nc.vector.tensor_copy, plain[0][:, wide : 2 * wide], raw_head[1][:], 1)
-        quantize(head_codes[:, 2 * P : 4 * P], head_scales[:, 2 * P : 4 * P], plain[0][:, wide : 2 * wide])
-        open_page(1)
+        head_values = tenant("page2", 2 * wide, BF16)
+        interleave(nc.scalar.copy, head_values[:, 0:wide], raw_head[0], 1)
+        quantize(head_codes[:, 0 : 2 * P], head_scales[:, 0 : 2 * P], head_values[:, 0:wide])
+        interleave(nc.vector.tensor_copy, head_values[:, wide : 2 * wide], raw_head[1], 1)
+        quantize(head_codes[:, 2 * P : 4 * P], head_scales[:, 2 * P : 4 * P], head_values[:, wide : 2 * wide])
         open_page(2)
 
         def entries(offsets, cols):
             return offsets[:, cols.start // STRIPE : cols.stop // STRIPE]
 
-        for hf in range(2):
-            cols = slice(hf * BANK, (hf + 1) * BANK)
+        for cols in (slice(0, QUARTER), slice(QUARTER, BANK), slice(BANK, S)):
             nc.vector.tensor_copy(picked[1][:, cols].bitcast(U32), table[1][:].bitcast(U32).indirect(entries(pick, cols)))
 
         late_planes = tenant("wide1", (PACK + 1) * T2, BF16)
@@ -279,7 +280,6 @@ def tile_list_voxel_occupancy_map_kernel(
             dst = woven[0][:, 2 * g * PASS : (2 * g + 2) * PASS].bitcast(F32).rearrange("p (k t u) -> p k t u", k=2, u=2)
             nc.scalar.copy(dst, bank[:].rearrange("p (k u t) -> p k t u", k=2, u=2))
 
-        woven = {}
         z_codes = {}
         z_scales = [keep.tile([P, T2], U8, name="zs%d" % b, align_bytes=64) for b in range(PASSES)]
 
@@ -329,31 +329,25 @@ def tile_list_voxel_occupancy_map_kernel(
             nc.vector.tensor_scalar(left_first[:, cols], shared[:, cols], -1.0, 1.0, MULT, ADD)
         scatter(0, low, left_first[:])
         both_logits(1)
-        product_zero = scratch[:, BANK:S]
+        third_values = grouped[:, 10 * PASS : 12 * PASS]
+        product_zero = third_values.bitcast(F32)
         multiply(0, high, product_zero)
         left_one = raw_next[:, BANK : BANK + S]
-        product_one = [scratch[:, 6 * QUARTER : 8 * QUARTER], occ_of(2, high)]
-        for hf, cols in enumerate((low, high)):
-            multiply(1, cols, product_one[hf])
+        product_one = [scratch[:, 6 * QUARTER : 8 * QUARTER], shared]
+        multiply(1, low, product_one[0])
         interleave(nc.scalar.copy, grouped[:, 0:wide], raw_next[:, 0:wide], PASSES)
         quantize(next_codes[:], next_scales[:], grouped[:, 0:wide])
         complement(raw_next[:, 0:BANK], product_zero)
         scatter(0, high, raw_next[:, 0:BANK])
+        interleave(nc.scalar.copy, third_values, raw_next[:, wide : 2 * wide], PASSES)
         complement(left_one[:, low], product_one[0])
-        nc.gpsimd.tensor_scalar(
-            grouped[:, 0:wide].rearrange("p (a c j) -> p a c j", a=PASSES, j=PACK),
-            raw_next[:, wide : 2 * wide].rearrange("p (a j c) -> p a c j", a=PASSES, j=PACK),
-            1.0,
-            0.0,
-            MULT,
-            ADD,
-        )
+        multiply(1, high, product_one[1])
         complement(left_one[:, high], product_one[1])
         both_logits(2)
-        quantize(late_codes[:, 0 : 2 * P], late_scales[:, 0 : 2 * P], grouped[:, 0:wide])
+        quantize(late_codes[:, 0 : 2 * P], late_scales[:, 0 : 2 * P], third_values)
         scatter(1, whole, left_one)
         turned[0] = tenant("wide0", BLOCKS * PASS, BF16)
-        product_two = [turned[0][:, 7 * PASS : 9 * PASS].bitcast(F32), shared]
+        product_two = [turned[0][:, 7 * PASS : 9 * PASS].bitcast(F32), product_zero]
         for hf, cols in enumerate((low, high)):
             multiply(2, cols, product_two[hf])
         for a in range(PASSES):
@@ -403,7 +397,6 @@ def tile_list_voxel_occupancy_map_kernel(
             if s == 2:
                 load_old(5)
             if s == PACK - 1:
-                woven[0] = keep.tile([P, PACK * T2], BF16, name="woven0", align_bytes=64)
                 for g in range(BLOCKS // 2):
                     turn_back(g)
             if s == PACK + 1:

@@ -79,17 +79,16 @@ def tile_list_voxel_occupancy_map_kernel(
 
         bias = [keep.tile([P, PACK], F32, name="bias%d" % b) for b in range(PASSES)]
         load_table(0)
-        nc.sync.dma_start(place[:], offs2)
-        with nc.allow_non_contiguous_dma(reason="one bias value a partition"):
-            nc.sync.dma_start(out=bias[0][:], in_=b1[0:PASS].rearrange("(q p) -> p q", p=P))
-        nc.sync.dma_start(out=bias[1][:], in_=b1[PASS : 2 * PASS].rearrange("(p i) -> p i", i=PACK))
         woven = {0: keep.tile([P, PACK * T2], BF16, name="woven0", align_bytes=64)}
         raw_head = [woven[0][:].bitcast(F32)[:, a * S : (a + 1) * S] for a in range(PASSES)]
         for a in range(PASSES):
             load_w1(raw_head[a], a, 0, 2 * P)
         load_table(1)
+        with nc.allow_non_contiguous_dma(reason="one bias value a partition"):
+            nc.sync.dma_start(out=bias[0][:], in_=b1[0:PASS].rearrange("(q p) -> p q", p=P))
         conf_plain = keep.tile([P, S], F32, name="conf_plain")
         nc.sync.dma_start(out=conf_plain[:], in_=wgs)
+        nc.sync.dma_start(place[:], offs2)
         raw_next = tenant("rows3", 2 * PASSES * PASS, F32)
         for q in (2, 3):
             for a in range(PASSES):
@@ -113,6 +112,7 @@ def tile_list_voxel_occupancy_map_kernel(
         load_w1(raw_late[0][:], 0, PASS, PASS)
         load_old(0)
         load_w1(raw_late[1][:], 1, PASS, PASS)
+        nc.sync.dma_start(out=bias[1][:], in_=b1[PASS : 2 * PASS].rearrange("(p i) -> p i", i=PACK))
         load_old(1)
         conf_pairs = [tenant("conf%d" % n, 2 * S, F32) for n in range(2)]
         conf_rows = wgs.rearrange("(m n i) j -> n m (i j)", n=2, i=2)
@@ -157,9 +157,9 @@ def tile_list_voxel_occupancy_map_kernel(
         grouped = keep.tile([P, 12 * PASS], BF16, name="grouped", align_bytes=64)
         head_codes = keep.tile([P, 4 * P], U32, name="head_codes", align_bytes=64)
         head_scales = keep.tile([P, 4 * P], U8, name="head_scales", align_bytes=64)
-        next_codes = keep.tile([P, 2 * P], U32, name="next_codes", align_bytes=64)
-        next_scales = keep.tile([P, 2 * P], U8, name="next_scales", align_bytes=64)
-        late_scales = keep.tile([P, 10 * P], U8, name="late_scales", align_bytes=64)
+        next_codes = keep.tile([P, 4 * P], U32, name="next_codes", align_bytes=64)
+        next_scales = keep.tile([P, 4 * P], U8, name="next_scales", align_bytes=64)
+        late_scales = keep.tile([P, 8 * P], U8, name="late_scales", align_bytes=64)
 
         def interleave(copy, dst, src, groups):
             copy(
@@ -199,24 +199,27 @@ def tile_list_voxel_occupancy_map_kernel(
 
         def occ_of(s, cols):
             if s == 0:
-                return scratch[:, BANK + cols.start : BANK + cols.stop]
+                return scratch[:, S + cols.start : S + cols.stop]
             if s == 1:
                 return occ_one[:, cols]
             if s == 2 and cols.start == 0:
-                return scratch[:, 5 * QUARTER : 7 * QUARTER]
+                return scratch[:, 7 * QUARTER : 9 * QUARTER]
+            if s == 3 and cols.start == 0:
+                return raw_late[0][:, cols]
             if s == 7:
                 return late_planes[:, 3 * T2 // 2 : 5 * T2 // 2].bitcast(F32)[:, cols]
             return plane_of(s - 2).bitcast(F32)[:, cols]
 
-        late_codes = keep.tile([P, 10 * P], U32, name="late_codes", align_bytes=64)
+        late_codes = keep.tile([P, 8 * P], U32, name="late_codes", align_bytes=64)
 
         def weights_of(s, a):
             if s < 2:
                 at = a * 2 * P + s * P
                 return head_codes[:, at : at + P], head_scales[:, at : at + P]
-            if s == 2:
-                return next_codes[:, a * P : (a + 1) * P], next_scales[:, a * P : (a + 1) * P]
-            at = a * P if s == 3 else 2 * P + a * PASS + (s - PACK) * P
+            if s < PACK:
+                at = (2 * (s - 2) + a) * P
+                return next_codes[:, at : at + P], next_scales[:, at : at + P]
+            at = a * PASS + (s - PACK) * P
             return late_codes[:, at : at + P], late_scales[:, at : at + P]
 
         banks_used = [0]
@@ -322,45 +325,42 @@ def tile_list_voxel_occupancy_map_kernel(
         for cols in (first, second, high):
             logits(0, cols)
         left_first = keep.tile([P, BANK], F32, name="left_first")
-        shared = scratch[:, 0:BANK]
+        shared = scratch[:, QUARTER : 3 * QUARTER]
         for cols in (first, second):
             nc.vector.tensor_tensor(shared[:, cols], occ_of(0, cols), conf_plain[:, cols], MULT)
         for cols in (first, second):
             nc.vector.tensor_scalar(left_first[:, cols], shared[:, cols], -1.0, 1.0, MULT, ADD)
         scatter(0, low, left_first[:])
-        both_logits(1)
-        third_values = grouped[:, 10 * PASS : 12 * PASS]
-        product_zero = third_values.bitcast(F32)
+        logits(1, low)
+        product_zero = scratch[:, 10 * QUARTER : 12 * QUARTER]
         multiply(0, high, product_zero)
-        left_one = raw_next[:, BANK : BANK + S]
-        product_one = [scratch[:, 6 * QUARTER : 8 * QUARTER], shared]
+        left_one = raw_next[:, 0:S]
+        product_one = [scratch[:, 8 * QUARTER : 10 * QUARTER], scratch[:, 0:BANK]]
         multiply(1, low, product_one[0])
-        interleave(nc.scalar.copy, grouped[:, 0:wide], raw_next[:, 0:wide], PASSES)
-        quantize(next_codes[:], next_scales[:], grouped[:, 0:wide])
-        complement(raw_next[:, 0:BANK], product_zero)
-        scatter(0, high, raw_next[:, 0:BANK])
-        interleave(nc.scalar.copy, third_values, raw_next[:, wide : 2 * wide], PASSES)
+        for n in range(2):
+            interleave(nc.scalar.copy, grouped[:, n * wide : (n + 1) * wide], raw_next[:, n * wide : (n + 1) * wide], PASSES)
+        quantize(next_codes[:], next_scales[:], grouped[:, 0 : 2 * wide])
+        complement(raw_next[:, S : S + BANK], product_zero)
+        scatter(0, high, raw_next[:, S : S + BANK])
+        logits(1, high)
         complement(left_one[:, low], product_one[0])
         multiply(1, high, product_one[1])
         complement(left_one[:, high], product_one[1])
         both_logits(2)
-        quantize(late_codes[:, 0 : 2 * P], late_scales[:, 0 : 2 * P], third_values)
         scatter(1, whole, left_one)
         turned[0] = tenant("wide0", BLOCKS * PASS, BF16)
-        product_two = [turned[0][:, 7 * PASS : 9 * PASS].bitcast(F32), product_zero]
-        for hf, cols in enumerate((low, high)):
-            multiply(2, cols, product_two[hf])
-        for a in range(PASSES):
+        product_two = turned[0][:, 6 * PASS : 10 * PASS].bitcast(F32)
+        for cols in (low, high):
+            multiply(2, cols, product_two[:, cols])
+        for a, cols in enumerate((low, high)):
             nc.scalar.copy(
-                grouped[:, (2 + 4 * a) * PASS : (6 + 4 * a) * PASS].rearrange("p (t m j) -> p m j t", t=PACK, j=PACK),
+                grouped[:, (4 + 4 * a) * PASS : (8 + 4 * a) * PASS].rearrange("p (t m j) -> p m j t", t=PACK, j=PACK),
                 raw_late[a][:].rearrange("p (j m t) -> p m j t", j=PACK, t=PACK),
             )
-        left = {2: raw_late[1][:, 0:S]}
-        both_logits(3)
-        for hf, cols in ((1, high), (0, low)):
-            complement(left[2][:, cols], product_two[hf])
+            logits(3, cols)
+        left = {2: raw_late[1][:, 0:S], 3: occ_one[:]}
+        complement(left[2], product_two)
         load_old(3)
-        load_old(4)
         w4_plane = keep.tile([P, PASSES, N], U8, name="w4_plane", align_bytes=64)
         nc.vector.memset(w4_plane[:].bitcast(I32), 0)
         for q in range(4):
@@ -369,17 +369,21 @@ def tile_list_voxel_occupancy_map_kernel(
                 in_=w4_scales[:, 4 * q : 4 * q + 4, :].rearrange("a r c -> r a c").bitcast(I32),
             )
         fade_old(0)
+        product_three = [scratch[:, BANK:S], scratch[:, S : S + BANK]]
+        multiply(3, low, product_three[0])
+        load_old(4)
         turn(0)
-        quantize(late_codes[:, 2 * P : 10 * P], late_scales[:, 2 * P : 10 * P], grouped[:, 2 * PASS : 10 * PASS])
+        quantize(late_codes[:], late_scales[:], grouped[:, 4 * PASS : 12 * PASS])
 
         def weigh(s):
             if s == AHEAD:
-                left[s] = scratch[:, BANK : BANK + S]
+                multiply(s, high, product_three[1])
+                complement(left[s], scratch[:, BANK : BANK + S])
             else:
                 product = tenant(old_slot[s - AHEAD], S, F32)
                 left[s] = product[:]
-            multiply(s, whole, left[s])
-            complement(left[s], left[s])
+                multiply(s, whole, left[s])
+                complement(left[s], left[s])
             if s < last:
                 both_logits(s + 1)
 
@@ -389,6 +393,9 @@ def tile_list_voxel_occupancy_map_kernel(
                 scatter(s, whole, left[s])
             if s + 2 <= last:
                 weigh(s + 2)
+            if s == PACK:
+                for g in range(BLOCKS // 2):
+                    turn_back(g)
             if s == PACK + 1:
                 load_old(6)
             fade_old(s)
@@ -396,9 +403,6 @@ def tile_list_voxel_occupancy_map_kernel(
                 turn(s)
             if s == 2:
                 load_old(5)
-            if s == PACK - 1:
-                for g in range(BLOCKS // 2):
-                    turn_back(g)
             if s == PACK + 1:
                 woven[1] = tenant("wide0", PACK * T2, BF16)
                 for c in range(CHUNKS):

@@ -32,6 +32,8 @@ AHEAD = 3
 STRIPE = 16
 QUARTER = BANK // 2
 BLOCKS = T2 // P
+EDGES = [0, BANK, 2 * BANK, 3 * BANK, 3 * BANK + QUARTER, T2]
+PIECES = len(EDGES) - 1
 
 
 def tile_list_voxel_occupancy_map_kernel(
@@ -90,10 +92,8 @@ def tile_list_voxel_occupancy_map_kernel(
         nc.sync.dma_start(out=conf_plain[:], in_=wgs)
         nc.sync.dma_start(place[:], offs2)
         raw_next = tenant("rows3", 2 * PASSES * PASS, F32)
-        for q in (2, 3):
-            for a in range(PASSES):
-                first = ((q - 2) * PASSES + a) * PASS
-                load_w1(raw_next[:, first : first + PASS], a, q * P, P)
+        for a in range(PASSES):
+            load_w1(raw_next[:, a * S : (a + 1) * S], a, 2 * P, 2 * P)
 
         old_rows = old.rearrange("(b p i) t -> b i p t", b=PASSES, i=PACK)
         old_tiles = {}
@@ -128,9 +128,9 @@ def tile_list_voxel_occupancy_map_kernel(
             return conf_pairs[i // 2][:, (i % 2) * S : (i % 2 + 1) * S]
 
         old_last = {}
-        for c in range(CHUNKS):
-            old_last[c] = tenant("last%d" % c, BANK, F32)
-            nc.sync.dma_start(out=old_last[c][:], in_=old_rows[PASSES - 1, PACK - 1][:, c * BANK : (c + 1) * BANK])
+        for c in range(PIECES):
+            old_last[c] = tenant("last%d" % c, EDGES[c + 1] - EDGES[c], F32)
+            nc.sync.dma_start(out=old_last[c][:], in_=old_rows[PASSES - 1, PACK - 1][:, EDGES[c] : EDGES[c + 1]])
         w4_codes = keep.tile([P, PASSES, 2 * N], U8, name="w4_codes", align_bytes=64)
         nc.sync.dma_start(out=w4_codes[:].bitcast(I32), in_=w4_words.rearrange("a p c -> p a c").bitcast(I32))
 
@@ -204,8 +204,6 @@ def tile_list_voxel_occupancy_map_kernel(
                 return occ_one[:, cols]
             if s == 2 and cols.start == 0:
                 return scratch[:, 7 * QUARTER : 9 * QUARTER]
-            if s == 3 and cols.start == 0:
-                return raw_late[0][:, cols]
             if s == 7:
                 return late_planes[:, 3 * T2 // 2 : 5 * T2 // 2].bitcast(F32)[:, cols]
             return plane_of(s - 2).bitcast(F32)[:, cols]
@@ -217,7 +215,7 @@ def tile_list_voxel_occupancy_map_kernel(
                 at = a * 2 * P + s * P
                 return head_codes[:, at : at + P], head_scales[:, at : at + P]
             if s < PACK:
-                at = (2 * (s - 2) + a) * P
+                at = (2 * a + s - 2) * P
                 return next_codes[:, at : at + P], next_scales[:, at : at + P]
             at = a * PASS + (s - PACK) * P
             return late_codes[:, at : at + P], late_scales[:, at : at + P]
@@ -260,7 +258,7 @@ def tile_list_voxel_occupancy_map_kernel(
             nc.gpsimd.tensor_tensor(plane_of(s), old_tiles[s], pages[s % PAGES][:], MULT)
 
         def fade_last(c):
-            nc.vector.tensor_tensor(plane_of(last)[:, chunk(c)], old_last[c][:], pages[last % PAGES][:, chunk(c)], MULT)
+            nc.vector.tensor_tensor(plane_of(last)[:, piece(c)], old_last[c][:], pages[last % PAGES][:, piece(c)], MULT)
 
         turned = {}
 
@@ -289,13 +287,16 @@ def tile_list_voxel_occupancy_map_kernel(
         def chunk(c):
             return slice(c * BANK, (c + 1) * BANK)
 
+        def piece(c):
+            return slice(EDGES[c], EDGES[c + 1])
+
         def weave(cols, copy, first_plane):
             dst = woven[1][:, cols.start * PACK : cols.stop * PACK].rearrange("p (m i t) -> p m t i", i=4, t=PACK)
             src = late_planes[:].rearrange("p (t c) -> p t c", c=T2)[:, first_plane : first_plane + 2, cols]
             copy(dst[:, :, first_plane : first_plane + 2, :], src.rearrange("p t (m i) -> p m t i", i=4))
 
         def quantize_z(b, c):
-            quantize(z_codes[(b, c)], z_scales[b][:, chunk(c)], woven[b][:, c * BANK * PACK : (c + 1) * BANK * PACK])
+            quantize(z_codes[(b, c)], z_scales[b][:, piece(c)], woven[b][:, EDGES[c] * PACK : EDGES[c + 1] * PACK])
 
         sums = {}
         staged = {}
@@ -306,20 +307,22 @@ def tile_list_voxel_occupancy_map_kernel(
                 if b == 0:
                     sums[g] = psum.tile([P, BANK], F32, name="sums", tag="bank%d" % (g % 8))
                 nc.tensor.matmul_mx(
-                    out=sums[g][:],
+                    out=sums[g][:, 0 : EDGES[c + 1] - EDGES[c]],
                     lhsT=w4_codes[:, b, 2 * n * P : 2 * (n + 1) * P].bitcast(FP4X4),
                     lhsT_scale=w4_plane[:, b, n * P : (n + 1) * P],
                     rhs=z_codes[(b, c)].bitcast(FP8X4),
-                    rhs_scale=z_scales[b][:, chunk(c)],
+                    rhs_scale=z_scales[b][:, piece(c)],
                     start=(b == 0),
                     stop=(b == PASSES - 1),
                 )
 
         def store(c, copies):
-            staged[c] = tenant(old_slot[c], NT * BANK, F32)
+            width = EDGES[c + 1] - EDGES[c]
+            staged[c] = tenant(old_slot[c if c < PACK else c + 1], NT * width, F32)
             for n in range(NT):
-                copies[n](staged[c][:, chunk(n)], sums[c * NT + n][:])
-                nc.sync.dma_start(out=out[n * P : (n + 1) * P, chunk(c)], in_=staged[c][:, chunk(n)])
+                held = staged[c][:, n * width : (n + 1) * width]
+                copies[n](held, sums[c * NT + n][:, 0:width])
+                nc.sync.dma_start(out=out[n * P : (n + 1) * P, piece(c)], in_=held)
 
         first, second = slice(0, QUARTER), slice(QUARTER, BANK)
         for cols in (first, second, high):
@@ -338,7 +341,7 @@ def tile_list_voxel_occupancy_map_kernel(
         product_one = [scratch[:, 8 * QUARTER : 10 * QUARTER], scratch[:, 0:BANK]]
         multiply(1, low, product_one[0])
         for n in range(2):
-            interleave(nc.scalar.copy, grouped[:, n * wide : (n + 1) * wide], raw_next[:, n * wide : (n + 1) * wide], PASSES)
+            interleave(nc.scalar.copy, grouped[:, n * wide : (n + 1) * wide], raw_next[:, n * wide : (n + 1) * wide], 1)
         quantize(next_codes[:], next_scales[:], grouped[:, 0 : 2 * wide])
         complement(raw_next[:, S : S + BANK], product_zero)
         scatter(0, high, raw_next[:, S : S + BANK])
@@ -352,13 +355,13 @@ def tile_list_voxel_occupancy_map_kernel(
         product_two = turned[0][:, 6 * PASS : 10 * PASS].bitcast(F32)
         for cols in (low, high):
             multiply(2, cols, product_two[:, cols])
-        for a, cols in enumerate((low, high)):
+        for a in range(PASSES):
             nc.scalar.copy(
                 grouped[:, (4 + 4 * a) * PASS : (8 + 4 * a) * PASS].rearrange("p (t m j) -> p m j t", t=PACK, j=PACK),
                 raw_late[a][:].rearrange("p (j m t) -> p m j t", j=PACK, t=PACK),
             )
-            logits(3, cols)
-        left = {2: raw_late[1][:, 0:S], 3: occ_one[:]}
+        both_logits(3)
+        left = {2: raw_late[1][:, 0:S]}
         complement(left[2], product_two)
         load_old(3)
         w4_plane = keep.tile([P, PASSES, N], U8, name="w4_plane", align_bytes=64)
@@ -369,21 +372,18 @@ def tile_list_voxel_occupancy_map_kernel(
                 in_=w4_scales[:, 4 * q : 4 * q + 4, :].rearrange("a r c -> r a c").bitcast(I32),
             )
         fade_old(0)
-        product_three = [scratch[:, BANK:S], scratch[:, S : S + BANK]]
-        multiply(3, low, product_three[0])
         load_old(4)
         turn(0)
         quantize(late_codes[:], late_scales[:], grouped[:, 4 * PASS : 12 * PASS])
 
         def weigh(s):
             if s == AHEAD:
-                multiply(s, high, product_three[1])
-                complement(left[s], scratch[:, BANK : BANK + S])
+                left[s] = scratch[:, S : 2 * S]
             else:
                 product = tenant(old_slot[s - AHEAD], S, F32)
                 left[s] = product[:]
-                multiply(s, whole, left[s])
-                complement(left[s], left[s])
+            multiply(s, whole, left[s])
+            complement(left[s], left[s])
             if s < last:
                 both_logits(s + 1)
 
@@ -409,18 +409,18 @@ def tile_list_voxel_occupancy_map_kernel(
                     weave(chunk(c), nc.scalar.copy, 0)
 
         second_codes = tenant("conf0", T2, U32)
-        first_slot = [old_slot[4], "last1", "last2", "last3"]
+        first_slot = [old_slot[4], "last1", "last2", "last3", "last4"]
         on_scalar = nc.scalar.copy
         on_vector = nc.vector.tensor_copy
 
         def first_pass(c):
-            first_codes = tenant(first_slot[c], BANK, U32)
+            first_codes = tenant(first_slot[c], EDGES[c + 1] - EDGES[c], U32)
             z_codes[(0, c)] = first_codes[:]
             quantize_z(0, c)
             readout(c, 0)
 
         def second_pass(c):
-            z_codes[(1, c)] = second_codes[:, chunk(c)]
+            z_codes[(1, c)] = second_codes[:, piece(c)]
             quantize_z(1, c)
             readout(c, 1)
 
@@ -444,8 +444,13 @@ def tile_list_voxel_occupancy_map_kernel(
         first_pass(2)
         fade_last(3)
         second_pass(2)
-        weave(chunk(3), on_vector, 2)
+        weave(piece(3), on_vector, 2)
         store(2, [on_scalar] * NT)
+        fade_last(4)
         first_pass(3)
         second_pass(3)
-        store(3, [on_vector, on_scalar, on_vector])
+        weave(piece(4), on_vector, 2)
+        store(3, [on_scalar] * NT)
+        first_pass(4)
+        second_pass(4)
+        store(4, [on_vector, on_scalar, on_vector])

@@ -25,14 +25,13 @@ PASS = P * PACK
 BANK = 512
 PASSES = 2
 SLICES = PASSES * PACK
-CHUNKS = T2 // BANK
+LAST = SLICES - 1
 NT = N // P
 PAGES = 3
-AHEAD = 3
 STRIPE = 16
-QUARTER = BANK // 2
+HALF = BANK // 2
 BLOCKS = T2 // P
-EDGES = [0, BANK, 2 * BANK, 3 * BANK, 3 * BANK + QUARTER, T2]
+EDGES = [0,512,1024,1536,1792,2048]
 PIECES = len(EDGES) - 1
 
 
@@ -45,13 +44,18 @@ def tile_list_voxel_occupancy_map_kernel(
         slots = ctx.enter_context(tc.tile_pool(name="slots", bufs=1))
         psum = ctx.enter_context(tc.psum_pool(name="psum", bufs=1))
 
+        def held(name, columns, dtype):
+            return keep.tile([P, columns], dtype, name=name, align_bytes=64)
+
         def tenant(tag, columns, dtype):
             return slots.tile([P, columns], dtype, name="tenant", tag=tag, align_bytes=64)
+
+        low, high, whole = slice(0, BANK), slice(BANK, S), slice(0, S)
+        first, second = slice(0, HALF), slice(HALF, BANK)
 
         pick = keep.tile([P, S // STRIPE], U16, name="pick")
         place = keep.tile([P, S // STRIPE], U16, name="place")
         nc.sync.dma_start(pick[:], offs)
-
         scale_win = tenant("page1", T, U8)
         nc.sync.dma_start(
             out=scale_win[0:32, :].bitcast(I32),
@@ -59,166 +63,137 @@ def tile_list_voxel_occupancy_map_kernel(
         )
         nc.vector.memset(scale_win[32:64, :].bitcast(I32), 0)
         nc.vector.memset(scale_win[64:P, :].bitcast(I32), 0)
-        table_plane = keep.tile([P, PASSES * S], U8, name="table_plane", align_bytes=64)
+        table_plane = held("table_plane", PASSES * S, U8)
         nc.gpsimd.memset(table_plane[:].bitcast(I32), 0)
-        ident_pairs = keep.tile([P, P], F32, name="ident_pairs")
-        ident = keep.tile([P, P], BF16, name="ident")
+        ident_pairs = held("ident_pairs", P, F32)
+        ident = held("ident", P, BF16)
         make_identity(nc, ident_pairs[:])
         make_identity(nc, ident[:])
-
-        table = []
 
         def load_table(a):
             words = tenant("wide%d" % a, T, I32)
             nc.sync.dma_start(out=words[:], in_=tab_words[a].rearrange("p t i -> p (t i)").bitcast(I32))
-            table.append(words)
+            return words
 
-        def load_w1(raw, a, first, count):
+        def load_w1(raw, a, start, count):
             nc.sync.dma_start(
                 out=raw.rearrange("p (j c) -> p j c", j=PACK),
-                in_=w1[a * PASS : (a + 1) * PASS, first : first + count].rearrange("(p j) c -> p j c", j=PACK),
+                in_=w1[a * PASS : (a + 1) * PASS, start : start + count].rearrange("(p j) c -> p j c", j=PACK),
             )
 
-        bias = [keep.tile([P, PACK], F32, name="bias%d" % b) for b in range(PASSES)]
-        load_table(0)
-        woven = {0: keep.tile([P, PACK * T2], BF16, name="woven0", align_bytes=64)}
+        woven = {0: held("woven0", PACK * T2, BF16)}
         raw_head = [woven[0][:].bitcast(F32)[:, a * S : (a + 1) * S] for a in range(PASSES)]
+        table = [load_table(0)]
         for a in range(PASSES):
             load_w1(raw_head[a], a, 0, 2 * P)
-        load_table(1)
+        table.append(load_table(1))
+
+        bias = [keep.tile([P, PACK], F32, name="bias%d" % b) for b in range(PASSES)]
         with nc.allow_non_contiguous_dma(reason="one bias value a partition"):
             nc.sync.dma_start(out=bias[0][:], in_=b1[0:PASS].rearrange("(q p) -> p q", p=P))
-        conf_plain = keep.tile([P, S], F32, name="conf_plain")
+        conf_plain = held("conf_plain", S, F32)
         nc.sync.dma_start(out=conf_plain[:], in_=wgs)
         nc.sync.dma_start(place[:], offs2)
-        raw_next = tenant("rows3", 2 * PASSES * PASS, F32)
+        raw_next = tenant("rows2", PASSES * S, F32)
         for a in range(PASSES):
             load_w1(raw_next[:, a * S : (a + 1) * S], a, 2 * P, 2 * P)
 
-        old_rows = old.rearrange("(b p i) t -> b i p t", b=PASSES, i=PACK)
-        old_tiles = {}
-        old_slot = ["rows0", "rows1", "rows2", "rows3", "rows4", "rows5"]
+        old_dealt = old.rearrange("(b p i) t -> b i p t", b=PASSES, i=PACK)
+        old_rows = {}
 
-        def load_old(s):
-            if s == 6:
-                old_tiles[s] = old_sixth
-            else:
-                rows = tenant(old_slot[s], T2, F32)
-                old_tiles[s] = rows[:]
-            source = old[s * P : (s + 1) * P, :] if s < PACK else old_rows[1, s - PACK]
-            nc.sync.dma_start(out=old_tiles[s], in_=source)
+        def load_old(s, rows):
+            old_rows[s] = rows
+            nc.sync.dma_start(out=rows, in_=old[s * P : (s + 1) * P, :] if s < PACK else old_dealt[1, s - PACK])
 
-        raw_late = [tenant("rows%d" % (4 + a), PACK * PASS, F32) for a in range(PASSES)]
-        load_w1(raw_late[0][:], 0, PASS, PASS)
-        load_old(0)
-        load_w1(raw_late[1][:], 1, PASS, PASS)
+        def row_slot(n, columns=T2):
+            rows = tenant("rows%d" % n, columns, F32)
+            return rows[:]
+
+        raw_late = [row_slot(3 + a) for a in range(PASSES)]
+        load_w1(raw_late[0], 0, PASS, PASS)
+        load_old(0, row_slot(0))
+        load_w1(raw_late[1], 1, PASS, PASS)
         nc.sync.dma_start(out=bias[1][:], in_=b1[PASS : 2 * PASS].rearrange("(p i) -> p i", i=PACK))
-        load_old(1)
-        conf_pairs = [tenant("conf%d" % n, 2 * S, F32) for n in range(2)]
-        conf_rows = wgs.rearrange("(m n i) j -> n m (i j)", n=2, i=2)
-        for n in range(2):
+        load_old(1, row_slot(1))
+
+        conf = {s: conf_plain for s in range(PACK)}
+        conf_rows = wgs.rearrange("(m i) j -> i m j", i=PACK)
+
+        def load_conf(s):
+            conf[s] = held("conf%d" % s, S, F32)
             for q in (0, 2, 1, 3):
-                nc.sync.dma_start(out=conf_pairs[n][32 * q : 32 * q + 32, :], in_=conf_rows[n])
-        load_old(2)
+                nc.sync.dma_start(out=conf[s][32 * q : 32 * q + 32, :], in_=conf_rows[s - PACK])
 
-        def conf_of(s):
-            if s < PACK:
-                return conf_plain[:]
-            i = s - PACK
-            return conf_pairs[i // 2][:, (i % 2) * S : (i % 2 + 1) * S]
-
-        old_last = {}
-        for c in range(PIECES):
-            old_last[c] = tenant("last%d" % c, EDGES[c + 1] - EDGES[c], F32)
-            nc.sync.dma_start(out=old_last[c][:], in_=old_rows[PASSES - 1, PACK - 1][:, EDGES[c] : EDGES[c + 1]])
-        w4_codes = keep.tile([P, PASSES, 2 * N], U8, name="w4_codes", align_bytes=64)
-        nc.sync.dma_start(out=w4_codes[:].bitcast(I32), in_=w4_words.rearrange("a p c -> p a c").bitcast(I32))
+        load_conf(4)
 
         pages = {}
 
-        def open_page(n):
+        def open_page(n, engine):
             pages[n] = tenant("page%d" % n, T2, F32)
-            (nc.gpsimd if n == 2 else nc.vector).memset(pages[n][:], 1.0)
-
-        open_page(0)
-
-        picked_scales = keep.tile([P, S], U8, name="picked_scales", align_bytes=64)
-        picked = [keep.tile([P, S], I32, name="picked%d" % a, align_bytes=64) for a in range(PASSES)]
-        nc.vector.tensor_copy(picked_scales[:], scale_win[:].indirect(pick[:]))
-        for q in range(4):
-            nc.gpsimd.dma_start(
-                out=table_plane[32 * q : 32 * q + 4, :].bitcast(I32),
-                in_=picked_scales[8 * q : 8 * q + 8, :].bitcast(I32),
-            )
-        open_page(1)
-        nc.vector.tensor_copy(picked[0][:].bitcast(U32), table[0][:].bitcast(U32).indirect(pick[:]))
-
-        plain = {s: keep.tile([P, T2], BF16, name="plain%d" % s, align_bytes=64) for s in (0, 2, 3)}
-        grouped = keep.tile([P, 12 * PASS], BF16, name="grouped", align_bytes=64)
-        head_codes = keep.tile([P, 4 * P], U32, name="head_codes", align_bytes=64)
-        head_scales = keep.tile([P, 4 * P], U8, name="head_scales", align_bytes=64)
-        next_codes = keep.tile([P, 4 * P], U32, name="next_codes", align_bytes=64)
-        next_scales = keep.tile([P, 4 * P], U8, name="next_scales", align_bytes=64)
-        late_scales = keep.tile([P, 8 * P], U8, name="late_scales", align_bytes=64)
-
-        def interleave(copy, dst, src, groups):
-            copy(
-                dst.rearrange("p (a m i j) -> p a m j i", a=groups, i=4, j=PACK),
-                src.rearrange("p (a j m i) -> p a m j i", a=groups, i=4, j=PACK),
-            )
-
-        def quantize(codes, scales, values):
-            nc.vector.quantize_mx(out=codes.bitcast(FP8X4), scales=scales, in_=values)
-
-        wide = 2 * PASS
-        head_values = tenant("page2", 2 * wide, BF16)
-        interleave(nc.scalar.copy, head_values[:, 0:wide], raw_head[0], 1)
-        quantize(head_codes[:, 0 : 2 * P], head_scales[:, 0 : 2 * P], head_values[:, 0:wide])
-        interleave(nc.vector.tensor_copy, head_values[:, wide : 2 * wide], raw_head[1], 1)
-        quantize(head_codes[:, 2 * P : 4 * P], head_scales[:, 2 * P : 4 * P], head_values[:, wide : 2 * wide])
-        open_page(2)
+            engine.memset(pages[n][:], 1.0)
 
         def entries(offsets, cols):
             return offsets[:, cols.start // STRIPE : cols.stop // STRIPE]
 
-        for cols in (slice(0, QUARTER), slice(QUARTER, BANK), slice(BANK, S)):
+        open_page(0, nc.vector)
+        picked_scales = held("picked_scales", S, U8)
+        picked = [held("picked%d" % a, S, I32) for a in range(PASSES)]
+        nc.vector.tensor_copy(picked_scales[:], scale_win[:].indirect(pick[:]))
+        for q in range(4):
+            nc.scalar.dma_start(
+                out=table_plane[32 * q : 32 * q + 4, :].bitcast(I32),
+                in_=picked_scales[8 * q : 8 * q + 8, :].bitcast(I32),
+            )
+        open_page(1, nc.gpsimd)
+        nc.vector.tensor_copy(picked[0][:].bitcast(U32), table[0][:].bitcast(U32).indirect(pick[:]))
+
+        codes = {name: held(name + "_codes", n * P, U32) for name, n in (("head", 4), ("next", 4), ("late", 8))}
+        scales = {name: held(name + "_scales", n * P, U8) for name, n in (("head", 4), ("next", 4), ("late", 8))}
+
+        def interleave(copy, dst, src):
+            copy(
+                dst.rearrange("p (m i j) -> p m j i", i=4, j=PACK),
+                src.rearrange("p (j m i) -> p m j i", i=4, j=PACK),
+            )
+
+        def quantize(words, plane, values):
+            nc.vector.quantize_mx(out=words.bitcast(FP8X4), scales=plane, in_=values)
+
+        head_values = tenant("page2", PASSES * S, BF16)
+        for a, copy in enumerate((nc.scalar.copy, nc.vector.tensor_copy)):
+            interleave(copy, head_values[:, a * S : (a + 1) * S], raw_head[a])
+            at = slice(a * 2 * P, (a + 1) * 2 * P)
+            quantize(codes["head"][:, at], scales["head"][:, at], head_values[:, a * S : (a + 1) * S])
+        open_page(2, nc.gpsimd)
+        for cols in (first, second, high):
             nc.vector.tensor_copy(picked[1][:, cols].bitcast(U32), table[1][:].bitcast(U32).indirect(entries(pick, cols)))
 
+        work = held("work", 9 * BANK, F32)
+        next_values = work[:, BANK : 3 * BANK].bitcast(BF16)
+        late_values = work[:, 3 * BANK : 7 * BANK].bitcast(BF16)
+        ring = [work[:, 5 * BANK : 7 * BANK], work[:, 0 : 2 * BANK], work[:, 7 * BANK : 9 * BANK]]
+        occ = {s: held("occ%d" % s, S, F32)[:] for s in range(2)}
+        plain = [held("plain%d" % n, T2, BF16) for n in range(2)]
         late_planes = tenant("wide1", (PACK + 1) * T2, BF16)
-        old_sixth = late_planes[:, (PACK - 1) * T2 : (PACK + 1) * T2].bitcast(F32)
 
         def plane_of(s):
             if s == 1:
-                return raw_late[1][:, S : 2 * S].bitcast(BF16)
+                return late_values[:, 0:T2]
             if s < PACK:
-                return plain[s][:]
+                return plain[s % 2][:]
             return late_planes[:, (s - PACK) * T2 : (s - PACK + 1) * T2]
 
-        scratch = grouped[:].bitcast(F32)
-        occ_one = keep.tile([P, S], F32, name="occ_one", align_bytes=64)
+        left = {}
 
-        def occ_of(s, cols):
-            if s == 0:
-                return scratch[:, S + cols.start : S + cols.stop]
-            if s == 1:
-                return occ_one[:, cols]
-            if s == 2 and cols.start == 0:
-                return scratch[:, 7 * QUARTER : 9 * QUARTER]
-            if s == 7:
-                return late_planes[:, 3 * T2 // 2 : 5 * T2 // 2].bitcast(F32)[:, cols]
-            return plane_of(s - 2).bitcast(F32)[:, cols]
-
-        late_codes = keep.tile([P, 8 * P], U32, name="late_codes", align_bytes=64)
+        def product_of(s):
+            return left[s] if s > 2 else ring[s]
 
         def weights_of(s, a):
-            if s < 2:
-                at = a * 2 * P + s * P
-                return head_codes[:, at : at + P], head_scales[:, at : at + P]
             if s < PACK:
-                at = (2 * a + s - 2) * P
-                return next_codes[:, at : at + P], next_scales[:, at : at + P]
-            at = a * PASS + (s - PACK) * P
-            return late_codes[:, at : at + P], late_scales[:, at : at + P]
+                name, at = ("head", "next")[s // 2], (2 * a + s % 2) * P
+            else:
+                name, at = "late", a * PASS + (s - PACK) * P
+            return codes[name][:, at : at + P], scales[name][:, at : at + P]
 
         banks_used = [0]
 
@@ -227,26 +202,20 @@ def tile_list_voxel_occupancy_map_kernel(
             banks_used[0] = banks_used[0] + 1
             count = cols.stop - cols.start
             for a in range(PASSES):
-                codes, scales = weights_of(s, a)
+                words, plane = weights_of(s, a)
                 nc.tensor.matmul_mx(
                     out=acc[:, 0:count],
-                    lhsT=codes.bitcast(FP8X4),
-                    lhsT_scale=scales,
+                    lhsT=words.bitcast(FP8X4),
+                    lhsT_scale=plane,
                     rhs=picked[a][:, cols].bitcast(FP8X4),
                     rhs_scale=table_plane[:, a * S + cols.start : a * S + cols.stop],
                     start=(a == 0),
                     stop=(a == PASSES - 1),
                 )
-            nc.scalar.activation(occ_of(s, cols), acc[:, 0:count], SIGMOID, bias=bias[s // PACK][:, s % PACK : s % PACK + 1])
+            nc.scalar.activation(occ[s][:, cols], acc[:, 0:count], SIGMOID, bias=bias[s // PACK][:, s % PACK : s % PACK + 1])
 
-        low, high, whole = slice(0, BANK), slice(BANK, S), slice(0, S)
-
-        def both_logits(s):
-            logits(s, low)
-            logits(s, high)
-
-        def multiply(s, cols, product):
-            nc.gpsimd.tensor_tensor(product, occ_of(s, cols), conf_of(s)[:, cols], MULT)
+        def multiply(s, cols):
+            nc.gpsimd.tensor_tensor(product_of(s)[:, cols], occ[s][:, cols], conf[s][:, cols], MULT)
 
         def complement(left, product):
             nc.scalar.activation(left, product, COPY, bias=1.0, scale=-1.0)
@@ -254,11 +223,8 @@ def tile_list_voxel_occupancy_map_kernel(
         def scatter(s, cols, left):
             nc.vector.tensor_copy(pages[s % PAGES][:].indirect(entries(place, cols)), left)
 
-        def fade_old(s):
-            nc.gpsimd.tensor_tensor(plane_of(s), old_tiles[s], pages[s % PAGES][:], MULT)
-
-        def fade_last(c):
-            nc.vector.tensor_tensor(plane_of(last)[:, piece(c)], old_last[c][:], pages[last % PAGES][:, piece(c)], MULT)
+        def fade(s):
+            nc.gpsimd.tensor_tensor(plane_of(s), old_rows[s], pages[s % PAGES][:], MULT)
 
         turned = {}
 
@@ -281,33 +247,130 @@ def tile_list_voxel_occupancy_map_kernel(
             dst = woven[0][:, 2 * g * PASS : (2 * g + 2) * PASS].bitcast(F32).rearrange("p (k t u) -> p k t u", k=2, u=2)
             nc.scalar.copy(dst, bank[:].rearrange("p (k u t) -> p k t u", k=2, u=2))
 
-        z_codes = {}
-        z_scales = [keep.tile([P, T2], U8, name="zs%d" % b, align_bytes=64) for b in range(PASSES)]
-
-        def chunk(c):
-            return slice(c * BANK, (c + 1) * BANK)
-
-        def piece(c):
-            return slice(EDGES[c], EDGES[c + 1])
-
         def weave(cols, copy, first_plane):
             dst = woven[1][:, cols.start * PACK : cols.stop * PACK].rearrange("p (m i t) -> p m t i", i=4, t=PACK)
             src = late_planes[:].rearrange("p (t c) -> p t c", c=T2)[:, first_plane : first_plane + 2, cols]
             copy(dst[:, :, first_plane : first_plane + 2, :], src.rearrange("p t (m i) -> p m t i", i=4))
 
-        def quantize_z(b, c):
-            quantize(z_codes[(b, c)], z_scales[b][:, piece(c)], woven[b][:, EDGES[c] * PACK : EDGES[c + 1] * PACK])
+        for cols in (first, second, high):
+            logits(0, cols)
+        for cols in (first, second):
+            nc.vector.tensor_tensor(ring[2][:, cols], occ[0][:, cols], conf_plain[:, cols], MULT)
+        for cols in (first, second):
+            nc.vector.tensor_scalar(ring[0][:, cols], ring[2][:, cols], -1.0, 1.0, MULT, ADD)
+        scatter(0, low, ring[0][:, low])
+        logits(1, low)
+        multiply(0, high)
+        multiply(1, low)
+        for a in range(PASSES):
+            interleave(nc.scalar.copy, next_values[:, a * S : (a + 1) * S], raw_next[:, a * S : (a + 1) * S])
+        quantize(codes["next"][:], scales["next"][:], next_values)
+        complement(raw_next[:, high], ring[0][:, high])
+        scatter(0, high, raw_next[:, high])
+        logits(1, high)
+        complement(ring[1][:, low], ring[1][:, low])
+        multiply(1, high)
+        occ[2], occ[3] = occ[0], occ[1]
+        logits(2, low)
+        complement(ring[1][:, high], ring[1][:, high])
+        logits(2, high)
+        scatter(1, whole, ring[1])
+        for cols in (low, high):
+            multiply(2, cols)
+        logits(3, low)
+        logits(3, high)
+        for a in range(PASSES):
+            nc.scalar.copy(
+                late_values[:, a * T2 : (a + 1) * T2].rearrange("p (t m j) -> p m j t", t=PACK, j=PACK),
+                raw_late[a].rearrange("p (j m t) -> p m j t", j=PACK, t=PACK),
+            )
+        left[2] = raw_late[1][:, whole]
+        complement(left[2], ring[2])
+        load_old(2, row_slot(2))
+        load_conf(5)
+        load_old(3, row_slot(3))
+        load_conf(6)
+        turned[0] = tenant("wide0", BLOCKS * PASS, BF16)
+        fade(0)
+        quantize(codes["late"][:], scales["late"][:], late_values)
 
+        def occupy(s):
+            occ[s] = row_slot(s - PACK, S)
+            logits(s, low)
+            logits(s, high)
+
+        def weigh(s):
+            left[s] = ring[s % 3] if s < LAST else row_slot(2, S)
+            multiply(s, whole)
+            complement(left[s], left[s])
+
+        def load_rest():
+            load_old(4, row_slot(4))
+            load_conf(7)
+            load_old(5, row_slot(0))
+            load_old(6, late_planes[:, (PACK - 1) * T2 : (PACK + 1) * T2].bitcast(F32))
+            for c in range(PIECES):
+                old_last[c] = tenant("last%d" % c, EDGES[c + 1] - EDGES[c], F32)
+                nc.sync.dma_start(out=old_last[c][:], in_=old_dealt[1, PACK - 1][:, EDGES[c] : EDGES[c + 1]])
+            nc.sync.dma_start(out=w4_codes[:].bitcast(I32), in_=w4_words.rearrange("a p c -> p a c").bitcast(I32))
+            for q in range(4):
+                nc.sync.dma_start(
+                    out=w4_plane[32 * q : 32 * q + 4, :, :].bitcast(I32),
+                    in_=w4_scales[:, 4 * q : 4 * q + 4, :].rearrange("a r c -> r a c").bitcast(I32),
+                )
+
+        old_last = {}
+        w4_codes = keep.tile([P, PASSES, 2 * N], U8, name="w4_codes", align_bytes=64)
+        w4_plane = keep.tile([P, PASSES, N], U8, name="w4_plane", align_bytes=64)
+        nc.vector.memset(w4_plane[:].bitcast(I32), 0)
+        occupy(PACK)
+        turn(0)
+        for s in range(2, LAST):
+            scatter(s, whole, left[s])
+            weigh(s + 1)
+            if s == 3:
+                load_rest()
+            fade(s - 1)
+            if s + 3 <= LAST:
+                occupy(s + 3)
+            if s - 1 < PACK:
+                turn(s - 1)
+            if s == 5:
+                for g in range(BLOCKS // 2):
+                    turn_back(g)
+        scatter(LAST, whole, left[LAST])
+        woven[1] = tenant("wide0", PACK * T2, BF16)
+        for c in range(T2 // BANK):
+            weave(slice(c * BANK, (c + 1) * BANK), nc.scalar.copy, 0)
+        fade(LAST - 1)
+
+        z_codes = {}
+        z_scales = [held("zs%d" % b, T2, U8) for b in range(PASSES)]
+        second_codes = tenant("page0", T2, U32)
         sums = {}
-        staged = {}
+        on_scalar = nc.scalar.copy
+        on_vector = nc.vector.tensor_copy
 
-        def readout(c, b):
+        def piece(c):
+            return slice(EDGES[c], EDGES[c + 1])
+
+        def width(c):
+            return EDGES[c + 1] - EDGES[c]
+
+        def half(c, h):
+            return slice(EDGES[c] + h * width(c) // 2, EDGES[c] + (h + 1) * width(c) // 2)
+
+        def fade_last(c):
+            nc.vector.tensor_tensor(plane_of(LAST)[:, piece(c)], old_last[c][:], pages[LAST % PAGES][:, piece(c)], MULT)
+
+        def readout(b, c):
+            quantize(z_codes[(b, c)], z_scales[b][:, piece(c)], woven[b][:, EDGES[c] * PACK : EDGES[c + 1] * PACK])
             for n in range(NT):
                 g = c * NT + n
                 if b == 0:
                     sums[g] = psum.tile([P, BANK], F32, name="sums", tag="bank%d" % (g % 8))
                 nc.tensor.matmul_mx(
-                    out=sums[g][:, 0 : EDGES[c + 1] - EDGES[c]],
+                    out=sums[g][:, 0 : width(c)],
                     lhsT=w4_codes[:, b, 2 * n * P : 2 * (n + 1) * P].bitcast(FP4X4),
                     lhsT_scale=w4_plane[:, b, n * P : (n + 1) * P],
                     rhs=z_codes[(b, c)].bitcast(FP8X4),
@@ -316,123 +379,27 @@ def tile_list_voxel_occupancy_map_kernel(
                     stop=(b == PASSES - 1),
                 )
 
-        def store(c, copies):
-            width = EDGES[c + 1] - EDGES[c]
-            staged[c] = tenant(old_slot[c if c < PACK else c + 1], NT * width, F32)
-            for n in range(NT):
-                held = staged[c][:, n * width : (n + 1) * width]
-                copies[n](held, sums[c * NT + n][:, 0:width])
-                nc.sync.dma_start(out=out[n * P : (n + 1) * P, piece(c)], in_=held)
-
-        first, second = slice(0, QUARTER), slice(QUARTER, BANK)
-        for cols in (first, second, high):
-            logits(0, cols)
-        left_first = keep.tile([P, BANK], F32, name="left_first")
-        shared = scratch[:, QUARTER : 3 * QUARTER]
-        for cols in (first, second):
-            nc.vector.tensor_tensor(shared[:, cols], occ_of(0, cols), conf_plain[:, cols], MULT)
-        for cols in (first, second):
-            nc.vector.tensor_scalar(left_first[:, cols], shared[:, cols], -1.0, 1.0, MULT, ADD)
-        scatter(0, low, left_first[:])
-        logits(1, low)
-        product_zero = scratch[:, 10 * QUARTER : 12 * QUARTER]
-        multiply(0, high, product_zero)
-        left_one = raw_next[:, 0:S]
-        product_one = [scratch[:, 8 * QUARTER : 10 * QUARTER], scratch[:, 0:BANK]]
-        multiply(1, low, product_one[0])
-        for n in range(2):
-            interleave(nc.scalar.copy, grouped[:, n * wide : (n + 1) * wide], raw_next[:, n * wide : (n + 1) * wide], 1)
-        quantize(next_codes[:], next_scales[:], grouped[:, 0 : 2 * wide])
-        complement(raw_next[:, S : S + BANK], product_zero)
-        scatter(0, high, raw_next[:, S : S + BANK])
-        logits(1, high)
-        complement(left_one[:, low], product_one[0])
-        multiply(1, high, product_one[1])
-        complement(left_one[:, high], product_one[1])
-        both_logits(2)
-        scatter(1, whole, left_one)
-        turned[0] = tenant("wide0", BLOCKS * PASS, BF16)
-        product_two = turned[0][:, 6 * PASS : 10 * PASS].bitcast(F32)
-        for cols in (low, high):
-            multiply(2, cols, product_two[:, cols])
-        for a in range(PASSES):
-            nc.scalar.copy(
-                grouped[:, (4 + 4 * a) * PASS : (8 + 4 * a) * PASS].rearrange("p (t m j) -> p m j t", t=PACK, j=PACK),
-                raw_late[a][:].rearrange("p (j m t) -> p m j t", j=PACK, t=PACK),
-            )
-        both_logits(3)
-        left = {2: raw_late[1][:, 0:S]}
-        complement(left[2], product_two)
-        load_old(3)
-        w4_plane = keep.tile([P, PASSES, N], U8, name="w4_plane", align_bytes=64)
-        nc.vector.memset(w4_plane[:].bitcast(I32), 0)
-        for q in range(4):
-            nc.sync.dma_start(
-                out=w4_plane[32 * q : 32 * q + 4, :, :].bitcast(I32),
-                in_=w4_scales[:, 4 * q : 4 * q + 4, :].rearrange("a r c -> r a c").bitcast(I32),
-            )
-        fade_old(0)
-        load_old(4)
-        turn(0)
-        quantize(late_codes[:], late_scales[:], grouped[:, 4 * PASS : 12 * PASS])
-
-        def weigh(s):
-            if s == AHEAD:
-                left[s] = scratch[:, S : 2 * S]
-            else:
-                product = tenant(old_slot[s - AHEAD], S, F32)
-                left[s] = product[:]
-            multiply(s, whole, left[s])
-            complement(left[s], left[s])
-            if s < last:
-                both_logits(s + 1)
-
-        last = SLICES - 1
-        for s in range(1, last):
-            if s > 1:
-                scatter(s, whole, left[s])
-            if s + 2 <= last:
-                weigh(s + 2)
-            if s == PACK:
-                for g in range(BLOCKS // 2):
-                    turn_back(g)
-            if s == PACK + 1:
-                load_old(6)
-            fade_old(s)
-            if s < PACK:
-                turn(s)
-            if s == 2:
-                load_old(5)
-            if s == PACK + 1:
-                woven[1] = tenant("wide0", PACK * T2, BF16)
-                for c in range(CHUNKS):
-                    weave(chunk(c), nc.scalar.copy, 0)
-
-        second_codes = tenant("conf0", T2, U32)
-        first_slot = [old_slot[4], "last1", "last2", "last3", "last4"]
-        on_scalar = nc.scalar.copy
-        on_vector = nc.vector.tensor_copy
-
         def first_pass(c):
-            first_codes = tenant(first_slot[c], EDGES[c + 1] - EDGES[c], U32)
-            z_codes[(0, c)] = first_codes[:]
-            quantize_z(0, c)
-            readout(c, 0)
+            words = tenant("last%d" % c if c else "rows2", width(c), U32)
+            z_codes[(0, c)] = words[:]
+            readout(0, c)
 
         def second_pass(c):
             z_codes[(1, c)] = second_codes[:, piece(c)]
-            quantize_z(1, c)
-            readout(c, 1)
+            readout(1, c)
 
-        def half(c, h):
-            return slice(c * BANK + h * QUARTER, c * BANK + (h + 1) * QUARTER)
+        def store(c, copies):
+            staged = row_slot(c, NT * width(c))
+            for n in range(NT):
+                part = staged[:, n * width(c) : (n + 1) * width(c)]
+                copies[n](part, sums[c * NT + n][:, 0 : width(c)])
+                nc.sync.dma_start(out=out[n * P : (n + 1) * P, piece(c)], in_=part)
 
-        scatter(last, whole, left[last])
         first_pass(0)
         fade_last(0)
         fade_last(1)
-        weave(chunk(1), on_scalar, 2)
-        weave(chunk(0), on_vector, 2)
+        weave(piece(1), on_scalar, 2)
+        weave(piece(0), on_vector, 2)
         fade_last(2)
         weave(half(2, 0), on_scalar, 2)
         second_pass(0)

@@ -177,6 +177,8 @@ def tile_list_voxel_occupancy_map_kernel(
         late_planes = tenant("wide1", (PACK + 1) * T2, BF16)
 
         def plane_of(s):
+            if s == 0:
+                return occ[0].bitcast(BF16)
             if s == 1:
                 return late_values[:, 0:T2]
             if s < PACK:

@@ -257,9 +257,9 @@ def tile_list_voxel_occupancy_map_kernel(
         for cols in (first, second, high):
             logits(0, cols)
         for cols in (first, second):
-            nc.vector.tensor_tensor(ring[2][:, cols], occ[0][:, cols], conf_plain[:, cols], MULT)
+            nc.vector.tensor_tensor(ring[1][:, cols], occ[0][:, cols], conf_plain[:, cols], MULT)
         for cols in (first, second):
-            nc.vector.tensor_scalar(ring[0][:, cols], ring[2][:, cols], -1.0, 1.0, MULT, ADD)
+            nc.vector.tensor_scalar(ring[0][:, cols], ring[1][:, cols], -1.0, 1.0, MULT, ADD)
         scatter(0, low, ring[0][:, low])
         logits(1, low)
         multiply(0, high)
@@ -267,16 +267,16 @@ def tile_list_voxel_occupancy_map_kernel(
         for a in range(PASSES):
             interleave(nc.scalar.copy, next_values[:, a * S : (a + 1) * S], raw_next[:, a * S : (a + 1) * S])
         quantize(codes["next"][:], scales["next"][:], next_values)
-        complement(raw_next[:, high], ring[0][:, high])
-        scatter(0, high, raw_next[:, high])
+        complement(raw_next[:, S : S + BANK], ring[0][:, high])
+        scatter(0, high, raw_next[:, S : S + BANK])
         logits(1, high)
-        complement(ring[1][:, low], ring[1][:, low])
+        complement(raw_next[:, low], ring[1][:, low])
         multiply(1, high)
         occ[2], occ[3] = occ[0], occ[1]
         logits(2, low)
-        complement(ring[1][:, high], ring[1][:, high])
+        complement(raw_next[:, high], ring[1][:, high])
         logits(2, high)
-        scatter(1, whole, ring[1])
+        scatter(1, whole, raw_next[:, whole])
         for cols in (low, high):
             multiply(2, cols)
         logits(3, low)

@@ -114,7 +114,6 @@ def tile_list_voxel_occupancy_map_kernel(
         load_old(0, row_slot(0))
         load_w1(raw_late[1], 1, PASS, PASS)
         nc.sync.dma_start(out=bias[1][:], in_=b1[PASS : 2 * PASS].rearrange("(p i) -> p i", i=PACK))
-        load_old(1, row_slot(1))
 
         conf = {s: conf_plain for s in range(PACK)}
         conf_rows = wgs.rearrange("(m i) j -> i m j", i=PACK)
@@ -124,7 +123,9 @@ def tile_list_voxel_occupancy_map_kernel(
             for q in (0, 2, 1, 3):
                 nc.sync.dma_start(out=conf[s][32 * q : 32 * q + 32, :], in_=conf_rows[s - PACK])
 
+        load_old(1, row_slot(1))
         load_conf(4)
+        load_conf(5)
 
         pages = {}
 
@@ -289,27 +290,29 @@ def tile_list_voxel_occupancy_map_kernel(
         left[2] = raw_late[1][:, whole]
         complement(left[2], ring[2])
         load_old(2, row_slot(2))
-        load_conf(5)
-        load_old(3, row_slot(3))
         load_conf(6)
+        load_old(3, row_slot(3))
+        load_conf(7)
         turned[0] = tenant("wide0", BLOCKS * PASS, BF16)
         fade(0)
         quantize(codes["late"][:], scales["late"][:], late_values)
 
         def occupy(s):
-            occ[s] = row_slot(s - PACK, S)
+            if s == 4:
+                occ[s] = turned[0][:, 6 * PASS : 10 * PASS].bitcast(F32)
+            else:
+                occ[s] = held("occ5", S, F32)[:] if s == 5 else row_slot(s - 6, S)
             logits(s, low)
             logits(s, high)
 
         def weigh(s):
-            left[s] = ring[s % 3] if s < LAST else row_slot(2, S)
+            left[s] = (ring + [occ[1]])[s - 3] if s < LAST else row_slot(0, S)
             multiply(s, whole)
             complement(left[s], left[s])
 
         def load_rest():
             load_old(4, row_slot(4))
-            load_conf(7)
-            load_old(5, row_slot(0))
+            load_old(5, row_slot(2))
             load_old(6, late_planes[:, (PACK - 1) * T2 : (PACK + 1) * T2].bitcast(F32))
             for c in range(PIECES):
                 old_last[c] = tenant("last%d" % c, EDGES[c + 1] - EDGES[c], F32)
@@ -325,16 +328,23 @@ def tile_list_voxel_occupancy_map_kernel(
         w4_codes = keep.tile([P, PASSES, 2 * N], U8, name="w4_codes", align_bytes=64)
         w4_plane = keep.tile([P, PASSES, N], U8, name="w4_plane", align_bytes=64)
         nc.vector.memset(w4_plane[:].bitcast(I32), 0)
-        occupy(PACK)
+        occupy(4)
+        weigh(3)
+        occupy(5)
+        occupy(6)
+        scatter(2, whole, left[2])
+        fade(1)
+        occupy(LAST)
+        weigh(4)
         turn(0)
-        for s in range(2, LAST):
+        turn(1)
+        for s in range(3, LAST):
             scatter(s, whole, left[s])
-            weigh(s + 1)
+            if s + 2 <= LAST:
+                weigh(s + 2)
+            fade(s - 1)
             if s == 3:
                 load_rest()
-            fade(s - 1)
-            if s + 3 <= LAST:
-                occupy(s + 3)
             if s - 1 < PACK:
                 turn(s - 1)
             if s == 5:
@@ -382,7 +392,7 @@ def tile_list_voxel_occupancy_map_kernel(
                 )
 
         def first_pass(c):
-            words = tenant("last%d" % c if c else "rows2", width(c), U32)
+            words = tenant("last%d" % c if c else "rows0", width(c), U32)
             z_codes[(0, c)] = words[:]
             readout(0, c)
 

@@ -31,8 +31,8 @@ PAGES = 3
 STRIPE = 16
 HALF = BANK // 2
 BLOCKS = T2 // P
-EDGES = [0,512,1024,1536,1792,2048]
-PIECES = len(EDGES) - 1
+SPANS = [(512, 768), (768, 1024), (0, 512), (1024, 1280), (1280, 1536), (1536, 1792), (1792, 2048)]
+PIECES = len(SPANS)
 
 
 def tile_list_voxel_occupancy_map_kernel(
@@ -49,6 +49,12 @@ def tile_list_voxel_occupancy_map_kernel(
 
         def tenant(tag, columns, dtype):
             return slots.tile([P, columns], dtype, name="tenant", tag=tag, align_bytes=64)
+
+        def piece(c):
+            return slice(SPANS[c][0], SPANS[c][1])
+
+        def width(c):
+            return SPANS[c][1] - SPANS[c][0]
 
         low, high, whole = slice(0, BANK), slice(BANK, S), slice(0, S)
         first, second = slice(0, HALF), slice(HALF, BANK)
@@ -250,10 +256,12 @@ def tile_list_voxel_occupancy_map_kernel(
             dst = woven[0][:, 2 * g * PASS : (2 * g + 2) * PASS].bitcast(F32).rearrange("p (k t u) -> p k t u", k=2, u=2)
             nc.scalar.copy(dst, bank[:].rearrange("p (k u t) -> p k t u", k=2, u=2))
 
-        def weave(cols, copy, first_plane):
+        def weave(cols, copy, planes):
             dst = woven[1][:, cols.start * PACK : cols.stop * PACK].rearrange("p (m i t) -> p m t i", i=4, t=PACK)
-            src = late_planes[:].rearrange("p (t c) -> p t c", c=T2)[:, first_plane : first_plane + 2, cols]
-            copy(dst[:, :, first_plane : first_plane + 2, :], src.rearrange("p t (m i) -> p m t i", i=4))
+            src = late_planes[:].rearrange("p (t c) -> p t c", c=T2)[:, planes, cols]
+            copy(dst[:, :, planes, :], src.rearrange("p t (m i) -> p m t i", i=4))
+
+        early_pair, late_pair, all_four = slice(0, 2), slice(2, PACK), slice(0, PACK)
 
         for cols in (first, second, high):
             logits(0, cols)
@@ -315,8 +323,8 @@ def tile_list_voxel_occupancy_map_kernel(
             load_old(5, row_slot(2))
             load_old(6, late_planes[:, (PACK - 1) * T2 : (PACK + 1) * T2].bitcast(F32))
             for c in range(PIECES):
-                old_last[c] = tenant("last%d" % c, EDGES[c + 1] - EDGES[c], F32)
-                nc.sync.dma_start(out=old_last[c][:], in_=old_dealt[1, PACK - 1][:, EDGES[c] : EDGES[c + 1]])
+                old_last[c] = tenant("last%d" % c, width(c), F32)
+                nc.sync.dma_start(out=old_last[c][:], in_=old_dealt[1, PACK - 1][:, piece(c)])
             nc.sync.dma_start(out=w4_codes[:].bitcast(I32), in_=w4_words.rearrange("a p c -> p a c").bitcast(I32))
             for q in range(4):
                 nc.sync.dma_start(
@@ -352,8 +360,8 @@ def tile_list_voxel_occupancy_map_kernel(
                     turn_back(g)
         scatter(LAST, whole, left[LAST])
         woven[1] = tenant("wide0", PACK * T2, BF16)
-        for c in range(T2 // BANK):
-            weave(slice(c * BANK, (c + 1) * BANK), nc.scalar.copy, 0)
+        for cols in (slice(0, 512), slice(512, 1024), slice(1024, 1536), slice(1536, 2048)):
+            weave(cols, nc.scalar.copy, early_pair)
         fade(LAST - 1)
 
         z_codes = {}
@@ -363,20 +371,16 @@ def tile_list_voxel_occupancy_map_kernel(
         on_scalar = nc.scalar.copy
         on_vector = nc.vector.tensor_copy
 
-        def piece(c):
-            return slice(EDGES[c], EDGES[c + 1])
-
-        def width(c):
-            return EDGES[c + 1] - EDGES[c]
-
         def half(c, h):
-            return slice(EDGES[c] + h * width(c) // 2, EDGES[c] + (h + 1) * width(c) // 2)
+            return slice(SPANS[c][0] + h * width(c) // 2, SPANS[c][0] + (h + 1) * width(c) // 2)
 
-        def fade_last(c):
-            nc.vector.tensor_tensor(plane_of(LAST)[:, piece(c)], old_last[c][:], pages[LAST % PAGES][:, piece(c)], MULT)
+        def fade_last(c, cols=None):
+            cols = cols or piece(c)
+            rows = old_last[c][:, cols.start - SPANS[c][0] : cols.stop - SPANS[c][0]]
+            nc.vector.tensor_tensor(plane_of(LAST)[:, cols], rows, pages[LAST % PAGES][:, cols], MULT)
 
         def readout(b, c):
-            quantize(z_codes[(b, c)], z_scales[b][:, piece(c)], woven[b][:, EDGES[c] * PACK : EDGES[c + 1] * PACK])
+            quantize(z_codes[(b, c)], z_scales[b][:, piece(c)], woven[b][:, SPANS[c][0] * PACK : SPANS[c][1] * PACK])
             for n in range(NT):
                 g = c * NT + n
                 if b == 0:
@@ -401,35 +405,34 @@ def tile_list_voxel_occupancy_map_kernel(
             readout(1, c)
 
         def store(c, copies):
-            staged = row_slot(c, NT * width(c))
+            staged = row_slot(c % 5, NT * width(c))
             for n in range(NT):
                 part = staged[:, n * width(c) : (n + 1) * width(c)]
                 copies[n](part, sums[c * NT + n][:, 0 : width(c)])
                 nc.sync.dma_start(out=out[n * P : (n + 1) * P, piece(c)], in_=part)
 
         first_pass(0)
+        fade_last(2, half(2, 0))
+        weave(half(2, 0), on_scalar, late_pair)
         fade_last(0)
+        fade_last(2, half(2, 1))
+        weave(half(2, 1), on_scalar, late_pair)
+        weave(piece(0), on_vector, late_pair)
         fade_last(1)
-        weave(piece(1), on_scalar, 2)
-        weave(piece(0), on_vector, 2)
-        fade_last(2)
-        weave(half(2, 0), on_scalar, 2)
         second_pass(0)
         store(0, [on_scalar] * NT)
+        weave(piece(1), on_vector, late_pair)
         first_pass(1)
         second_pass(1)
         store(1, [on_scalar] * NT)
-        weave(half(2, 1), on_vector, 2)
         first_pass(2)
         fade_last(3)
         second_pass(2)
-        weave(piece(3), on_vector, 2)
         store(2, [on_scalar] * NT)
-        fade_last(4)
-        first_pass(3)
-        second_pass(3)
-        weave(piece(4), on_vector, 2)
-        store(3, [on_scalar] * NT)
-        first_pass(4)
-        second_pass(4)
-        store(4, [on_vector, on_scalar, on_vector])
+        for c in range(3, PIECES):
+            weave(piece(c), on_vector, late_pair)
+            if c + 1 < PIECES:
+                fade_last(c + 1)
+            first_pass(c)
+            second_pass(c)
+            store(c, [on_scalar] * NT if c + 1 < PIECES else [on_vector, on_scalar, on_vector])

@@ -59,6 +59,11 @@ def tile_list_voxel_occupancy_map_kernel(
         low, high, whole = slice(0, BANK), slice(BANK, S), slice(0, S)
         first, second = slice(0, HALF), slice(HALF, BANK)
 
+        warm = keep.tile([P, 1], F32, name="warm")
+        warmed = keep.tile([P, 1], F32, name="warmed")
+        nc.vector.memset(warm[:], 0.0)
+        nc.scalar.activation(warmed[:], warm[:], SIGMOID)
+
         pick = keep.tile([P, S // STRIPE], U16, name="pick")
         place = keep.tile([P, S // STRIPE], U16, name="place")
         nc.sync.dma_start(pick[:], offs)

@@ -64,6 +64,9 @@ def tile_list_voxel_occupancy_map_kernel(
         nc.vector.memset(warm[:], 0.0)
         nc.scalar.activation(warmed[:], warm[:], SIGMOID)
 
+        bias_rows = held("bias_rows", P, F32)
+        nc.gpsimd.memset(bias_rows[:], 0.0)
+
         pick = keep.tile([P, S // STRIPE], U16, name="pick")
         place = keep.tile([P, S // STRIPE], U16, name="place")
         nc.sync.dma_start(pick[:], offs)
@@ -97,11 +100,13 @@ def tile_list_voxel_occupancy_map_kernel(
         table = [load_table(0)]
         for a in range(PASSES):
             load_w1(raw_head[a], a, 0, 2 * P)
+        nc.sync.dma_start(out=bias_rows[0:PACK, :], in_=b1[0:PASS].rearrange("(q p) -> q p", p=P))
         table.append(load_table(1))
 
         bias = [keep.tile([P, PACK], F32, name="bias%d" % b) for b in range(PASSES)]
-        with nc.allow_non_contiguous_dma(reason="one bias value a partition"):
-            nc.sync.dma_start(out=bias[0][:], in_=b1[0:PASS].rearrange("(q p) -> p q", p=P))
+        turned_bias = psum.tile([P, P], F32, name="turned_bias", tag="bank0")
+        nc.tensor.transpose(turned_bias[:], bias_rows[:], ident_pairs[:])
+        nc.scalar.copy(bias[0][:], turned_bias[:, 0:PACK])
         conf_plain = held("conf_plain", S, F32)
         nc.sync.dma_start(out=conf_plain[:], in_=wgs)
         nc.sync.dma_start(place[:], offs2)
@@ -147,7 +152,7 @@ def tile_list_voxel_occupancy_map_kernel(
         def entries(offsets, cols):
             return offsets[:, cols.start // STRIPE : cols.stop // STRIPE]
 
-        open_page(0, nc.vector)
+        open_page(0, nc.gpsimd)
         picked_scales = held("picked_scales", S, U8)
         picked = [held("picked%d" % a, S, I32) for a in range(PASSES)]
         nc.vector.tensor_copy(picked_scales[:], scale_win[:].indirect(pick[:]))
@@ -156,7 +161,7 @@ def tile_list_voxel_occupancy_map_kernel(
                 out=table_plane[32 * q : 32 * q + 4, :].bitcast(I32),
                 in_=picked_scales[8 * q : 8 * q + 8, :].bitcast(I32),
             )
-        open_page(1, nc.gpsimd)
+        open_page(1, nc.vector)
         nc.vector.tensor_copy(picked[0][:].bitcast(U32), table[0][:].bitcast(U32).indirect(pick[:]))
 
         codes = {name: held(name + "_codes", n * P, U32) for name, n in (("head", 4), ("next", 4), ("late", 8))}
@@ -176,7 +181,7 @@ def tile_list_voxel_occupancy_map_kernel(
             interleave(copy, head_values[:, a * S : (a + 1) * S], raw_head[a])
             at = slice(a * 2 * P, (a + 1) * 2 * P)
             quantize(codes["head"][:, at], scales["head"][:, at], head_values[:, a * S : (a + 1) * S])
-        open_page(2, nc.gpsimd)
+        open_page(2, nc.vector)
         for cols in (first, second, high):
             nc.vector.tensor_copy(picked[1][:, cols].bitcast(U32), table[1][:].bitcast(U32).indirect(entries(pick, cols)))
 

@@ -98,10 +98,11 @@ def tile_list_voxel_occupancy_map_kernel(
         woven = {0: held("woven0", PACK * T2, BF16)}
         raw_head = [woven[0][:].bitcast(F32)[:, a * S : (a + 1) * S] for a in range(PASSES)]
         table = [load_table(0)]
-        for a in range(PASSES):
-            load_w1(raw_head[a], a, 0, 2 * P)
+        load_w1(raw_head[0], 0, 0, 2 * P)
         nc.sync.dma_start(out=bias_rows[0:PACK, :], in_=b1[0:PASS].rearrange("(q p) -> q p", p=P))
         table.append(load_table(1))
+        for s in range(2):
+            load_w1(raw_head[1][:, s * BANK : (s + 1) * BANK], 1, s * P, P)
 
         bias = [keep.tile([P, PACK], F32, name="bias%d" % b) for b in range(PASSES)]
         turned_bias = psum.tile([P, P], F32, name="turned_bias", tag="bank0")
@@ -154,7 +155,7 @@ def tile_list_voxel_occupancy_map_kernel(
 
         open_page(0, nc.gpsimd)
         picked_scales = held("picked_scales", S, U8)
-        picked = [held("picked%d" % a, S, I32) for a in range(PASSES)]
+        picked = {(0, 0): held("picked0", S, I32), (1, 0): held("picked1", BANK, I32)}
         nc.vector.tensor_copy(picked_scales[:], scale_win[:].indirect(pick[:]))
         for q in range(4):
             nc.scalar.dma_start(
@@ -162,7 +163,7 @@ def tile_list_voxel_occupancy_map_kernel(
                 in_=picked_scales[8 * q : 8 * q + 8, :].bitcast(I32),
             )
         open_page(1, nc.vector)
-        nc.vector.tensor_copy(picked[0][:].bitcast(U32), table[0][:].bitcast(U32).indirect(pick[:]))
+        nc.vector.tensor_copy(picked[(0, 0)][:].bitcast(U32), table[0][:].bitcast(U32).indirect(pick[:]))
 
         codes = {name: held(name + "_codes", n * P, U32) for name, n in (("head", 4), ("next", 4), ("late", 8))}
         scales = {name: held(name + "_scales", n * P, U8) for name, n in (("head", 4), ("next", 4), ("late", 8))}
@@ -176,14 +177,30 @@ def tile_list_voxel_occupancy_map_kernel(
         def quantize(words, plane, values):
             nc.vector.quantize_mx(out=words.bitcast(FP8X4), scales=plane, in_=values)
 
-        head_values = tenant("page2", PASSES * S, BF16)
-        for a, copy in enumerate((nc.scalar.copy, nc.vector.tensor_copy)):
-            interleave(copy, head_values[:, a * S : (a + 1) * S], raw_head[a])
-            at = slice(a * 2 * P, (a + 1) * 2 * P)
-            quantize(codes["head"][:, at], scales["head"][:, at], head_values[:, a * S : (a + 1) * S])
+        head_values = tenant("page2", S, BF16)
+        interleave(nc.scalar.copy, head_values[:], raw_head[0])
+        quantize(codes["head"][:, 0 : 2 * P], scales["head"][:, 0 : 2 * P], head_values[:])
         open_page(2, nc.vector)
-        for cols in (first, second, high):
-            nc.vector.tensor_copy(picked[1][:, cols].bitcast(U32), table[1][:].bitcast(U32).indirect(entries(pick, cols)))
+
+        def picked_of(a, cols):
+            if a == 1 and cols.start >= BANK:
+                return picked[(1, 1)][:, cols.start - BANK : cols.stop - BANK]
+            return picked[(a, 0)][:, cols]
+
+        def gather(cols):
+            nc.vector.tensor_copy(picked_of(1, cols).bitcast(U32), table[1][:].bitcast(U32).indirect(entries(pick, cols)))
+
+        def behind_table(s, values):
+            interleave(nc.scalar.copy, values[:], raw_head[1][:, s * BANK : (s + 1) * BANK])
+            at = slice((2 + s) * P, (3 + s) * P)
+            quantize(codes["head"][:, at], scales["head"][:, at], values[:])
+
+        gather(first)
+        gather(second)
+        behind_table(0, tenant("picked_high", BANK, BF16))
+        picked[(1, 1)] = tenant("picked_high", BANK, I32)
+        gather(high)
+        behind_table(1, held("values_behind", BANK, BF16))
 
         work = held("work", 9 * BANK, F32)
         next_values = work[:, BANK : 3 * BANK].bitcast(BF16)
@@ -226,7 +243,7 @@ def tile_list_voxel_occupancy_map_kernel(
                     out=acc[:, 0:count],
                     lhsT=words.bitcast(FP8X4),
                     lhsT_scale=plane,
-                    rhs=picked[a][:, cols].bitcast(FP8X4),
+                    rhs=picked_of(a, cols).bitcast(FP8X4),
                     rhs_scale=table_plane[:, a * S + cols.start : a * S + cols.stop],
                     start=(a == 0),
                     stop=(a == PASSES - 1),

@@ -57,7 +57,7 @@ def tile_list_voxel_occupancy_map_kernel(
             return SPANS[c][1] - SPANS[c][0]
 
         low, high, whole = slice(0, BANK), slice(BANK, S), slice(0, S)
-        first, second = slice(0, HALF), slice(HALF, BANK)
+        first, second, third, fourth = (slice(n * HALF, (n + 1) * HALF) for n in range(4))
 
         warm = keep.tile([P, 1], F32, name="warm")
         warmed = keep.tile([P, 1], F32, name="warmed")
@@ -109,7 +109,8 @@ def tile_list_voxel_occupancy_map_kernel(
         nc.tensor.transpose(turned_bias[:], bias_rows[:], ident_pairs[:])
         nc.scalar.copy(bias[0][:], turned_bias[:, 0:PACK])
         conf_plain = held("conf_plain", S, F32)
-        nc.sync.dma_start(out=conf_plain[:], in_=wgs)
+        for cols in (low, high):
+            nc.sync.dma_start(out=conf_plain[:, cols], in_=wgs[:, cols])
         nc.sync.dma_start(place[:], offs2)
         raw_next = tenant("rows2", PASSES * S, F32)
         for a in range(PASSES):
@@ -127,16 +128,22 @@ def tile_list_voxel_occupancy_map_kernel(
             return rows[:]
 
         raw_late = [row_slot(3 + a) for a in range(PASSES)]
-        load_w1(raw_late[0], 0, PASS, PASS)
         load_old(0, row_slot(0))
-        load_w1(raw_late[1], 1, PASS, PASS)
+        load_w1(raw_late[0], 0, PASS, PASS)
+        for h in range(2):
+            nc.sync.dma_start(
+                out=raw_late[1].rearrange("p (j c) -> p j c", j=PACK)[:, :, h * HALF : (h + 1) * HALF],
+                in_=w1[PASS : 2 * PASS, PASS + h * HALF : PASS + (h + 1) * HALF].rearrange("(p j) c -> p j c", j=PACK),
+            )
         nc.sync.dma_start(out=bias[1][:], in_=b1[PASS : 2 * PASS].rearrange("(p i) -> p i", i=PACK))
 
         conf = {s: conf_plain for s in range(PACK)}
         conf_rows = wgs.rearrange("(m i) j -> i m j", i=PACK)
 
+        conf_pair = held("conf_pair", 2 * S, F32)
+
         def load_conf(s):
-            conf[s] = held("conf%d" % s, S, F32)
+            conf[s] = conf_pair[:, s % 2 * S : (s % 2 + 1) * S] if s < 6 else held("conf%d" % s, S, F32)
             for q in (0, 2, 1, 3):
                 nc.sync.dma_start(out=conf[s][32 * q : 32 * q + 32, :], in_=conf_rows[s - PACK])
 
@@ -155,7 +162,7 @@ def tile_list_voxel_occupancy_map_kernel(
 
         open_page(0, nc.gpsimd)
         picked_scales = held("picked_scales", S, U8)
-        picked = {(0, 0): held("picked0", S, I32), (1, 0): held("picked1", BANK, I32)}
+        picked = {(0, 0): held("picked0", S, I32), (1, 0): held("picked1", S - HALF, I32)}
         nc.vector.tensor_copy(picked_scales[:], scale_win[:].indirect(pick[:]))
         for q in range(4):
             nc.scalar.dma_start(
@@ -183,8 +190,8 @@ def tile_list_voxel_occupancy_map_kernel(
         open_page(2, nc.vector)
 
         def picked_of(a, cols):
-            if a == 1 and cols.start >= BANK:
-                return picked[(1, 1)][:, cols.start - BANK : cols.stop - BANK]
+            if a == 1 and cols.start == fourth.start:
+                return picked[(1, 1)][:]
             return picked[(a, 0)][:, cols]
 
         def gather(cols):
@@ -197,9 +204,10 @@ def tile_list_voxel_occupancy_map_kernel(
 
         gather(first)
         gather(second)
-        behind_table(0, tenant("picked_high", BANK, BF16))
-        picked[(1, 1)] = tenant("picked_high", BANK, I32)
-        gather(high)
+        gather(third)
+        behind_table(0, tenant("picked_last", BANK, BF16))
+        picked[(1, 1)] = tenant("picked_last", HALF, I32)
+        gather(fourth)
         behind_table(1, held("values_behind", BANK, BF16))
 
         work = held("work", 9 * BANK, F32)
@@ -237,16 +245,17 @@ def tile_list_voxel_occupancy_map_kernel(
             acc = psum.tile([P, BANK], F32, name="acc", tag="bank%d" % (4 + banks_used[0] % 4))
             banks_used[0] = banks_used[0] + 1
             count = cols.stop - cols.start
-            for a in range(PASSES):
+            steps = [(0, cols), (1, third), (1, fourth)] if cols == high else [(0, cols), (1, cols)]
+            for n, (a, part) in enumerate(steps):
                 words, plane = weights_of(s, a)
                 nc.tensor.matmul_mx(
-                    out=acc[:, 0:count],
+                    out=acc[:, part.start - cols.start : part.stop - cols.start],
                     lhsT=words.bitcast(FP8X4),
                     lhsT_scale=plane,
-                    rhs=picked_of(a, cols).bitcast(FP8X4),
-                    rhs_scale=table_plane[:, a * S + cols.start : a * S + cols.stop],
-                    start=(a == 0),
-                    stop=(a == PASSES - 1),
+                    rhs=picked_of(a, part).bitcast(FP8X4),
+                    rhs_scale=table_plane[:, a * S + part.start : a * S + part.stop],
+                    start=(n == 0),
+                    stop=(n == len(steps) - 1),
                 )
             nc.scalar.activation(occ[s][:, cols], acc[:, 0:count], SIGMOID, bias=bias[s // PACK][:, s % PACK : s % PACK + 1])
 
@@ -260,7 +269,8 @@ def tile_list_voxel_occupancy_map_kernel(
             nc.vector.tensor_copy(pages[s % PAGES][:].indirect(entries(place, cols)), left)
 
         def fade(s):
-            nc.gpsimd.tensor_tensor(plane_of(s), old_rows[s], pages[s % PAGES][:], MULT)
+            for cols in (slice(0, S), slice(S, T2)) if s == 5 else (slice(0, T2),):
+                nc.gpsimd.tensor_tensor(plane_of(s)[:, cols], old_rows[s][:, cols], pages[s % PAGES][:, cols], MULT)
 
         turned = {}
 
@@ -317,10 +327,10 @@ def tile_list_voxel_occupancy_map_kernel(
             multiply(2, cols)
         logits(3, low)
         logits(3, high)
-        for a in range(PASSES):
+        for a, rows in ((0, slice(0, P)), (1, slice(0, P // 2)), (1, slice(P // 2, P))):
             nc.scalar.copy(
-                late_values[:, a * T2 : (a + 1) * T2].rearrange("p (t m j) -> p m j t", t=PACK, j=PACK),
-                raw_late[a].rearrange("p (j m t) -> p m j t", j=PACK, t=PACK),
+                late_values[:, a * T2 : (a + 1) * T2].rearrange("p (t m j) -> p m j t", t=PACK, j=PACK)[:, rows],
+                raw_late[a].rearrange("p (j m t) -> p m j t", j=PACK, t=PACK)[:, rows],
             )
         left[2] = raw_late[1][:, whole]
         complement(left[2], ring[2])
@@ -333,17 +343,24 @@ def tile_list_voxel_occupancy_map_kernel(
         quantize(codes["late"][:], scales["late"][:], late_values)
 
         def occupy(s):
-            if s == 4:
-                occ[s] = turned[0][:, 6 * PASS : 10 * PASS].bitcast(F32)
+            if s < 6:
+                occ[s] = turned[0][:, s * PASS * 4 - 12 * PASS : s * PASS * 4 - 8 * PASS].bitcast(F32)
             else:
-                occ[s] = held("occ5", S, F32)[:] if s == 5 else row_slot(s - 6, S)
+                occ[s] = row_slot(s - 6, S)
             logits(s, low)
             logits(s, high)
 
         def weigh(s):
-            left[s] = (ring + [occ[1]])[s - 3] if s < LAST else row_slot(0, S)
-            multiply(s, whole)
-            complement(left[s], left[s])
+            if s != 4:
+                left[s] = row_slot(0, S) if s == LAST else {3: ring[0], 6: occ[1]}[s]
+                multiply(s, whole)
+                complement(left[s], left[s])
+                return
+            both = held("left_pair", 2 * S, F32)
+            nc.gpsimd.tensor_tensor(both[:], turned[0][:, 4 * PASS : 12 * PASS].bitcast(F32), conf_pair[:], MULT)
+            for n in range(2):
+                left[s + n] = both[:, n * S : (n + 1) * S]
+                complement(left[s + n], left[s + n])
 
         def load_rest():
             load_old(4, row_slot(4))
@@ -375,7 +392,7 @@ def tile_list_voxel_occupancy_map_kernel(
         turn(1)
         for s in range(3, LAST):
             scatter(s, whole, left[s])
-            if s + 2 <= LAST:
+            if s in (4, 5):
                 weigh(s + 2)
             fade(s - 1)
             if s == 3:
@@ -445,6 +462,8 @@ def tile_list_voxel_occupancy_map_kernel(
         fade_last(2, half(2, 1))
         weave(half(2, 1), on_scalar, late_pair)
         weave(piece(0), on_vector, late_pair)
+        fade_last(3)
+        weave(piece(3), on_scalar, late_pair)
         fade_last(1)
         second_pass(0)
         store(0, [on_scalar] * NT)
@@ -453,10 +472,13 @@ def tile_list_voxel_occupancy_map_kernel(
         second_pass(1)
         store(1, [on_scalar] * NT)
         first_pass(2)
-        fade_last(3)
+        fade_last(4)
         second_pass(2)
         store(2, [on_scalar] * NT)
-        for c in range(3, PIECES):
+        first_pass(3)
+        second_pass(3)
+        store(3, [on_scalar] * NT)
+        for c in range(4, PIECES):
             weave(piece(c), on_vector, late_pair)
             if c + 1 < PIECES:
                 fade_last(c + 1)

@@ -269,8 +269,7 @@ def tile_list_voxel_occupancy_map_kernel(
             nc.vector.tensor_copy(pages[s % PAGES][:].indirect(entries(place, cols)), left)
 
         def fade(s):
-            for cols in (slice(0, S), slice(S, T2)) if s == 5 else (slice(0, T2),):
-                nc.gpsimd.tensor_tensor(plane_of(s)[:, cols], old_rows[s][:, cols], pages[s % PAGES][:, cols], MULT)
+            nc.gpsimd.tensor_tensor(plane_of(s), old_rows[s], pages[s % PAGES][:], MULT)
 
         turned = {}
 

from contextlib import ExitStack

import concourse.mybir as mybir
from concourse.masks import make_identity

K, H, N, T, S, T2 = 1024, 1024, 384, 4096, 1024, 2048
FLOPS = 2 * K * H * S + 2 * H * N * T2

F32 = mybir.dt.float32
BF16 = mybir.dt.bfloat16
I32 = mybir.dt.int32
U32 = mybir.dt.uint32
U16 = mybir.dt.uint16
U8 = mybir.dt.uint8
FP8X4 = mybir.dt.float8_e4m3fn_x4
FP4X4 = mybir.dt.float4_e2m1fn_x4
MULT = mybir.AluOpType.mult
ADD = mybir.AluOpType.add
SIGMOID = mybir.ActivationFunctionType.Sigmoid
COPY = mybir.ActivationFunctionType.Copy

P = 128
PACK = 4
PASS = P * PACK
BANK = 512
PASSES = 2
SLICES = PASSES * PACK
LAST = SLICES - 1
NT = N // P
PAGES = 3
STRIPE = 16
HALF = BANK // 2
BLOCKS = T2 // P
SPANS = [(512, 768), (768, 1024), (0, 512), (1024, 1280), (1280, 1536), (1536, 1792), (1792, 2048)]
PIECES = len(SPANS)


def tile_list_voxel_occupancy_map_kernel(
    tc, tab_words, tab_scales, offs, w1, b1, wgs, offs2, old, w4_words, w4_scales, out
):
    nc = tc.nc
    with ExitStack() as ctx:
        keep = ctx.enter_context(tc.tile_pool(name="keep", bufs=1))
        slots = ctx.enter_context(tc.tile_pool(name="slots", bufs=1))
        psum = ctx.enter_context(tc.psum_pool(name="psum", bufs=1))

        def held(name, columns, dtype):
            return keep.tile([P, columns], dtype, name=name, align_bytes=64)

        def tenant(tag, columns, dtype):
            return slots.tile([P, columns], dtype, name="tenant", tag=tag, align_bytes=64)

        def piece(c):
            return slice(SPANS[c][0], SPANS[c][1])

        def width(c):
            return SPANS[c][1] - SPANS[c][0]

        low, high, whole = slice(0, BANK), slice(BANK, S), slice(0, S)
        first, second, third, fourth = (slice(n * HALF, (n + 1) * HALF) for n in range(4))

        warm = keep.tile([P, 1], F32, name="warm")
        warmed = keep.tile([P, 1], F32, name="warmed")
        nc.vector.memset(warm[:], 0.0)
        nc.scalar.activation(warmed[:], warm[:], SIGMOID)

        bias_rows = held("bias_rows", P, F32)
        nc.gpsimd.memset(bias_rows[:], 0.0)

        pick = keep.tile([P, S // STRIPE], U16, name="pick")
        place = keep.tile([P, S // STRIPE], U16, name="place")
        nc.sync.dma_start(pick[:], offs)
        scale_win = tenant("page1", T, U8)
        nc.sync.dma_start(
            out=scale_win[0:32, :].bitcast(I32),
            in_=tab_scales.rearrange("a m t -> m a t").bitcast(I32),
        )
        nc.vector.memset(scale_win[32:64, :].bitcast(I32), 0)
        nc.vector.memset(scale_win[64:P, :].bitcast(I32), 0)
        table_plane = held("table_plane", PASSES * S, U8)
        nc.gpsimd.memset(table_plane[:].bitcast(I32), 0)
        ident_pairs = held("ident_pairs", P, F32)
        ident = held("ident", P, BF16)
        make_identity(nc, ident_pairs[:])
        make_identity(nc, ident[:])

        def load_table(a):
            words = tenant("wide%d" % a, T, I32)
            nc.sync.dma_start(out=words[:], in_=tab_words[a].rearrange("p t i -> p (t i)").bitcast(I32))
            return words

        def load_w1(raw, a, start, count):
            nc.sync.dma_start(
                out=raw.rearrange("p (j c) -> p j c", j=PACK),
                in_=w1[a * PASS : (a + 1) * PASS, start : start + count].rearrange("(p j) c -> p j c", j=PACK),
            )

        woven = {0: held("woven0", PACK * T2, BF16)}
        raw_head = [woven[0][:].bitcast(F32)[:, a * S : (a + 1) * S] for a in range(PASSES)]
        table = [load_table(0)]
        load_w1(raw_head[0], 0, 0, 2 * P)
        nc.sync.dma_start(out=bias_rows[0:PACK, :], in_=b1[0:PASS].rearrange("(q p) -> q p", p=P))
        table.append(load_table(1))
        for s in range(2):
            load_w1(raw_head[1][:, s * BANK : (s + 1) * BANK], 1, s * P, P)

        bias = [keep.tile([P, PACK], F32, name="bias%d" % b) for b in range(PASSES)]
        turned_bias = psum.tile([P, P], F32, name="turned_bias", tag="bank0")
        nc.tensor.transpose(turned_bias[:], bias_rows[:], ident_pairs[:])
        nc.scalar.copy(bias[0][:], turned_bias[:, 0:PACK])
        conf_plain = held("conf_plain", S, F32)
        for cols in (low, high):
            nc.sync.dma_start(out=conf_plain[:, cols], in_=wgs[:, cols])
        nc.sync.dma_start(place[:], offs2)
        raw_next = tenant("rows2", PASSES * S, F32)
        for a in range(PASSES):
            load_w1(raw_next[:, a * S : (a + 1) * S], a, 2 * P, 2 * P)

        old_dealt = old.rearrange("(b p i) t -> b i p t", b=PASSES, i=PACK)
        old_rows = {}

        def load_old(s, rows):
            old_rows[s] = rows
            nc.sync.dma_start(out=rows, in_=old[s * P : (s + 1) * P, :] if s < PACK else old_dealt[1, s - PACK])

        def row_slot(n, columns=T2):
            rows = tenant("rows%d" % n, columns, F32)
            return rows[:]

        raw_late = [row_slot(3 + a) for a in range(PASSES)]
        load_old(0, row_slot(0))
        load_w1(raw_late[0], 0, PASS, PASS)
        for h in range(2):
            nc.sync.dma_start(
                out=raw_late[1].rearrange("p (j c) -> p j c", j=PACK)[:, :, h * HALF : (h + 1) * HALF],
                in_=w1[PASS : 2 * PASS, PASS + h * HALF : PASS + (h + 1) * HALF].rearrange("(p j) c -> p j c", j=PACK),
            )
        nc.sync.dma_start(out=bias[1][:], in_=b1[PASS : 2 * PASS].rearrange("(p i) -> p i", i=PACK))

        conf = {s: conf_plain for s in range(PACK)}
        conf_rows = wgs.rearrange("(m i) j -> i m j", i=PACK)

        conf_pair = held("conf_pair", 2 * S, F32)

        def load_conf(s):
            conf[s] = conf_pair[:, s % 2 * S : (s % 2 + 1) * S] if s < 6 else held("conf%d" % s, S, F32)
            for q in (0, 2, 1, 3):
                nc.sync.dma_start(out=conf[s][32 * q : 32 * q + 32, :], in_=conf_rows[s - PACK])

        load_old(1, row_slot(1))
        load_conf(4)
        load_conf(5)

        pages = {}

        def open_page(n, engine):
            pages[n] = tenant("page%d" % n, T2, F32)
            engine.memset(pages[n][:], 1.0)

        def entries(offsets, cols):
            return offsets[:, cols.start // STRIPE : cols.stop // STRIPE]

        open_page(0, nc.gpsimd)
        picked_scales = held("picked_scales", S, U8)
        picked = {(0, 0): held("picked0", S, I32), (1, 0): held("picked1", S - HALF, I32)}
        nc.vector.tensor_copy(picked_scales[:], scale_win[:].indirect(pick[:]))
        for q in range(4):
            nc.scalar.dma_start(
                out=table_plane[32 * q : 32 * q + 4, :].bitcast(I32),
                in_=picked_scales[8 * q : 8 * q + 8, :].bitcast(I32),
            )
        open_page(1, nc.vector)
        nc.vector.tensor_copy(picked[(0, 0)][:].bitcast(U32), table[0][:].bitcast(U32).indirect(pick[:]))

        codes = {name: held(name + "_codes", n * P, U32) for name, n in (("head", 4), ("next", 4), ("late", 8))}
        scales = {name: held(name + "_scales", n * P, U8) for name, n in (("head", 4), ("next", 4), ("late", 8))}

        def interleave(copy, dst, src):
            copy(
                dst.rearrange("p (m i j) -> p m j i", i=4, j=PACK),
                src.rearrange("p (j m i) -> p m j i", i=4, j=PACK),
            )

        def quantize(words, plane, values):
            nc.vector.quantize_mx(out=words.bitcast(FP8X4), scales=plane, in_=values)

        head_values = tenant("page2", S, BF16)
        interleave(nc.scalar.copy, head_values[:], raw_head[0])
        quantize(codes["head"][:, 0 : 2 * P], scales["head"][:, 0 : 2 * P], head_values[:])
        open_page(2, nc.vector)

        def picked_of(a, cols):
            if a == 1 and cols.start == fourth.start:
                return picked[(1, 1)][:]
            return picked[(a, 0)][:, cols]

        def gather(cols):
            nc.vector.tensor_copy(picked_of(1, cols).bitcast(U32), table[1][:].bitcast(U32).indirect(entries(pick, cols)))

        def behind_table(s, values):
            interleave(nc.scalar.copy, values[:], raw_head[1][:, s * BANK : (s + 1) * BANK])
            at = slice((2 + s) * P, (3 + s) * P)
            quantize(codes["head"][:, at], scales["head"][:, at], values[:])

        gather(first)
        gather(second)
        gather(third)
        behind_table(0, tenant("picked_last", BANK, BF16))
        picked[(1, 1)] = tenant("picked_last", HALF, I32)
        gather(fourth)
        behind_table(1, held("values_behind", BANK, BF16))

        work = held("work", 9 * BANK, F32)
        next_values = work[:, BANK : 3 * BANK].bitcast(BF16)
        late_values = work[:, 3 * BANK : 7 * BANK].bitcast(BF16)
        ring = [work[:, 5 * BANK : 7 * BANK], work[:, 0 : 2 * BANK], work[:, 7 * BANK : 9 * BANK]]
        occ = {s: held("occ%d" % s, S, F32)[:] for s in range(2)}
        plain = [held("plain%d" % n, T2, BF16) for n in range(2)]
        late_planes = tenant("wide1", (PACK + 1) * T2, BF16)

        def plane_of(s):
            if s == 0:
                return occ[0].bitcast(BF16)
            if s == 1:
                return late_values[:, 0:T2]
            if s < PACK:
                return plain[s % 2][:]
            return late_planes[:, (s - PACK) * T2 : (s - PACK + 1) * T2]

        left = {}

        def product_of(s):
            return left[s] if s > 2 else ring[s]

        def weights_of(s, a):
            if s < PACK:
                name, at = ("head", "next")[s // 2], (2 * a + s % 2) * P
            else:
                name, at = "late", a * PASS + (s - PACK) * P
            return codes[name][:, at : at + P], scales[name][:, at : at + P]

        banks_used = [0]

        def logits(s, cols):
            acc = psum.tile([P, BANK], F32, name="acc", tag="bank%d" % (4 + banks_used[0] % 4))
            banks_used[0] = banks_used[0] + 1
            count = cols.stop - cols.start
            steps = [(0, cols), (1, third), (1, fourth)] if cols == high else [(0, cols), (1, cols)]
            for n, (a, part) in enumerate(steps):
                words, plane = weights_of(s, a)
                nc.tensor.matmul_mx(
                    out=acc[:, part.start - cols.start : part.stop - cols.start],
                    lhsT=words.bitcast(FP8X4),
                    lhsT_scale=plane,
                    rhs=picked_of(a, part).bitcast(FP8X4),
                    rhs_scale=table_plane[:, a * S + part.start : a * S + part.stop],
                    start=(n == 0),
                    stop=(n == len(steps) - 1),
                )
            nc.scalar.activation(occ[s][:, cols], acc[:, 0:count], SIGMOID, bias=bias[s // PACK][:, s % PACK : s % PACK + 1])

        def multiply(s, cols):
            nc.gpsimd.tensor_tensor(product_of(s)[:, cols], occ[s][:, cols], conf[s][:, cols], MULT)

        def complement(left, product):
            nc.scalar.activation(left, product, COPY, bias=1.0, scale=-1.0)

        def scatter(s, cols, left):
            nc.vector.tensor_copy(pages[s % PAGES][:].indirect(entries(place, cols)), left)

        def fade(s):
            nc.gpsimd.tensor_tensor(plane_of(s), old_rows[s], pages[s % PAGES][:], MULT)

        turned = {}

        def turn(q):
            for g in range(2):
                bank = psum.tile([P, 8 * P], BF16, name="turn", tag="bank%d" % g)
                for k in range(8):
                    at = (8 * g + k) * P
                    nc.tensor.transpose(bank[:, k * P : (k + 1) * P], plane_of(q)[:, at : at + P], ident[:])
                dst = turned[0][:].rearrange("p (k r) -> p k r", r=PASS)[:, 8 * g : 8 * g + 8, q * P : (q + 1) * P]
                nc.scalar.copy(dst, bank[:].rearrange("p (k r) -> p k r", r=P))

        def turn_back(g):
            bank = psum.tile([P, BANK], F32, name="back", tag="bank%d" % (g % 4))
            for k in range(2):
                at = (2 * g + k) * PASS
                words = turned[0][:, at : at + PASS].bitcast(F32)
                for u in range(2):
                    nc.tensor.transpose(bank[:, (2 * k + u) * P : (2 * k + u + 1) * P], words[:, u : 2 * P : 2], ident_pairs[:])
            dst = woven[0][:, 2 * g * PASS : (2 * g + 2) * PASS].bitcast(F32).rearrange("p (k t u) -> p k t u", k=2, u=2)
            nc.scalar.copy(dst, bank[:].rearrange("p (k u t) -> p k t u", k=2, u=2))

        def weave(cols, copy, planes):
            dst = woven[1][:, cols.start * PACK : cols.stop * PACK].rearrange("p (m i t) -> p m t i", i=4, t=PACK)
            src = late_planes[:].rearrange("p (t c) -> p t c", c=T2)[:, planes, cols]
            copy(dst[:, :, planes, :], src.rearrange("p t (m i) -> p m t i", i=4))

        early_pair, late_pair, all_four = slice(0, 2), slice(2, PACK), slice(0, PACK)

        for cols in (first, second, high):
            logits(0, cols)
        for cols in (first, second):
            nc.vector.tensor_tensor(ring[1][:, cols], occ[0][:, cols], conf_plain[:, cols], MULT)
        for cols in (first, second):
            nc.vector.tensor_scalar(ring[0][:, cols], ring[1][:, cols], -1.0, 1.0, MULT, ADD)
        scatter(0, low, ring[0][:, low])
        logits(1, low)
        multiply(0, high)
        multiply(1, low)
        for a in range(PASSES):
            interleave(nc.scalar.copy, next_values[:, a * S : (a + 1) * S], raw_next[:, a * S : (a + 1) * S])
        quantize(codes["next"][:], scales["next"][:], next_values)
        complement(raw_next[:, S : S + BANK], ring[0][:, high])
        scatter(0, high, raw_next[:, S : S + BANK])
        logits(1, high)
        complement(raw_next[:, low], ring[1][:, low])
        multiply(1, high)
        occ[2], occ[3] = occ[0], occ[1]
        logits(2, low)
        complement(raw_next[:, high], ring[1][:, high])
        logits(2, high)
        scatter(1, whole, raw_next[:, whole])
        for cols in (low, high):
            multiply(2, cols)
        logits(3, low)
        logits(3, high)
        for a, rows in ((0, slice(0, P)), (1, slice(0, P // 2)), (1, slice(P // 2, P))):
            nc.scalar.copy(
                late_values[:, a * T2 : (a + 1) * T2].rearrange("p (t m j) -> p m j t", t=PACK, j=PACK)[:, rows],
                raw_late[a].rearrange("p (j m t) -> p m j t", j=PACK, t=PACK)[:, rows],
            )
        left[2] = raw_late[1][:, whole]
        complement(left[2], ring[2])
        load_old(2, row_slot(2))
        load_conf(6)
        load_old(3, row_slot(3))
        load_conf(7)
        turned[0] = tenant("wide0", BLOCKS * PASS, BF16)
        fade(0)
        quantize(codes["late"][:], scales["late"][:], late_values)

        def occupy(s):
            if s < 6:
                occ[s] = turned[0][:, s * PASS * 4 - 12 * PASS : s * PASS * 4 - 8 * PASS].bitcast(F32)
            else:
                occ[s] = row_slot(s - 6, S)
            logits(s, low)
            logits(s, high)

        def weigh(s):
            if s != 4:
                left[s] = row_slot(0, S) if s == LAST else {3: ring[0], 6: occ[1]}[s]
                multiply(s, whole)
                complement(left[s], left[s])
                return
            both = held("left_pair", 2 * S, F32)
            nc.gpsimd.tensor_tensor(both[:], turned[0][:, 4 * PASS : 12 * PASS].bitcast(F32), conf_pair[:], MULT)
            for n in range(2):
                left[s + n] = both[:, n * S : (n + 1) * S]
                complement(left[s + n], left[s + n])

        def load_rest():
            load_old(4, row_slot(4))
            load_old(5, row_slot(2))
            load_old(6, late_planes[:, (PACK - 1) * T2 : (PACK + 1) * T2].bitcast(F32))
            for c in range(PIECES):
                old_last[c] = tenant("last%d" % c, width(c), F32)
                nc.sync.dma_start(out=old_last[c][:], in_=old_dealt[1, PACK - 1][:, piece(c)])
            nc.sync.dma_start(out=w4_codes[:].bitcast(I32), in_=w4_words.rearrange("a p c -> p a c").bitcast(I32))
            for q in range(4):
                nc.sync.dma_start(
                    out=w4_plane[32 * q : 32 * q + 4, :, :].bitcast(I32),
                    in_=w4_scales[:, 4 * q : 4 * q + 4, :].rearrange("a r c -> r a c").bitcast(I32),
                )

        old_last = {}
        w4_codes = keep.tile([P, PASSES, 2 * N], U8, name="w4_codes", align_bytes=64)
        w4_plane = keep.tile([P, PASSES, N], U8, name="w4_plane", align_bytes=64)
        nc.vector.memset(w4_plane[:].bitcast(I32), 0)
        occupy(4)
        weigh(3)
        occupy(5)
        occupy(6)
        scatter(2, whole, left[2])
        fade(1)
        occupy(LAST)
        weigh(4)
        turn(0)
        turn(1)
        for s in range(3, LAST):
            scatter(s, whole, left[s])
            if s in (4, 5):
                weigh(s + 2)
            fade(s - 1)
            if s == 3:
                load_rest()
            if s - 1 < PACK:
                turn(s - 1)
            if s == 5:
                for g in range(BLOCKS // 2):
                    turn_back(g)
        scatter(LAST, whole, left[LAST])
        woven[1] = tenant("wide0", PACK * T2, BF16)
        for cols in (slice(0, 512), slice(512, 1024), slice(1024, 1536), slice(1536, 2048)):
            weave(cols, nc.scalar.copy, early_pair)
        fade(LAST - 1)

        z_codes = {}
        z_scales = [held("zs%d" % b, T2, U8) for b in range(PASSES)]
        second_codes = tenant("page0", T2, U32)
        sums = {}
        on_scalar = nc.scalar.copy
        on_vector = nc.vector.tensor_copy

        def half(c, h):
            return slice(SPANS[c][0] + h * width(c) // 2, SPANS[c][0] + (h + 1) * width(c) // 2)

        def fade_last(c, cols=None):
            cols = cols or piece(c)
            rows = old_last[c][:, cols.start - SPANS[c][0] : cols.stop - SPANS[c][0]]
            nc.vector.tensor_tensor(plane_of(LAST)[:, cols], rows, pages[LAST % PAGES][:, cols], MULT)

        def readout(b, c):
            quantize(z_codes[(b, c)], z_scales[b][:, piece(c)], woven[b][:, SPANS[c][0] * PACK : SPANS[c][1] * PACK])
            for n in range(NT):
                g = c * NT + n
                if b == 0:
                    sums[g] = psum.tile([P, BANK], F32, name="sums", tag="bank%d" % (g % 8))
                nc.tensor.matmul_mx(
                    out=sums[g][:, 0 : width(c)],
                    lhsT=w4_codes[:, b, 2 * n * P : 2 * (n + 1) * P].bitcast(FP4X4),
                    lhsT_scale=w4_plane[:, b, n * P : (n + 1) * P],
                    rhs=z_codes[(b, c)].bitcast(FP8X4),
                    rhs_scale=z_scales[b][:, piece(c)],
                    start=(b == 0),
                    stop=(b == PASSES - 1),
                )

        def first_pass(c):
            words = tenant("last%d" % c if c else "rows0", width(c), U32)
            z_codes[(0, c)] = words[:]
            readout(0, c)

        def second_pass(c):
            z_codes[(1, c)] = second_codes[:, piece(c)]
            readout(1, c)

        def store(c, copies):
            staged = row_slot(c % 5, NT * width(c))
            for n in range(NT):
                part = staged[:, n * width(c) : (n + 1) * width(c)]
                copies[n](part, sums[c * NT + n][:, 0 : width(c)])
                nc.sync.dma_start(out=out[n * P : (n + 1) * P, piece(c)], in_=part)

        first_pass(0)
        fade_last(2, half(2, 0))
        weave(half(2, 0), on_scalar, late_pair)
        fade_last(0)
        fade_last(2, half(2, 1))
        weave(half(2, 1), on_scalar, late_pair)
        weave(piece(0), on_vector, late_pair)
        fade_last(3)
        weave(piece(3), on_scalar, late_pair)
        fade_last(1)
        second_pass(0)
        store(0, [on_scalar] * NT)
        weave(piece(1), on_vector, late_pair)
        first_pass(1)
        second_pass(1)
        store(1, [on_scalar] * NT)
        first_pass(2)
        fade_last(4)
        second_pass(2)
        store(2, [on_scalar] * NT)
        first_pass(3)
        second_pass(3)
        store(3, [on_scalar] * NT)
        for c in range(4, PIECES):
            weave(piece(c), on_vector, late_pair)
            if c + 1 < PIECES:
                fade_last(c + 1)
            first_pass(c)
            second_pass(c)
            store(c, [on_scalar] * NT if c + 1 < PIECES else [on_vector, on_scalar, on_vector])
